import numpy as np, ml_dtypes
CORES = [40,41,42,43,44,45,46,47]
N = 8
BF = ml_dtypes.bfloat16
def f(rng, *shape):
    return (rng.standard_normal(shape, dtype=np.float32) * np.exp2(rng.integers(-2, 3, shape[:-1] + (1,)))).astype(BF)
def wide(rng, *shape):
    v = f(rng, *shape).astype(np.float32); k = shape[:-2] + (1, shape[-1])
    return (v * np.exp2(rng.integers(-6, 7, k)) * (rng.random(k) > 0.0625)).astype(BF)
E, EP, A, AP, TY = 512, 64, 64, 8, 32
TR, M, SH = 2048, 2, 6
CAPP, CAPO, L = 320, 160, 1280
def vals(rng, v):
    return v.astype(np.float32) * (np.float32(0.5) + rng.random(v.shape, dtype=np.float32))
def held(ent, att, g):
    h = np.zeros(E * A, bool); h[(ent[:, g].astype(np.int64) * A + att[:, g]).reshape(-1)] = True
    return h
def places(cls, form, g):
    fo = form[:, g].reshape(N, TY, A)[np.arange(N)[:, None], cls[:, g]].reshape(E, A)
    return [np.arange(E)[:, None] * A + ((fo >> (SH * i)) & (A - 1)) for i in range(M)]
def present(ent, att, cls, form, g):
    h = held(ent, att, g); ok = np.ones((E, A), bool)
    for p in places(cls, form, g):
        ok = ok & h[p]
    return ok
def deal(rng):
    mean = TR // N; m = np.zeros((8, N, N), np.int64)
    for g in range(8):
        for r in range(N):
            o = rng.permutation(N); x = rng.integers(0, CAPP - mean + 1, N // 2); m[g, r, o[0::2]] = mean + x; m[g, r, o[1::2]] = mean - x
    return m
def triples(rng, m, late):
    ent = np.zeros((N, 8, TR), np.int32); att = np.zeros((N, 8, TR), np.int32)
    for g in range(8):
        mine = [[] for r in range(N)]
        for q in range(N):
            pri = rng.random((EP, A)) + late[g, q * EP:(q + 1) * EP, None]; pri[:, 0] = 9
            cuts = np.add.accumulate(m[g, :, q])
            k = rng.permutation(np.argsort(pri, axis=None)[:cuts[-1]]) + q * EP * A
            for r, part in enumerate(np.split(k, cuts[:-1])):
                mine[r].append(part)
        for r in range(N):
            k = rng.permutation(np.concatenate(mine[r])); ent[r, g] = k >> SH; att[r, g] = k & (A - 1)
    return ent, att
def formulas(rng, same):
    fs = rng.integers(1, A, (M, N, 8, TY * A)); fs = np.where(rng.random(fs.shape[1:]) < same, fs[:1], fs)
    return np.where(rng.random(fs.shape) < 0.015625, 0, fs)
def pack(fs):
    v = fs[0]
    for i in range(1, M):
        v = v + (fs[i] << (SH * i))
    return v.astype(np.int32)
def trim(rng, d, full=False):
    for g in range(8):
        ok = present(d["ent"], d["att"], d["cls"], d["form"], g).reshape(N, EP, A)
        for q in range(N):
            n = np.zeros((TY, A), np.int64); np.add.at(n, d["cls"][q, g], ok[q].astype(np.int64))
            for c in range(N):
                w = n[:, c * AP:(c + 1) * AP].reshape(-1)
                if np.sum(w) <= CAPO:
                    continue
                o = rng.permutation(TY * AP)
                if full:
                    o = o[np.argsort(-w[o], kind="stable")]
                s = 0; w = w.tolist()
                for i in o.tolist():
                    if s + w[i] > CAPO:
                        d["form"][q, g, (i // AP) * A + c * AP + (i & (AP - 1))] = 0
                    else:
                        s += w[i]
    return d
def setup_inputs(rng):
    ent, att = triples(rng, deal(rng), np.zeros((8, E)))
    d = {"val": vals(rng, f(rng, N, 128, TR)), "ent": ent, "att": att, "cls": rng.integers(0, TY, (N, 8, EP)).astype(np.int32), "form": pack(formulas(rng, 0.0625))}
    return trim(rng, d)
def setup_inputs_full(rng):
    d = setup_inputs(rng); m = np.zeros((8, N, N), np.int64); crowd = int(rng.integers(8)); odd = int(rng.integers(N))
    for g in range(8):
        s = int(rng.integers(N))
        for r in range(N):
            rest = TR
            for i in range(N):
                o = r + s + i
                if g == crowd:
                    o = s - i if r == odd else s + i
                c = min(CAPP, rest); m[g, r, o % N] = c; rest -= c
    d["ent"], d["att"] = triples(rng, m, np.zeros((8, E)))
    d["cls"] = rng.permuted(np.tile(np.arange(EP) % TY, (N, 8, 1)), axis=2).astype(np.int32)
    fs = np.zeros((M, N, 8, TY * A), np.int64)
    for g in range(8):
        h = held(d["ent"], d["att"], g).reshape(N, EP, A)
        for q in range(N):
            o = np.argsort(np.sum(h[q], axis=1), kind="stable"); rep = np.zeros(TY, np.int64); rep[d["cls"][q, g][o]] = o
            fs[:, q, g] = np.argmax(rng.random((M, TY, A, A)) * h[q][rep][None, :, None, :], axis=3).reshape(M, -1)
    d["form"] = pack(fs); return trim(rng, d, True)
def setup_inputs_ragged(rng):
    d = setup_inputs(rng)
    late = np.stack([np.concatenate([rng.permutation(np.repeat(np.array([-1.0, 0.0, 0.0, 1.0]), EP // 4)) for q in range(N)]) for g in range(8)])
    d["ent"], d["att"] = triples(rng, deal(rng), late); fo = pack(formulas(rng, 0.0625)).reshape(N, 8, TY, A)
    for g in range(8):
        for c in range(N):
            fo[:, g, :, c * AP + int(rng.integers(AP))] = 0
        q, c = int(rng.integers(N)), int(rng.integers(N)); fo[q, g, :, c * AP:(c + 1) * AP] = 0
    d["form"] = np.ascontiguousarray(fo.reshape(N, 8, TY * A)); return trim(rng, d)
def setup_inputs_one(rng):
    d = setup_inputs(rng); d["cls"] = np.repeat(rng.integers(0, TY, (N, 8, 1)), EP, axis=2).astype(np.int32)
    k = np.sort(d["ent"] * A + d["att"], axis=2); k[1::2] = k[1::2, :, ::-1].copy()
    d["ent"] = (k >> SH).astype(np.int32); d["att"] = (k & (A - 1)).astype(np.int32)
    d["form"] = pack(formulas(rng, 0.5)); return trim(rng, d)
def setup_inputs_spread(rng):
    d = setup_inputs(rng); d["val"] = vals(rng, wide(rng, N, 128, TR)); return d
def check_inputs(d):
    bad = []
    for name, lo, hi in (("ent", 0, E), ("att", 1, A), ("cls", 0, TY), ("form", 0, A ** M)):
        if not ((d[name] >= lo) & (d[name] < hi)).all():
            bad.append("range of " + name)
    if not (np.abs(d["val"].astype(np.float32)) < 2.0 ** 100).all():
        bad.append("finite")
    if bad:
        return bad
    ent, att = d["ent"], d["att"]
    for g in range(8):
        if np.count_nonzero(held(ent, att, g)) != N * TR:
            bad.append("distinct triples")
        if max(int(np.bincount(ent[r, g] // EP, minlength=N).max()) for r in range(N)) > CAPP:
            bad.append("triples of a rank for an owner")
        if np.sum(present(ent, att, d["cls"], d["form"], g).reshape(N, EP, N, AP), axis=(1, 3)).max() > CAPO:
            bad.append("derived cells of a pair of owners")
    return sorted(set(bad))
def reference(val, ent, att, cls, form):
    y = np.zeros((N, 128, L), np.float32); who = np.full((N, 8, L), -1, np.float32); cnt = np.zeros((N, 8, AP), np.float32)
    for g in range(8):
        cell = np.zeros((E * A, 16), np.float32)
        for r in range(N):
            cell[ent[r, g].astype(np.int64) * A + att[r, g]] = val[r, 16 * g:16 * g + 16].T.astype(np.float32)
        ps = places(cls, form, g); ok = present(ent, att, cls, form, g)
        new = cell[ps[0]] - cell[ps[1]]
        for p in ps[2:]:
            new = new + cell[p]
        for c in range(N):
            o = np.ascontiguousarray(ok[:, c * AP:(c + 1) * AP].T); a, e = np.nonzero(o); n = len(e)
            y[c, 16 * g:16 * g + 16, :n] = new[e, c * AP + a].T.astype(np.float32); who[c, g, :n] = e; cnt[c, g] = np.sum(o, axis=1)
    return {"y": y, "who": who, "cnt": cnt}

@@ -1,0 +1,383 @@
+from concourse.bass import DstId, RemoteDMATransfer
+from concourse.mybir import AluOpType as A, ActivationFunctionType as F, AxisListType
+
+N, TR, CP, CO, L = 8, 2048, 320, 160, 1280
+TW = 5568
+MID = 1328.0
+f32, bf, i32, u16, f16 = "float32", "bfloat16", "int32", "uint16", "float16"
+SB = {
+    "EA": (256, i32), "VAL": (TR, f32), "FX": (128, i32), "CL4": (16, i32), "Z": (512, f32),
+    "PC1": (8, i32), "MI": (128, i32), "XF": (144, f32), "COL": (8, f32), "CI": (8, i32), "MA": (128, i32),
+    "BLK": (128, bf), "BS": (144, bf), "BW": (144, bf), "BH": (144, f16), "IDN": (128, bf), "GT": (128, bf), "TRI": (128, bf), "IK": (128, bf),
+    "OWI": (128, i32), "OWB": (128, bf), "OW8": (128, bf), "EL6": (128, i32), "K0": (128, f32), "KZ": (128, f32), "KT": (128, f32), "KO": (128, f32),
+    "O": (1024, bf), "S": (1024, bf), "X": (1024, bf), "HI": (128, i32), "Y1": (128, f32), "Y2": (128, f32), "Y3": (128, f32), "D1": (128, u16),
+    "P": (TR, f32), "DI": (320, f32), "WA": (2560, f32), "WB": (2560, f32), "NA": (320, f32), "NB": (320, f32), "NM": (320, f32),
+    "KS": (160, u16), "TS": (160, u16), "KR": (160, u16), "S1": (2560, f32), "R1": (2560, f32), "PC": (2560, f32),
+    "TA": (TW, f32), "TB": (TW, f32), "FZ": (128, f32), "FW": (128, f32), "LC": (16, u16), "FE": (256, i32), "FF": (512, i32),
+    "E64": (512, i32), "FG": (512, i32), "LL": (512, u16), "G1": (4096, f32), "N1": (256, f32), "N2": (256, f32),
+    "MN": (256, f32), "PR": (256, bf), "KC": (256, bf), "S2": (256, bf), "CW": (264, f32), "H1": (264, f32), "H2": (264, f32),
+    "CS": (64, f32), "CL": (128, f32), "K160": (160, bf), "CM": (2560, bf), "D32": (80, bf), "LB": (80, u16), "K1": (L, f32),
+    "M": (L, bf), "X1": (L, f16), "X2": (L, f16), "L1": (80, u16), "L2": (80, u16), "GV": (L, f32), "S2V": (L, f32), "R2": (L + 8, f32),
+    "BI": (80, i32), "BU": (80, i32), "UE": (80, f32), "ES": (80, f32), "EL": (96, f32), "EW": (1536, f32),
+    "PI": (8, f32), "PU": (8, u16), "IS": (64, f32), "EX": (64, f32), "NS": (64, f32), "INC": (72, f32), "DL": (64, f32), "DD": (64, f32),
+    "EM": (72, f32), "SG": (192, f32), "U0": (64, f32), "MK": (64, f32), "SM": (128, f32), "SC": (8, f32), "SO": (4, u16), "CN": (8, f32),
+    "JW": (L + 72, f32), "JS": (L, f16), "JN": (80, f32),
+    "SR": (80, f32), "SQ": (80, f32), "LV": (80, u16), "WI": (80, i32), "W1": (80, f32), "W2": (80, f32), "W3": (80, f32), "LW": (80, u16),
+}
+SCRATCH = {k: ("sbuf", [128, w], t) for k, (w, t) in SB.items()}
+SCRATCH.update({"P%d" % k: ("psum", [128, 512], f32) for k in range(8)})
+ND = 40
+SEMAPHORES = ["cv", "cs", "cp", "cg", "ls", "aK", "aV", "aC", "aE", "aY"] + ["d%d" % k for k in range(ND)]
+
+
+def rank_program(g, core, T, topo):
+    r = T.rank_of(core)
+    if r is None:
+        return
+    Q = {"v": g.vector, "s": g.scalar, "p": g.tensor, "y": g.sync, "g": g}
+    total, seen, lastw, readers, nd = {}, {}, {}, {}, [0]
+
+    def wait(q, tok):
+        if seen.get((q, tok[0]), 0) < tok[1]:
+            Q[q].wait_ge(T.sem[tok[0]], tok[1])
+            seen[(q, tok[0])] = tok[1]
+
+    def before(q, rd, wr):
+        need = {}
+        for k in rd:
+            toks = list(lastw.get(k, []))
+            if k[0] == "P" and k[1:].isdigit():
+                toks += [t for t in readers.get(k, []) if t[0] != "c" + q]
+            for s, n in toks:
+                need[s] = max(need.get(s, 0), n)
+        for k in wr:
+            for s, n in lastw.get(k, []) + readers.get(k, []):
+                need[s] = max(need.get(s, 0), n)
+        for s in sorted(need):
+            wait(q, (s, need[s]))
+
+    def after(tok, rd, wr):
+        for k in rd:
+            readers.setdefault(k, []).append(tok)
+        for k in wr:
+            lastw[k] = [tok]
+            readers[k] = []
+
+    def bump(s, n):
+        total[s] = total.get(s, 0) + n
+        return (s, total[s])
+
+    def op(q, fn, rd, wr):
+        rd, wr = rd.split(), wr.split()
+        before(q, rd, wr)
+        fn().then_inc(T.sem["c" + q], 1)
+        after(bump("c" + q, 1), rd, wr)
+
+    def dma(q, out, in_, rd, wr, **kw):
+        rd, wr = rd.split(), wr.split()
+        before(q, rd, wr)
+        s = "d%d" % nd[0]
+        nd[0] += 1
+        Q[q].dma_start(out, in_, **kw).then_inc(T.sem[s], 16)
+        after(bump(s, 16), rd, wr)
+
+    def mm(out, bank, items):
+        before("p", [], [bank])
+        allr = []
+        for n, (lt, rh, rd) in enumerate(items):
+            before("p", rd.split(), [])
+            allr += rd.split()
+            ins = g.tensor.matmul(out, lt, rh, n == 0, n == len(items) - 1)
+        ins.then_inc(T.sem.cp, 1)
+        after(bump("cp", 1), allr, [bank])
+
+    V, S = g.vector, g.scalar
+
+    def ts(out, in0, s1, s2, o0, o1, rd, wr):
+        if o1 is None:
+            op("v", lambda: V.tensor_scalar(out, in0, s1, None, o0), rd, wr)
+        else:
+            op("v", lambda: V.tensor_scalar(out, in0, s1, s2, o0, o1), rd, wr)
+
+    def tt(out, a, b, o, rd, wr):
+        op("v", lambda: V.tensor_tensor(out, a, b, o), rd, wr)
+
+    def cp(out, a, rd, wr):
+        op("v", lambda: V.tensor_copy(out, a), rd, wr)
+
+    def ms(out, c, wr):
+        op("v", lambda: V.memset(out, c), "", wr)
+
+    def scan(out, d0, d1, o0, o1, rd, wr):
+        op("v", lambda: V.tensor_tensor_scan(out, d0, d1, 0.0, o0, o1), rd, wr)
+
+    def act(out, a, fn, rd, wr, **kw):
+        op("s", lambda: S.activation(out, a, fn, **kw), rd, wr)
+
+    def iota(name, out, pat, base, cm, wr=None):
+        kw = {} if SB[name][1] == i32 else {"allow_small_or_imprecise_dtypes": True}
+        op("g", lambda: g.iota(out, pat, base, cm, **kw), "", wr or name)
+
+    cores = list(T.cores)
+    far = [k for k in range(N) if topo.die(cores[k]) != topo.die(core)]
+    near = [k for k in range(N) if k != r and k not in far]
+    eng = topo.engines(core, cores[far[0]])
+
+    def send(dests, masks, src, dst, sem, rd):
+        before("g", rd.split(), [])
+        trs = []
+        for k, m in zip(dests, masks):
+            rid, pid = topo.addr(cores[k])[:2]
+            trs.append(RemoteDMATransfer(dst_ids=[DstId(rid=rid, pnc=pid)], dma_engine_mask=sum(1 << e for e in m),
+                                         remote_sem=T.sem[sem], src=src(k), dst=dst))
+        g.remote_dma_fused(trs, local_sem=T.sem.ls)
+        bump("ls", sum(len(m) for m in masks))
+
+    def exchange(src, dst, sem, rd, key):
+        ev, od = eng[0::2], eng[1::2]
+        masks = [ev[2 * n:2 * n + 2] for n in range(len(far))] + [od[2 * n:2 * n + 2] for n in range(len(near))]
+        send(far + near, masks, src, dst, sem, rd)
+        before("y", rd.split(), [key])
+        g.sync.dma_start(dst, src(r)).then_inc(T.sem[sem], 16)
+        after(bump(sem, 2 * (N - 1) + 16), [], [key])
+
+    def diag(out, bank, lhs, lk, srcs, extra=()):
+        items = list(extra)
+        for buf, c0, n, key in srcs:
+            items += [(lhs[:, 15 - i:143 - i], buf[:, c0 + i:c0 + n:16], lk + " " + key) for i in range(16)]
+        mm(out, bank, items)
+
+    dma("y", T.EA[:, 0:128], T.ent[:], "", "EN")
+    dma("s", T.EA[:, 128:256], T.att[:], "", "AT")
+    dma("y", T.VAL[:], T.val[:], "", "VAL")
+    iota("PC1", T.PC1[:, 0:1], [[1, 1]], 0, 1)
+    iota("MI", T.MI[:], [[1, 128]], 0, 0)
+    iota("XF", T.XF[:], [[1, 144]], 0, 0)
+    iota("DI", T.DI[:, 160:320], [[0, 8], [16, 20]], 4160 + CP * (r % 4), 1, "DIk")
+    iota("P", T.P[:, 0:1024], [[1, 64], [128, 16]], 32, 0, "Pa")
+    ms(T.Z[:], 0.0, "Z")
+    ms(T.DI[:, 0:160], float(TR + 31), "DIt")
+    act(T.TA[:, 64:576], T.Z[:], F.Silu, "Z", "TA0")
+    for nm in ("WA", "WB"):
+        dma("y", T[nm][0::16, :], T.DI[:, 0:160], "DIt", nm + "t")
+    for nm in ("WA", "WB"):
+        dma("y", T[nm][1::16, :], T.DI[:, 160:320], "DIk", nm + "k")
+    for h in range(2):
+        dma("y", T.FX[:, 64 * h:64 * h + 64], T.form[h::2, :], "", "FX%d" % h)
+    for ah in range(4):
+        dma("y", T.CL4[ah::4, :], T.cls[:], "", "CL4%d" % ah)
+    ts(T.CI[:, 1:2], T.PC1[:, 0:1], 112, None, A.bitwise_and, None, "PC1", "CI1")
+    ts(T.CI[:, 2:3], T.PC1[:, 0:1], 15, None, A.bitwise_and, None, "PC1", "CI2")
+    ts(T.CI[:, 3:4], T.PC1[:, 0:1], 3, None, A.bitwise_and, None, "PC1", "CI3")
+    cp(T.COL[:, 0:1], T.PC1[:, 0:1], "PC1", "C0")
+    ts(T.MA[:], T.MI[:], 112, None, A.bitwise_and, None, "MI", "MA")
+    cp(T.COL[:, 1:3], T.CI[:, 1:3], "CI1 CI2", "C1")
+    ts(T.COL[:, 3:4], T.CI[:, 3:4], 32.0, None, A.mult, None, "CI3", "C3")
+    ts(T.GT[:], T.XF[:, 0:128], T.COL[:, 0:1], -1.0, A.is_lt, A.mult, "XF C0", "GT")
+    ts(T.IDN[:], T.XF[:, 0:128], T.COL[:, 0:1], None, A.is_equal, None, "XF C0", "IDN")
+    ts(T.IK[:], T.XF[:, 0:128], T.COL[:, 0:1], 1024.0, A.is_equal, A.mult, "XF C0", "IK")
+    ts(T.BLK[:], T.MA[:], T.COL[:, 1:2], None, A.is_equal, None, "MA C1", "BLK")
+    tt(T.GT[:], T.GT[:], T.BLK[:], A.mult, "GT BLK", "GT")
+    tt(T.TRI[:], T.GT[:], T.IK[:], A.add, "GT IK", "TRI")
+
+    ts(T.EL6[:], T.EA[:, 0:128], 63, None, A.bitwise_and, None, "EN", "EL6")
+    ts(T.OWI[:], T.EA[:, 0:128], 6, None, A.arith_shift_right, None, "EN", "OWI")
+    ts(T.K0[:], T.EL6[:], 64.0, 64.0, A.mult, A.add, "EL6", "K0")
+    cp(T.OWB[:], T.OWI[:], "OWI", "OWB")
+    for b in range(4):
+        tt(T.KZ[:, 32 * b:32 * b + 32], T.K0[:, b::4], T.EA[:, 128 + b::4], A.add, "K0 AT", "KZ%d" % b)
+
+    def hot(q):
+        ts(T.O[:, 128 * q:128 * q + 128], T.OWB[:], float(q), None, A.is_equal, None, "OWB", "O%d" % q)
+
+    def scan1(q):
+        o = T.O[:, 128 * q:128 * q + 128]
+        scan(T.S[:, 128 * q:128 * q + 128], o, o, A.add, A.max, "O%d" % q, "S%d" % q)
+
+    for q in range(4):
+        hot(q)
+    op("v", lambda: V.transpose(T.KT[:], T.KZ[:]), "KZ0 KZ1 KZ2 KZ3", "KT")
+    for q in range(4):
+        scan1(q)
+    for q in range(4, 8):
+        hot(q)
+    ts(T.OW8[:], T.OWB[:], 0.125, None, A.mult, None, "OWB", "OW8")
+    for q in range(4, 8):
+        scan1(q)
+    act(T.P[:, 1024:2048], T.P[:, 0:1024], F.Identity, "Pa", "Pb", bias=64.0)
+    for h in range(2):
+        for b in range(4):
+            act(T.KO[:, 64 * h + 16 * b:64 * h + 16 * b + 16], T.KT[:, 32 * b + 16 * h:32 * b + 16 * h + 16], F.Copy, "KT", "KO%d%d" % (h, b))
+        dma("s", T.P[16 * h + 1::32, :], T.KO[:, 64 * h:64 * h + 64], " ".join("KO%d%d" % (h, b) for b in range(4)) + " Pa Pb", "Pk%d" % h)
+    act(T.TA[:, 576:1088], T.Z[:], F.Copy, "Z", "TA1")
+    act(T.TA[:, 1088:1600], T.Z[:], F.Copy, "Z", "TA2")
+    for hf in range(2):
+        ks = range(4 * hf, 4 * hf + 4)
+        mm(T["P%d" % hf][:], "P%d" % hf, [(T.TRI[:], T.O[:, 512 * hf:512 * hf + 512], "TRI " + " ".join("O%d" % q for q in ks)),
+                                          (T.BLK[:], T.S[:, 512 * hf:512 * hf + 512], "BLK " + " ".join("S%d" % q for q in ks))])
+    for hf in range(2):
+        ts(T.X[:, 512 * hf:512 * hf + 512], T["P%d" % hf][:], -1088.0, -64.0, A.add, A.max, "P%d" % hf, "X%d" % hf)
+    mm(T.P2[:, 0:128], "P2", [(T.IDN[:], T.OW8[:], "IDN OW8")] +
+       [(T.IDN[:], T.X[:, 128 * q:128 * q + 128], "X%d" % (q // 4)) for q in range(8)])
+    ts(T.HI[:], T.P2[:, 0:128], 511.0 - 7.9375, 0.0625, A.add, A.mult, "P2", "HI")
+    ts(T.Y1[:], T.P2[:, 0:128], 511.0, 160.0, A.add, A.mult, "P2", "Y1")
+    ts(T.Y2[:], T.HI[:], -2559.0, None, A.mult, None, "HI", "Y2")
+    tt(T.Y3[:], T.Y1[:], T.Y2[:], A.add, "Y1 Y2", "Y3")
+    cp(T.D1[:], T.Y3[:], "Y3", "D1")
+    cp(T.WA[:, 0:2560].indirect(T.D1[:, 0:64]), T.P[:, 0:1024], "D1 Pa Pk0 Pk1", "WAk WAt")
+    act(T.WB[:, 0:2560].indirect(T.D1[:, 64:128]), T.P[:, 1024:2048], F.Silu, "D1 Pb Pk0 Pk1", "WBk WBt")
+    dma("y", T.NA[:, 160:320], T.WA[1::16, :], "WAk", "NAk")
+    dma("s", T.NB[:, 160:320], T.WB[1::16, :], "WBk", "NBk")
+    dma("y", T.NA[:, 0:160], T.WA[0::16, :], "WAt", "NAt")
+    dma("s", T.NB[:, 0:160], T.WB[0::16, :], "WBt", "NBt")
+    for k in range(3, 8):
+        act(T.TA[:, 64 + 512 * k:576 + 512 * k], T.Z[:], F.Copy, "Z", "TA%d" % k)
+    TAK = " ".join("TA%d" % k for k in range(8))
+    dma("g", T.TB[0::16, 64:4160], T.Z[:, 0:256], "Z", "TB")
+    iota("PC", T.PC[:], [[1, 2560]], 32, 0)
+    iota("CL", T.CL[:], [[CO, 8], [0, 16]], 0, 0)
+    for h in range(2):
+        for b in range(4):
+            cp(T.FZ[:, 32 * b + 16 * h:32 * b + 16 * h + 16], T.FX[:, 64 * h + 16 * b:64 * h + 16 * b + 16], "FX%d" % h, "FZ%d%d" % (h, b))
+    ts(T.LC[:], T.CL4[:], T.COL[:, 3:4], None, A.add, None, "CL40 CL41 CL42 CL43 C3", "LC")
+    op("v", lambda: V.transpose(T.FW[:], T.FZ[:]), " ".join("FZ%d%d" % (h, b) for h in range(2) for b in range(4)), "FW")
+    ms(T.EL[:, 80:96], -1.0, "ELs")
+    ms(T.R2[:, L:L + 8], 0.0, "R2s")
+    cp(T.FE[:], T.FW[:, 0:128].indirect(T.LC[:]), "FW LC", "FE")
+    ts(T.BS[:], T.XF[:], T.COL[:, 1:2], 15.0, A.subtract, A.is_equal, "XF C1", "BS")
+    tt(T.NM[:, 160:320], T.NA[:, 160:320], T.NB[:, 160:320], A.min, "NAk NBk", "NMk")
+    ts(T.KS[:], T.NM[:, 160:320], 0.25, None, A.add, None, "NMk", "KS")
+    tt(T.NM[:, 0:160], T.NA[:, 0:160], T.NB[:, 0:160], A.min, "NAt NBt", "NMt")
+    ts(T.TS[:], T.NM[:, 0:160], -31.75, None, A.add, None, "NMt", "TS")
+    exchange(lambda k: T.KS[:, 20 * k:20 * k + 20], T.KR[:, 20 * r:20 * r + 20], "aK", "KS CL ELs R2s", "KR")
+    cp(T.S1[:, 0:L], T.VAL[:, 0:TR].indirect(T.TS[:, 0:80]), "VAL TS", "S1a")
+    act(T.S1[:, L:2 * L], T.VAL[:, 0:TR].indirect(T.TS[:, 80:160]), F.Copy, "VAL TS", "S1b")
+    exchange(lambda k: T.S1[:, CP * k:CP * k + CP], T.R1[:, CP * r:CP * r + CP], "aV", "S1a S1b", "R1")
+    for k in range(2):
+        iota("E64", T.E64[:, 256 * k:256 * k + 256], [[64, 16], [1024, 4], [0, 4]], 0, 0, "E64%d" % k)
+
+    cp(T.TA[:, 0:TW].indirect(T.KR[:, 0:80]), T.PC[:, 0:L], "KR PC", TAK)
+    act(T.TB[:, 0:TW].indirect(T.KR[:, 80:160]), T.PC[:, L:2 * L], F.Silu, "KR PC", "TB")
+    dma("g", T.TA[0::16, 64:4160], T.TB[0::16, 64:4160], "TB " + TAK, TAK, accum_op=A.add, max_dma_last_dim=2048)
+    iota("KC", T.KC[:], [[0, 8], [1, 32]], 0, 0)
+    iota("K160", T.K160[:], [[1, CO]], 0, 0)
+    iota("D32", T.D32[:], [[32, 8], [0, 10]], 0, 0)
+    iota("PI", T.PI[:, 0:4], [[2, 4]], 0, 0)
+    iota("JN", T.JN[:], [[16, 80]], 0, 0)
+    iota("U0", T.U0[:], [[1, 64]], L + 1, 0)
+    iota("K1", T.K1[:], [[0, 8], [1, CO]], 1025, 0)
+    iota("EW", T.EW[:], [[0, 1536]], -1, 0)
+    ts(T.FF[:, 0:256], T.FE[:], 63, None, A.bitwise_and, None, "FE", "FF0")
+    ts(T.FF[:, 256:512], T.FE[:], 6, None, A.arith_shift_right, None, "FE", "FF1")
+    tt(T.FG[:], T.FF[:], T.E64[:], A.add, "FF0 FF1 E640 E641", "FG")
+    ts(T.BW[:], T.BS[:], T.COL[:, 2:3], None, A.mult, None, "BS C1", "BW")
+    cp(T.LL[:], T.FG[:], "FG", "LL")
+    cp(T.BH[:], T.BS[:], "BS", "BH")
+    act(T.G1[:], T.TA[:, 64:4160].indirect(T.LL[:, 0:256]), F.Copy, TAK + " LL", "G1")
+    cp(T.TB[:, 0:4096], T.TA[:, 64:4160].indirect(T.LL[:, 256:512]), TAK + " LL", "TB")
+    dma("s", T.N1[:], T.G1[0::16, :], "G1", "N1")
+    dma("y", T.N2[:], T.TB[0::16, 0:4096], "TB", "N2")
+    ms(T.JW[:], 0.0, "JW")
+    ms(T.CW[:, 256:264], 0.0, "CWs")
+    ms(T.H1[:, 256:264], 0.0, "H1s")
+    ms(T.H2[:, 256:264], 0.0, "H2s")
+    ms(T.INC[:, 0:1], 0.0, "INC0")
+    ms(T.EM[:, 64:65], 0.0, "EMs")
+    ms(T.DD[:, 63:64], 128.0, "DDs")
+    ts(T.CI[:, 4:5], T.PC1[:, 0:1], 7, None, A.bitwise_and, None, "PC1", "CI4")
+    ts(T.CI[:, 5:6], T.PC1[:, 0:1], 3, 1, A.arith_shift_right, A.bitwise_and, "PC1", "CI5")
+    ts(T.MA[:], T.MI[:], 15, None, A.bitwise_and, None, "MI", "MA")
+    ts(T.COL[:, 4:5], T.CI[:, 4:5], 16.0, None, A.mult, None, "CI4", "C4")
+    ts(T.MK[:], T.MA[:, 0:64], T.COL[:, 2:3], None, A.is_equal, None, "MA C1", "MK")
+    tt(T.COL[:, 5:6], T.COL[:, 4:5], T.CI[:, 5:6], A.add, "C4 CI5", "C5")
+    ts(T.JN[:], T.JN[:], T.COL[:, 2:3], None, A.add, None, "JN C1", "JN")
+    ts(T.PU[:, 0:4], T.PI[:, 0:4], T.COL[:, 5:6], 8.0, A.add, A.add, "PI C5", "PU0")
+    ts(T.PU[:, 4:8], T.PI[:, 0:4], T.COL[:, 5:6], 7.0, A.add, A.add, "PI C5", "PU1")
+    for u in range(4):
+        tt(T.MN[:, u::4], T.N1[:, 64 * u:64 * u + 64], T.N2[:, 64 * u:64 * u + 64], A.min, "N1 N2", "MN%d" % u)
+    ts(T.PR[:], T.MN[:], 1.0, None, A.is_gt, None, "MN0 MN1 MN2 MN3", "PR")
+    scan(T.S2[:], T.KC[:], T.PR[:], A.min, A.add, "KC PR", "S2")
+    for nm, src in (("H2", "N2"), ("H1", "N1")):
+        for u in range(4):
+            act(T[nm][:, u:256:4], T[src][:, 64 * u:64 * u + 64], F.Identity, src, "%s%d" % (nm, u), bias=-MID)
+    diag(T.P3[:, 0:16], "P3", T.BS, "BS", [(T.S2, 0, 256, "S2")])
+    mm(T.P4[:, 0:64], "P4", [(T.BLK[:], T.S2[:, 3::4], "BLK S2")])
+    mm(T.P5[:, 0:256], "P5", [(T.TRI[:], T.PR[:], "TRI PR"), (T.BLK[:], T.S2[:], "BLK S2")])
+    act(T.CS[:], T.P4[:, 0:64], F.Identity, "P4", "CS", bias=float(CO * r))
+    act(T.CW[:, 0:256], T.P5[:, 0:256], F.Copy, "P5", "CW")
+    exchange(lambda k: T.CS[:, 8 * k:8 * k + 8], T.CL[:, 16 * r + 8:16 * r + 16], "aC", "CS", "CL")
+    for hf in range(2):
+        for d in range(N):
+            ts(T.CM[:, L * hf + CO * d:L * hf + CO * d + CO], T.K160[:], T.P3[:, 2 * d + hf:2 * d + hf + 1], None, A.is_ge, None,
+               "K160 P3", "CM%d%d" % (hf, d))
+    diag(T.P6[:, 0:80], "P6", T.BS, "BS", [(T.CM, L * hf, L, " ".join("CM%d%d" % (hf, d) for d in range(N))) for hf in range(2)],
+         [(T.IDN[:], T.D32[:], "IDN D32")])
+    cp(T.LB[:], T.P6[:, 0:80], "P6", "LB")
+    tt(T.M[:], T.CW[:, 0:264].indirect(T.LB[:]), T.K1[:], A.is_equal, "CW CWs LB K1", "M")
+    cp(T.BI[:], T.P6[:, 0:80], "P6", "BI")
+    tt(T.X2[:], T.H2[:, 0:264].indirect(T.LB[:]), T.M[:], A.mult, "H20 H21 H22 H23 H2s LB M", "X2")
+    ts(T.BU[:], T.BI[:], 3, None, A.bitwise_and, None, "BI", "BU")
+    diag(T.P7[:, 0:80], "P7", T.BW, "BW", [(T.M, 0, L, "M")])
+    diag(T.P0[:, 0:80], "P0", T.BH, "BH", [(T.X2, 0, L, "X2")])
+    cp(T.IS[:], T.CL[:, 0:128].indirect(T.PU[:, 0:4]), "CL PU0", "IS")
+    cp(T.EX[:], T.CL[:, 0:128].indirect(T.PU[:, 4:8]), "CL PU1", "EX")
+    ts(T.UE[:], T.BU[:], 16.0, 64.0 * r, A.mult, A.add, "BU", "UE")
+    tt(T.NS[:], T.IS[:], T.EX[:], A.subtract, "IS EX", "NS")
+    tt(T.ES[:], T.P7[:, 0:80], T.UE[:], A.add, "P7 UE", "ES")
+    exchange(lambda k: T.ES[:, 10 * k:10 * k + 10], T.EL[:, 10 * r:10 * r + 10], "aE", "ES", "EL")
+    dma("y", T.EW[0::16, :], T.EL[:], "EL ELs", "EW")
+    tt(T.X1[:], T.H1[:, 0:264].indirect(T.LB[:]), T.M[:], A.mult, "H10 H11 H12 H13 H1s LB M", "X1")
+    ts(T.L2[:], T.P0[:, 0:80], MID - 32.0, None, A.add, None, "P0", "L2")
+    diag(T.P1[:, 0:80], "P1", T.BH, "BH", [(T.X1, 0, L, "X1")])
+    halves = sorted([range(0, 4), range(4, 8)], key=lambda h: r in h)
+    for h in halves:
+        act(T.GV[:, CO * h[0]:CO * h[0] + 640], T.R1[:, 0:2560].indirect(T.L2[:, 10 * h[0]:10 * h[0] + 40]), F.Copy, "R1 L2", "GV%d" % h[0])
+    scan(T.INC[:, 1:65], T.NS[:], T.NS[:], A.add, A.max, "NS", "INC")
+    ts(T.EM[:, 0:64], T.NS[:], 0.0, None, A.is_equal, None, "NS", "EM")
+    ts(T.SG[:, 0:64], T.NS[:], 0.0, 0.0625, A.is_gt, A.mult, "NS", "NZ")
+    tt(T.DL[:], T.IS[:], T.INC[:, 1:65], A.subtract, "IS INC", "DL")
+    tt(T.SM[:, 0:64], T.EM[:, 1:65], T.U0[:], A.mult, "EM EMs U0", "O1")
+    tt(T.SG[:, 64:128], T.DL[:], T.SG[:, 0:64], A.mult, "DL NZ", "DN")
+    tt(T.SM[:, 64:128], T.SM[:, 0:64], T.INC[:, 1:65], A.max, "O1 INC", "OF")
+    scan(T.SG[:, 128:192], T.EM[:, 0:64], T.SG[:, 64:128], A.mult, A.add, "EM DN", "CA")
+    tt(T.SM[:, 0:64], T.SM[:, 64:128], T.MK[:], A.mult, "OF MK", "O1")
+    tt(T.DD[:, 0:63], T.SG[:, 129:192], T.SG[:, 128:191], A.subtract, "CA", "DD")
+    for k in range(4):
+        op("v", lambda k=k: V.tensor_reduce(T.SC[:, k:k + 1], T.SM[:, 16 * k:16 * k + 16], AxisListType.X, A.add), "O1", "SC%d" % k)
+    ts(T.L1[:], T.P1[:, 0:80], MID - 32.0, None, A.add, None, "P1", "L1")
+    cp(T.SO[:], T.SC[:, 0:4], "SC0 SC1 SC2 SC3", "SO")
+    for h in halves:
+        c0 = CO * h[0]
+        tt(T.S2V[:, c0:c0 + 640], T.R1[:, 0:2560].indirect(T.L1[:, 10 * h[0]:10 * h[0] + 40]), T.GV[:, c0:c0 + 640], A.subtract,
+           "R1 L1 GV%d" % h[0], "SV%d" % h[0])
+        ds = [k for k in h if k != r]
+        send(ds, [eng[4 * n:4 * n + 4] for n in range(len(ds))], lambda k: T.S2V[:, CO * k:CO * k + CO],
+             T.R2[:, CO * r:CO * r + CO], "aY", "SV%d" % h[0])
+    before("y", ["SV%d" % halves[1][0]], [])
+    g.sync.dma_start(T.R2[:, CO * r:CO * r + CO], T.S2V[:, CO * r:CO * r + CO]).then_inc(T.sem.aY, 16)
+    after(bump("aY", 4 * (N - 1) + 16), [], ["R2"])
+    cp(T.JW[:, 0:L + 72].indirect(T.SO[:]), T.DD[:], "SO DD DDs", "JW")
+    tt(T.CN[:], T.INC[:, 8:65:8], T.INC[:, 0:57:8], A.subtract, "INC INC0", "CN")
+    scan(T.JS[:], T.JW[:, 0:L], T.GV[:], A.add, A.min, "JW BIG", "JS") if False else None
+    op("v", lambda: V.tensor_tensor_scan(T.JS[:], T.JW[:, 0:L], T.K1[:], 0.0, A.add, A.min), "JW K1", "JS")
+    dma("s", T.cnt[:], T.CN[0::16, :], "CN", "cnt")
+    diag(T.P2[:, 0:80], "P2", T.BH, "BH", [(T.JS, 0, L, "JS")])
+    tt(T.SR[:], T.P2[:, 0:80], T.JN[:], A.add, "P2 JN", "SR")
+    ts(T.LV[:], T.SR[:], float(L), None, A.min, None, "SR", "LV")
+    ts(T.W1[:], T.SR[:], float(L), -7.5, A.min, A.add, "SR", "W1")
+    ts(T.SQ[:], T.SR[:], float(L), 96.0, A.min, A.mult, "SR", "SQ")
+    act(T.WA[:, 640:L], T.R2[:, 0:L + 8].indirect(T.LV[:, 40:80]), F.Copy, "R2 R2s LV NAk NAt", "YO1")
+    dma("s", T.y[:, 640:L], T.WA[:, 640:L], "YO1", "y1")
+    ts(T.WI[:], T.W1[:], 0.0625, None, A.mult, None, "W1", "WI")
+    ts(T.W2[:], T.WI[:], -1535.0, None, A.mult, None, "WI", "W2")
+    tt(T.W3[:], T.SQ[:], T.W2[:], A.add, "SQ W2", "W3")
+    cp(T.LW[:], T.W3[:], "W3", "LW")
+    cp(T.WA[:, 0:640], T.R2[:, 0:L + 8].indirect(T.LV[:, 0:40]), "R2 R2s LV NAk NAt", "YO0")
+    dma("y", T.y[:, 0:640], T.WA[:, 0:640], "YO0", "y0")
+    cp(T.WB[:, 0:640], T.EW[:, 0:1536].indirect(T.LW[:, 0:40]), "EW LW NBk NBt", "WH0")
+    act(T.WB[:, 640:L], T.EW[:, 0:1536].indirect(T.LW[:, 40:80]), F.Copy, "EW LW NBk NBt", "WH1")
+    dma("y", T.who[:], T.WB[0::16, 0:L], "WH0 WH1", "who")
+    done = [s for (q, s), n in seen.items() if n == total[s]]
+    for s in sorted(total):
+        if s not in done:
+            wait("g", (s, total[s]))

@@ -1,33 +1,34 @@
 from concourse.bass import DstId, RemoteDMATransfer
-from concourse.mybir import AluOpType as A, ActivationFunctionType as F, AxisListType
+from concourse.mybir import AluOpType as A, ActivationFunctionType as F
 
 N, TR, CP, CO, L = 8, 2048, 320, 160, 1280
 TW = 5568
 MID = 1328.0
 f32, bf, i32, u16, f16 = "float32", "bfloat16", "int32", "uint16", "float16"
 SB = {
-    "EA": (256, i32), "VAL": (TR, f32), "FX": (128, i32), "CL4": (16, i32), "Z": (512, f32),
-    "PC1": (8, i32), "MI": (128, i32), "XF": (144, f32), "COL": (8, f32), "CI": (8, i32), "MA": (128, i32),
-    "BLK": (128, bf), "BS": (144, bf), "BW": (144, bf), "BH": (144, f16), "IDN": (128, bf), "GT": (128, bf), "TRI": (128, bf), "IK": (128, bf),
-    "OWI": (128, i32), "OWB": (128, bf), "OW8": (128, bf), "EL6": (128, i32), "K0": (128, f32), "KZ": (128, f32), "KT": (128, f32), "KO": (128, f32),
-    "O": (1024, bf), "S": (1024, bf), "X": (1024, bf), "HI": (128, i32), "Y1": (128, f32), "Y2": (128, f32), "Y3": (128, f32), "D1": (128, u16),
-    "P": (TR, f32), "DI": (320, f32), "WA": (2560, f32), "WB": (2560, f32), "NA": (320, f32), "NB": (320, f32), "NM": (320, f32),
-    "KS": (160, u16), "TS": (160, u16), "KR": (160, u16), "S1": (2560, f32), "R1": (2560, f32), "PC": (2560, f32),
+    "EA": (128, i32), "EB": (256, i32), "VAL": (32 + TR, f32), "FX": (128, i32), "CL4": (16, i32), "Z": (512, f32),
+    "XD": (128, bf), "VB": (128, bf), "PC1": (8, i32), "XF": (144, f32), "COL": (8, f32), "CI": (8, i32),
+    "BA": (128, bf), "BB": (128, bf), "BLK": (128, bf), "GT": (128, bf), "IK": (128, bf), "TRI": (128, bf), "IB": (128, bf),
+    "IM": (7 * 128, f16), "BS": (144, bf), "BP": (144, bf), "BH": (144, f16), "BLH": (128, f16), "D4": (8, bf), "IDN": (128, bf),
+    "OWB": (128, bf), "K0": (128, f32), "KZ": (128, f32), "KT": (128, f32),
+    "O": (1024, bf), "S": (1024, bf), "X": (1024, f16), "HB": (128, f16), "D1": (128, u16),
+    "P": (TR, f32), "DI": (320, f32), "WA": (2560, f32), "WB": (2560, f32), "NA": (320, f32), "NB": (320, f32),
+    "KS": (160, f32), "KF": (160, f32), "TS": (160, u16), "KR": (160, u16), "S1": (2560, f32), "R1": (32 + 2560, f32), "PC": (2560, f32),
     "TA": (TW, f32), "TB": (TW, f32), "FZ": (128, f32), "FW": (128, f32), "LC": (16, u16), "FE": (256, i32), "FF": (512, i32),
-    "E64": (512, i32), "FG": (512, i32), "LL": (512, u16), "G1": (4096, f32), "N1": (256, f32), "N2": (256, f32),
-    "MN": (256, f32), "PR": (256, bf), "KC": (256, bf), "S2": (256, bf), "CW": (264, f32), "H1": (264, f32), "H2": (264, f32),
-    "CS": (64, f32), "CL": (128, f32), "K160": (160, bf), "CM": (2560, bf), "D32": (80, bf), "LB": (80, u16), "K1": (L, f32),
-    "M": (L, bf), "X1": (L, f16), "X2": (L, f16), "L1": (80, u16), "L2": (80, u16), "GV": (L, f32), "S2V": (L, f32), "R2": (L + 8, f32),
-    "BI": (80, i32), "BU": (80, i32), "UE": (80, f32), "ES": (80, f32), "EL": (96, f32), "EW": (1536, f32),
-    "PI": (8, f32), "PU": (8, u16), "IS": (64, f32), "EX": (64, f32), "NS": (64, f32), "INC": (72, f32), "DL": (64, f32), "DD": (64, f32),
-    "EM": (72, f32), "SG": (192, f32), "U0": (64, f32), "MK": (64, f32), "SM": (128, f32), "SC": (8, f32), "SO": (4, u16), "CN": (8, f32),
-    "JW": (L + 72, f32), "JS": (L, f16), "JN": (80, f32),
-    "SR": (80, f32), "SQ": (80, f32), "LV": (80, u16), "WI": (80, i32), "W1": (80, f32), "W2": (80, f32), "W3": (80, f32), "LW": (80, u16),
+    "E64": (256, i32), "FG": (512, i32), "LL": (512, u16), "G": (8192, f32), "NN": (512, f32),
+    "MN": (256, bf), "PR": (256, bf), "KC": (128, bf), "S2": (256, bf), "CW": (272, f32),
+    "CS": (64, f32), "CL": (128, f32), "KP": (CO, bf), "CM": (2560, bf), "D32": (40, bf), "LB": (80, u16), "K1": (640, bf),
+    "C16": (80, f16), "AH": (80, f16), "PH": (80, f16), "C": (L, bf), "LP": (80, u16), "XN": (2560, f16), "LN": (160, u16),
+    "GV": (L, f32), "SV": (L, f32), "R2": (L + 8, f32), "ES": (80, f32), "EL": (96, f32),
+    "PI": (8, f32), "PU": (8, u16), "IS": (64, f32), "EX": (64, f32), "NS": (64, f32), "INC": (72, f32), "DL": (72, f32),
+    "SJ": (128, f16), "SH": (8, i32), "SG": (16, f32), "XP": (128, f16), "LK": (512, f16), "RA": (320, f16), "RB": (320, f16),
+    "CB": (80, bf), "JN": (80, f16), "EO": (80, f16), "CN": (8, f32), "LV": (80, u16), "SF": (80, f16), "HF": (80, f16), "LW": (80, u16),
 }
 SCRATCH = {k: ("sbuf", [128, w], t) for k, (w, t) in SB.items()}
 SCRATCH.update({"P%d" % k: ("psum", [128, 512], f32) for k in range(8)})
-ND = 40
+ND = 44
 SEMAPHORES = ["cv", "cs", "cp", "cg", "ls", "aK", "aV", "aC", "aE", "aY"] + ["d%d" % k for k in range(ND)]
+MULT = [1.0, 140.0, 2.0, -127.0, -64.0, 96.0, -1535.0]
 
 
 def rank_program(g, core, T, topo):
@@ -81,13 +82,13 @@ def rank_program(g, core, T, topo):
         Q[q].dma_start(out, in_, **kw).then_inc(T.sem[s], 16)
         after(bump(s, 16), rd, wr)
 
-    def mm(out, bank, items):
+    def mm(bank, items, start=True):
         before("p", [], [bank])
         allr = []
-        for n, (lt, rh, rd) in enumerate(items):
+        for n, (out, lt, rh, rd) in enumerate(items):
             before("p", rd.split(), [])
             allr += rd.split()
-            ins = g.tensor.matmul(out, lt, rh, n == 0, n == len(items) - 1)
+            ins = g.tensor.matmul(out, lt, rh, start and n == 0, n == len(items) - 1)
         ins.then_inc(T.sem.cp, 1)
         after(bump("cp", 1), allr, [bank])
 
@@ -114,14 +115,31 @@ def rank_program(g, core, T, topo):
     def act(out, a, fn, rd, wr, **kw):
         op("s", lambda: S.activation(out, a, fn, **kw), rd, wr)
 
+    def lin(out, a, scale, bias, rd, wr):
+        act(out, a, F.Identity, rd, wr, scale=scale, bias=bias)
+
     def iota(name, out, pat, base, cm, wr=None):
         kw = {} if SB[name][1] == i32 else {"allow_small_or_imprecise_dtypes": True}
         op("g", lambda: g.iota(out, pat, base, cm, **kw), "", wr or name)
+
+    def im(c):
+        k = MULT.index(c)
+        return T.IM[:, 128 * k:128 * k + 128]
+
+    def keys(fmt, *rng):
+        out = [fmt]
+        for n in rng:
+            out = [s.replace("#", str(k), 1) for s in out for k in (range(n) if isinstance(n, int) else n)]
+        return " ".join(out)
 
     cores = list(T.cores)
     far = [k for k in range(N) if topo.die(cores[k]) != topo.die(core)]
     near = [k for k in range(N) if k != r and k not in far]
     eng = topo.engines(core, cores[far[0]])
+    ev, od = eng[0::2], eng[1::2]
+    pairs = {k: ev[2 * n:2 * n + 2] for n, k in enumerate(far)}
+    pairs.update({k: od[2 * n:2 * n + 2] for n, k in enumerate(near)})
+    halves = sorted([0, 1], key=lambda h: h == r // 4)
 
     def send(dests, masks, src, dst, sem, rd):
         before("g", rd.split(), [])
@@ -133,250 +151,356 @@ def rank_program(g, core, T, topo):
         g.remote_dma_fused(trs, local_sem=T.sem.ls)
         bump("ls", sum(len(m) for m in masks))
 
-    def exchange(src, dst, sem, rd, key):
-        ev, od = eng[0::2], eng[1::2]
-        masks = [ev[2 * n:2 * n + 2] for n in range(len(far))] + [od[2 * n:2 * n + 2] for n in range(len(near))]
-        send(far + near, masks, src, dst, sem, rd)
-        before("y", rd.split(), [key])
-        g.sync.dma_start(dst, src(r)).then_inc(T.sem[sem], 16)
-        after(bump(sem, 2 * (N - 1) + 16), [], [key])
+    def lands(sem, n, key):
+        after(bump(sem, n * (N - 1)), [], [key])
 
-    def diag(out, bank, lhs, lk, srcs, extra=()):
-        items = list(extra)
-        for buf, c0, n, key in srcs:
-            items += [(lhs[:, 15 - i:143 - i], buf[:, c0 + i:c0 + n:16], lk + " " + key) for i in range(16)]
-        mm(out, bank, items)
+    def diag(out, lhs, lk, buf, c0, n, key):
+        return [(out, lhs[:, 15 - i:143 - i], buf[:, c0 + i:c0 + n:16], lk + " " + key) for i in range(16)]
 
-    dma("y", T.EA[:, 0:128], T.ent[:], "", "EN")
-    dma("s", T.EA[:, 128:256], T.att[:], "", "AT")
-    dma("y", T.VAL[:], T.val[:], "", "VAL")
-    iota("PC1", T.PC1[:, 0:1], [[1, 1]], 0, 1)
-    iota("MI", T.MI[:], [[1, 128]], 0, 0)
-    iota("XF", T.XF[:], [[1, 144]], 0, 0)
-    iota("DI", T.DI[:, 160:320], [[0, 8], [16, 20]], 4160 + CP * (r % 4), 1, "DIk")
-    iota("P", T.P[:, 0:1024], [[1, 64], [128, 16]], 32, 0, "Pa")
-    ms(T.Z[:], 0.0, "Z")
+    def pieces(c0, c1):
+        cuts = sorted({c0, c1} | ({r, r + 1} if c0 <= r < c1 else set()))
+        return list(zip(cuts[:-1], cuts[1:]))
+
+    for h in range(2):
+        dma("ys"[h], T.EA[:, 64 * h:64 * h + 64], T.ent[:, 1024 * h:1024 * h + 1024], "", "EA%d" % h)
+    for h in range(2):
+        dma("y", T.EB[:, 64 * h:64 * h + 64], T.ent[h::2, :], "", "EB%d" % h)
+        dma("s", T.EB[:, 128 + 64 * h:192 + 64 * h], T.att[h::2, :], "", "AB%d" % h)
+    dma("y", T.VAL[:, 32:], T.val[:], "", "VAL")
+    iota("VB", T.VB[:], [[16, 8], [0, 16]], 0, -1)
+    iota("XD", T.XD[:], [[1, 128]], 0, -1)
+    iota("P", T.P[:, 0:1024], [[1, 32], [1024, 2], [64, 16]], 32, 0, "Pa")
+    iota("DI", T.DI[:, 160:320], [[4096, 8], [16, 20]], 4160 + CP * (r % 4), 1, "DIk")
+    ms(T.Z[:, 0:64], 0.0, "Z0")
+    act(T.TA[:, 64:128], T.Z[:, 0:64], F.Silu, "Z0", "TA8")
+    ms(T.Z[:, 64:512], 0.0, "Z")
     ms(T.DI[:, 0:160], float(TR + 31), "DIt")
-    act(T.TA[:, 64:576], T.Z[:], F.Silu, "Z", "TA0")
     for nm in ("WA", "WB"):
         dma("y", T[nm][0::16, :], T.DI[:, 0:160], "DIt", nm + "t")
+    ts(T.BA[:], T.VB[:], -16.0, None, A.is_gt, None, "VB", "BA")
+    ts(T.BB[:], T.VB[:], 0.0, None, A.is_gt, None, "VB", "BB")
+    ts(T.GT[:], T.XD[:], 0.0, -1.0, A.is_lt, A.mult, "XD", "GT")
+    ts(T.IK[:], T.XD[:], 0.0, 1024.0, A.is_equal, A.mult, "XD", "IK")
+    tt(T.BLK[:], T.BA[:], T.BB[:], A.subtract, "BA BB", "BLK")
+    tt(T.GT[:], T.GT[:], T.BA[:], A.mult, "GT BA", "GT")
+    ts(im(1.0), T.XD[:], 0.0, None, A.is_equal, None, "XD", "I1")
+    tt(T.TRI[:], T.GT[:], T.IK[:], A.add, "GT IK", "TRI")
     for nm in ("WA", "WB"):
         dma("y", T[nm][1::16, :], T.DI[:, 160:320], "DIk", nm + "k")
+
+    for h in range(2):
+        ts(T.OWB[:, h::2], T.EA[:, 64 * h:64 * h + 64], 1.0 / 64, 129.0 - 63.0 / 128, A.mult, A.add, "EA%d" % h, "OW%d" % h)
+    lin(T.K0[:], T.EB[:, 0:128], 64.0, 64.0, "EB0 EB1", "K0")
+    for hf in range(2):
+        for q in range(4 * hf, 4 * hf + 4):
+            ts(T.O[:, 128 * q:128 * q + 128], T.OWB[:], 129.0 + q, None, A.is_equal, None, "OW0 OW1", "O%d" % q)
+        for q in range(4 * hf, 4 * hf + 4):
+            o = T.O[:, 128 * q:128 * q + 128]
+            scan(T.S[:, 128 * q:128 * q + 128], o, o, A.add, A.max, "O%d" % q, "S%d" % q)
+        ks, out = range(4 * hf, 4 * hf + 4), T["P%d" % hf][:]
+        mm("P%d" % hf, [(out, T.TRI[:], T.O[:, 512 * hf:512 * hf + 512], "TRI " + keys("O#", ks)),
+                        (out, T.BLK[:], T.S[:, 512 * hf:512 * hf + 512], "BLK " + keys("S#", ks))])
+    lin(T.P[:, 1024:2048], T.P[:, 0:1024], 1.0, 32.0, "Pa", "Pb")
+    for h in range(2):
+        for b in range(2):
+            c = 64 * h + b
+            tt(T.KZ[:, 64 * h + 32 * b:64 * h + 32 * b + 32], T.K0[:, c:64 * h + 64:2], T.EB[:, 128 + c:192 + 64 * h:2], A.add, "K0 AB%d" % h, "KZ%d%d" % (h, b))
+    op("v", lambda: V.transpose(T.KT[:], T.KZ[:]), keys("KZ##", 2, 2), "KT")
+    for h in range(2):
+        dma("ys"[h], T.P[16 * h + 1::32, :], T.KT[:, 64 * h:64 * h + 64], "KT Pa Pb", "Pk%d" % h)
     for h in range(2):
         dma("y", T.FX[:, 64 * h:64 * h + 64], T.form[h::2, :], "", "FX%d" % h)
     for ah in range(4):
         dma("y", T.CL4[ah::4, :], T.cls[:], "", "CL4%d" % ah)
-    ts(T.CI[:, 1:2], T.PC1[:, 0:1], 112, None, A.bitwise_and, None, "PC1", "CI1")
-    ts(T.CI[:, 2:3], T.PC1[:, 0:1], 15, None, A.bitwise_and, None, "PC1", "CI2")
-    ts(T.CI[:, 3:4], T.PC1[:, 0:1], 3, None, A.bitwise_and, None, "PC1", "CI3")
-    cp(T.COL[:, 0:1], T.PC1[:, 0:1], "PC1", "C0")
-    ts(T.MA[:], T.MI[:], 112, None, A.bitwise_and, None, "MI", "MA")
-    cp(T.COL[:, 1:3], T.CI[:, 1:3], "CI1 CI2", "C1")
-    ts(T.COL[:, 3:4], T.CI[:, 3:4], 32.0, None, A.mult, None, "CI3", "C3")
-    ts(T.GT[:], T.XF[:, 0:128], T.COL[:, 0:1], -1.0, A.is_lt, A.mult, "XF C0", "GT")
-    ts(T.IDN[:], T.XF[:, 0:128], T.COL[:, 0:1], None, A.is_equal, None, "XF C0", "IDN")
-    ts(T.IK[:], T.XF[:, 0:128], T.COL[:, 0:1], 1024.0, A.is_equal, A.mult, "XF C0", "IK")
-    ts(T.BLK[:], T.MA[:], T.COL[:, 1:2], None, A.is_equal, None, "MA C1", "BLK")
-    tt(T.GT[:], T.GT[:], T.BLK[:], A.mult, "GT BLK", "GT")
-    tt(T.TRI[:], T.GT[:], T.IK[:], A.add, "GT IK", "TRI")
-
-    ts(T.EL6[:], T.EA[:, 0:128], 63, None, A.bitwise_and, None, "EN", "EL6")
-    ts(T.OWI[:], T.EA[:, 0:128], 6, None, A.arith_shift_right, None, "EN", "OWI")
-    ts(T.K0[:], T.EL6[:], 64.0, 64.0, A.mult, A.add, "EL6", "K0")
-    cp(T.OWB[:], T.OWI[:], "OWI", "OWB")
-    for b in range(4):
-        tt(T.KZ[:, 32 * b:32 * b + 32], T.K0[:, b::4], T.EA[:, 128 + b::4], A.add, "K0 AT", "KZ%d" % b)
-
-    def hot(q):
-        ts(T.O[:, 128 * q:128 * q + 128], T.OWB[:], float(q), None, A.is_equal, None, "OWB", "O%d" % q)
-
-    def scan1(q):
-        o = T.O[:, 128 * q:128 * q + 128]
-        scan(T.S[:, 128 * q:128 * q + 128], o, o, A.add, A.max, "O%d" % q, "S%d" % q)
-
-    for q in range(4):
-        hot(q)
-    op("v", lambda: V.transpose(T.KT[:], T.KZ[:]), "KZ0 KZ1 KZ2 KZ3", "KT")
-    for q in range(4):
-        scan1(q)
-    for q in range(4, 8):
-        hot(q)
-    ts(T.OW8[:], T.OWB[:], 0.125, None, A.mult, None, "OWB", "OW8")
-    for q in range(4, 8):
-        scan1(q)
-    act(T.P[:, 1024:2048], T.P[:, 0:1024], F.Identity, "Pa", "Pb", bias=64.0)
-    for h in range(2):
-        for b in range(4):
-            act(T.KO[:, 64 * h + 16 * b:64 * h + 16 * b + 16], T.KT[:, 32 * b + 16 * h:32 * b + 16 * h + 16], F.Copy, "KT", "KO%d%d" % (h, b))
-        dma("s", T.P[16 * h + 1::32, :], T.KO[:, 64 * h:64 * h + 64], " ".join("KO%d%d" % (h, b) for b in range(4)) + " Pa Pb", "Pk%d" % h)
-    act(T.TA[:, 576:1088], T.Z[:], F.Copy, "Z", "TA1")
-    act(T.TA[:, 1088:1600], T.Z[:], F.Copy, "Z", "TA2")
-    for hf in range(2):
-        ks = range(4 * hf, 4 * hf + 4)
-        mm(T["P%d" % hf][:], "P%d" % hf, [(T.TRI[:], T.O[:, 512 * hf:512 * hf + 512], "TRI " + " ".join("O%d" % q for q in ks)),
-                                          (T.BLK[:], T.S[:, 512 * hf:512 * hf + 512], "BLK " + " ".join("S%d" % q for q in ks))])
-    for hf in range(2):
-        ts(T.X[:, 512 * hf:512 * hf + 512], T["P%d" % hf][:], -1088.0, -64.0, A.add, A.max, "P%d" % hf, "X%d" % hf)
-    mm(T.P2[:, 0:128], "P2", [(T.IDN[:], T.OW8[:], "IDN OW8")] +
-       [(T.IDN[:], T.X[:, 128 * q:128 * q + 128], "X%d" % (q // 4)) for q in range(8)])
-    ts(T.HI[:], T.P2[:, 0:128], 511.0 - 7.9375, 0.0625, A.add, A.mult, "P2", "HI")
-    ts(T.Y1[:], T.P2[:, 0:128], 511.0, 160.0, A.add, A.mult, "P2", "Y1")
-    ts(T.Y2[:], T.HI[:], -2559.0, None, A.mult, None, "HI", "Y2")
-    tt(T.Y3[:], T.Y1[:], T.Y2[:], A.add, "Y1 Y2", "Y3")
-    cp(T.D1[:], T.Y3[:], "Y3", "D1")
+    act(T.X[:, 0:512], T.P0[:], F.Relu, "P0", "X0", bias=-1024.0)
+    ts(T.X[:, 512:1024], T.P1[:], -1024.0, 0.0, A.add, A.max, "P1", "X1")
+    ts(im(140.0), T.XD[:], 0.0, 140.0, A.is_equal, A.mult, "XD", "I140")
+    ts(T.IB[:], T.XD[:], 0.0, 20.0, A.is_equal, A.mult, "XD", "IB")
+    mm("P2", [(T.P2[:, 0:128], im(1.0), T.X[:, 128 * q:128 * q + 128], "I1 X%d" % (q // 4)) for q in range(8)])
+    act(T.TA[:, 128:576], T.Z[:, 64:512], F.Copy, "Z", "TA0")
+    for k in range(1, 3):
+        act(T.TA[:, 64 + 512 * k:576 + 512 * k], T.Z[:], F.Copy, "Z0 Z", "TA%d" % k)
+    ts(T.HB[:], T.P2[:, 0:128], 20489.5, 0.05, A.add, A.mult, "P2", "HB")
+    out = T.P3[:, 0:128]
+    mm("P3", [(out, T.IB[:], T.OWB[:], "IB OW0 OW1")] + [(out, im(1.0), T.X[:, 128 * q:128 * q + 128], "X%d" % (q // 4)) for q in range(8)] +
+       [(out, im(140.0), T.HB[:], "I140 HB")])
+    ts(T.D1[:], out, -(1.0 + 140 * 1025 + 20 * 129), None, A.add, None, "P3", "D1")
     cp(T.WA[:, 0:2560].indirect(T.D1[:, 0:64]), T.P[:, 0:1024], "D1 Pa Pk0 Pk1", "WAk WAt")
     act(T.WB[:, 0:2560].indirect(T.D1[:, 64:128]), T.P[:, 1024:2048], F.Silu, "D1 Pb Pk0 Pk1", "WBk WBt")
     dma("y", T.NA[:, 160:320], T.WA[1::16, :], "WAk", "NAk")
     dma("s", T.NB[:, 160:320], T.WB[1::16, :], "WBk", "NBk")
     dma("y", T.NA[:, 0:160], T.WA[0::16, :], "WAt", "NAt")
     dma("s", T.NB[:, 0:160], T.WB[0::16, :], "WBt", "NBt")
-    for k in range(3, 8):
-        act(T.TA[:, 64 + 512 * k:576 + 512 * k], T.Z[:], F.Copy, "Z", "TA%d" % k)
-    TAK = " ".join("TA%d" % k for k in range(8))
-    dma("g", T.TB[0::16, 64:4160], T.Z[:, 0:256], "Z", "TB")
-    iota("PC", T.PC[:], [[1, 2560]], 32, 0)
-    iota("CL", T.CL[:], [[CO, 8], [0, 16]], 0, 0)
+    for k in range(3, 7):
+        act(T.TA[:, 64 + 512 * k:576 + 512 * k], T.Z[:], F.Copy, "Z0 Z", "TA%d" % k)
+    iota("PC1", T.PC1[:, 0:1], [[1, 1]], 0, 1)
+    iota("XF", T.XF[:], [[1, 144]], 0, 0)
+    dma("g", T.TB[0::16, 64:4160], T.Z[:, 64:320], "Z", "TB")
+    iota("PC", T.PC[:, 0:L], [[1, L]], 32, 0, "PCa")
+    iota("CL", T.CL[:], [[CO, 8], [0, 16]], 0, 0, "CLi")
+    iota("E64", T.E64[:], [[64, 16], [1024, 4], [0, 4]], 0, 0)
+    iota("KC", T.KC[:], [[0, 4], [1, 32]], 0, 0)
+    iota("KP", T.KP[:], [[1, 16], [16, 10]], 0, 0)
+    for k, m in ((1, 112), (2, 15), (3, 3), (4, 7)):
+        ts(T.CI[:, k:k + 1], T.PC1[:, 0:1], m, None, A.bitwise_and, None, "PC1", "CI%d" % k)
     for h in range(2):
         for b in range(4):
             cp(T.FZ[:, 32 * b + 16 * h:32 * b + 16 * h + 16], T.FX[:, 64 * h + 16 * b:64 * h + 16 * b + 16], "FX%d" % h, "FZ%d%d" % (h, b))
+    ts(T.COL[:, 3:4], T.CI[:, 3:4], 32.0, None, A.mult, None, "CI3", "C3")
+    op("v", lambda: V.transpose(T.FW[:], T.FZ[:]), keys("FZ##", 2, 4), "FW")
     ts(T.LC[:], T.CL4[:], T.COL[:, 3:4], None, A.add, None, "CL40 CL41 CL42 CL43 C3", "LC")
-    op("v", lambda: V.transpose(T.FW[:], T.FZ[:]), " ".join("FZ%d%d" % (h, b) for h in range(2) for b in range(4)), "FW")
+    cp(T.COL[:, 1:3], T.CI[:, 1:3], "CI1 CI2", "C1")
+    ms(T.VAL[:, 0:32], 0.0, "VALs")
+    ms(T.R1[:, 0:32], 0.0, "R1s")
     ms(T.EL[:, 80:96], -1.0, "ELs")
     ms(T.R2[:, L:L + 8], 0.0, "R2s")
+    tt(T.KS[:], T.NA[:, 160:320], T.NB[:, 160:320], A.min, "NAk NBk", "KS")
+    send(far + near, [pairs[k] for k in far + near], lambda k: T.KS[:, 20 * k:20 * k + 20], T.KF[:, 20 * r:20 * r + 20], "aK", "KS CLi ELs R2s R1s")
+    lands("aK", 2, "KF")
+    tt(T.TS[:], T.NA[:, 0:160], T.NB[:, 0:160], A.min, "NAt NBt", "TS")
+    act(T.KF[:, 20 * r:20 * r + 20], T.KS[:, 20 * r:20 * r + 20], F.Copy, "KS", "KFo")
+    for hf in range(2):
+        for c0, c1 in pieces(4 * hf, 4 * hf + 4):
+            out = T.R1[:, 32 + CP * r:32 + CP * r + CP] if c0 == r else T.S1[:, CP * c0:CP * c1]
+            win, key = T.VAL[:, 0:32 + TR].indirect(T.TS[:, 20 * c0:20 * c1]), "R1o" if c0 == r else "S1%d" % c0
+            if hf == 0:
+                cp(out, win, "VAL VALs TS", key)
+            else:
+                act(out, win, F.Copy, "VAL VALs TS", key)
+    send(far + near, [pairs[k] for k in far + near], lambda k: T.S1[:, CP * k:CP * k + CP], T.R1[:, 32 + CP * r:32 + CP * r + CP], "aV",
+         keys("S1#", 8))
+    lands("aV", 2, "R1")
+    lin(T.PC[:, L:2 * L], T.PC[:, 0:L], 1.0, float(L), "PCa", "PCb")
+    for k in range(7, 8):
+        act(T.TA[:, 64 + 512 * k:576 + 512 * k], T.Z[:], F.Copy, "Z0 Z", "TA%d" % k)
+    TAK = keys("TA#", 9)
     cp(T.FE[:], T.FW[:, 0:128].indirect(T.LC[:]), "FW LC", "FE")
-    ts(T.BS[:], T.XF[:], T.COL[:, 1:2], 15.0, A.subtract, A.is_equal, "XF C1", "BS")
-    tt(T.NM[:, 160:320], T.NA[:, 160:320], T.NB[:, 160:320], A.min, "NAk NBk", "NMk")
-    ts(T.KS[:], T.NM[:, 160:320], 0.25, None, A.add, None, "NMk", "KS")
-    tt(T.NM[:, 0:160], T.NA[:, 0:160], T.NB[:, 0:160], A.min, "NAt NBt", "NMt")
-    ts(T.TS[:], T.NM[:, 0:160], -31.75, None, A.add, None, "NMt", "TS")
-    exchange(lambda k: T.KS[:, 20 * k:20 * k + 20], T.KR[:, 20 * r:20 * r + 20], "aK", "KS CL ELs R2s", "KR")
-    cp(T.S1[:, 0:L], T.VAL[:, 0:TR].indirect(T.TS[:, 0:80]), "VAL TS", "S1a")
-    act(T.S1[:, L:2 * L], T.VAL[:, 0:TR].indirect(T.TS[:, 80:160]), F.Copy, "VAL TS", "S1b")
-    exchange(lambda k: T.S1[:, CP * k:CP * k + CP], T.R1[:, CP * r:CP * r + CP], "aV", "S1a S1b", "R1")
-    for k in range(2):
-        iota("E64", T.E64[:, 256 * k:256 * k + 256], [[64, 16], [1024, 4], [0, 4]], 0, 0, "E64%d" % k)
-
-    cp(T.TA[:, 0:TW].indirect(T.KR[:, 0:80]), T.PC[:, 0:L], "KR PC", TAK)
-    act(T.TB[:, 0:TW].indirect(T.KR[:, 80:160]), T.PC[:, L:2 * L], F.Silu, "KR PC", "TB")
-    dma("g", T.TA[0::16, 64:4160], T.TB[0::16, 64:4160], "TB " + TAK, TAK, accum_op=A.add, max_dma_last_dim=2048)
-    iota("KC", T.KC[:], [[0, 8], [1, 32]], 0, 0)
-    iota("K160", T.K160[:], [[1, CO]], 0, 0)
-    iota("D32", T.D32[:], [[32, 8], [0, 10]], 0, 0)
-    iota("PI", T.PI[:, 0:4], [[2, 4]], 0, 0)
-    iota("JN", T.JN[:], [[16, 80]], 0, 0)
-    iota("U0", T.U0[:], [[1, 64]], L + 1, 0)
-    iota("K1", T.K1[:], [[0, 8], [1, CO]], 1025, 0)
-    iota("EW", T.EW[:], [[0, 1536]], -1, 0)
     ts(T.FF[:, 0:256], T.FE[:], 63, None, A.bitwise_and, None, "FE", "FF0")
     ts(T.FF[:, 256:512], T.FE[:], 6, None, A.arith_shift_right, None, "FE", "FF1")
-    tt(T.FG[:], T.FF[:], T.E64[:], A.add, "FF0 FF1 E640 E641", "FG")
-    ts(T.BW[:], T.BS[:], T.COL[:, 2:3], None, A.mult, None, "BS C1", "BW")
-    cp(T.LL[:], T.FG[:], "FG", "LL")
-    cp(T.BH[:], T.BS[:], "BS", "BH")
-    act(T.G1[:], T.TA[:, 64:4160].indirect(T.LL[:, 0:256]), F.Copy, TAK + " LL", "G1")
-    cp(T.TB[:, 0:4096], T.TA[:, 64:4160].indirect(T.LL[:, 256:512]), TAK + " LL", "TB")
-    dma("s", T.N1[:], T.G1[0::16, :], "G1", "N1")
-    dma("y", T.N2[:], T.TB[0::16, 0:4096], "TB", "N2")
-    ms(T.JW[:], 0.0, "JW")
-    ms(T.CW[:, 256:264], 0.0, "CWs")
-    ms(T.H1[:, 256:264], 0.0, "H1s")
-    ms(T.H2[:, 256:264], 0.0, "H2s")
+    for w in range(2):
+        tt(T.FG[:, 256 * w:256 * w + 256], T.FF[:, 256 * w:256 * w + 256], T.E64[:], A.add, "FF%d E64" % w, "FG%d" % w)
+    iota("K1", T.K1[:], [[0, 4], [1, CO]], 0, 0)
+    iota("D32", T.D32[:], [[32, 4], [0, 10]], 0, 0)
+    iota("PI", T.PI[:, 0:4], [[2, 4]], 0, 0)
+    iota("CB", T.CB[:], [[16, 80]], 0, 0)
+
+    ts(T.KR[:, 0:80], T.KF[:, 0:80], -4096.0 * r, None, A.add, None, "KF KFo", "KR0")
+    lin(T.KR[:, 80:160], T.KF[:, 80:160], 1.0, -4096.0 * r, "KF KFo", "KR1")
+    cp(T.TA[:, 0:TW].indirect(T.KR[:, 0:80]), T.PC[:, 0:L], "KR0 PCa", TAK)
+    act(T.TB[:, 0:TW].indirect(T.KR[:, 80:160]), T.PC[:, L:2 * L], F.Silu, "KR1 PCb", "TB")
+    dma("g", T.TA[0::16, 64:4160], T.TB[0::16, 64:4160], "TB " + TAK, TAK, accum_op=A.add, max_dma_last_dim=2048)
+    for j, h in enumerate(halves):
+        for w in range(2):
+            for b in range(2):
+                c0 = 128 * (2 * j + w)
+                if w == 0:
+                    cp(T.LL[:, c0 + b:c0 + 128:2], T.FG[:, 2 * h + b:256:4], "FG0", "LL%d%d%d" % (j, w, b))
+                else:
+                    act(T.LL[:, c0 + b:c0 + 128:2], T.FG[:, 256 + 2 * h + b:512:4], F.Copy, "FG1", "LL%d%d%d" % (j, w, b))
+    ts(T.BS[:], T.XF[:], T.COL[:, 1:2], 15.0, A.subtract, A.is_equal, "XF C1", "BS")
+    ts(T.COL[:, 6:7], T.COL[:, 2:3], 0.0, None, A.is_equal, None, "C1", "C6")
+    ts(T.IDN[:], T.XD[:], 0.0, None, A.is_equal, None, "XD", "IDN")
+    tt(T.D4[:, 0:4], T.BLK[:, 0::32], T.BLK[:, 16::32], A.add, "BLK", "D4")
+    for c in MULT[2:]:
+        ts(im(c), T.XD[:], 0.0, c, A.is_equal, A.mult, "XD", "I%d" % c)
+    ts(T.BP[:], T.BS[:], 128.0, None, A.mult, None, "BS", "BP")
+    ts(T.BH[:], T.BS[:], T.COL[:, 6:7], None, A.mult, None, "BS C6", "BH")
+    for j in range(2):
+        ms(T.CW[:, 136 * j + 128:136 * j + 136], 0.0, "CWs%d" % j)
     ms(T.INC[:, 0:1], 0.0, "INC0")
-    ms(T.EM[:, 64:65], 0.0, "EMs")
-    ms(T.DD[:, 63:64], 128.0, "DDs")
-    ts(T.CI[:, 4:5], T.PC1[:, 0:1], 7, None, A.bitwise_and, None, "PC1", "CI4")
+    ms(T.DL[:, 0:1], 0.0, "DL0")
     ts(T.CI[:, 5:6], T.PC1[:, 0:1], 3, 1, A.arith_shift_right, A.bitwise_and, "PC1", "CI5")
-    ts(T.MA[:], T.MI[:], 15, None, A.bitwise_and, None, "MI", "MA")
     ts(T.COL[:, 4:5], T.CI[:, 4:5], 16.0, None, A.mult, None, "CI4", "C4")
-    ts(T.MK[:], T.MA[:, 0:64], T.COL[:, 2:3], None, A.is_equal, None, "MA C1", "MK")
+    act(T.BLH[:], T.BLK[:], F.Copy, "BLK", "BLH")
+    ts(T.XP[:], T.XF[:, 0:128], T.COL[:, 1:2], 100.0, A.subtract, A.add, "XF C1", "XP")
     tt(T.COL[:, 5:6], T.COL[:, 4:5], T.CI[:, 5:6], A.add, "C4 CI5", "C5")
-    ts(T.JN[:], T.JN[:], T.COL[:, 2:3], None, A.add, None, "JN C1", "JN")
+    tt(T.XP[:], T.XP[:], T.BLK[:], A.mult, "XP BLK", "XP")
+    ts(T.JN[:], T.CB[:], T.COL[:, 2:3], None, A.add, None, "CB C1", "JN")
     ts(T.PU[:, 0:4], T.PI[:, 0:4], T.COL[:, 5:6], 8.0, A.add, A.add, "PI C5", "PU0")
     ts(T.PU[:, 4:8], T.PI[:, 0:4], T.COL[:, 5:6], 7.0, A.add, A.add, "PI C5", "PU1")
-    for u in range(4):
-        tt(T.MN[:, u::4], T.N1[:, 64 * u:64 * u + 64], T.N2[:, 64 * u:64 * u + 64], A.min, "N1 N2", "MN%d" % u)
-    ts(T.PR[:], T.MN[:], 1.0, None, A.is_gt, None, "MN0 MN1 MN2 MN3", "PR")
-    scan(T.S2[:], T.KC[:], T.PR[:], A.min, A.add, "KC PR", "S2")
-    for nm, src in (("H2", "N2"), ("H1", "N1")):
+
+    def look(q, j, w, c0, c1, last):
+        b = 2 * j + w
+        out, win = T.G[:, 2048 * b + 16 * c0:2048 * b + 16 * c1], T.TA[:, 64:4160].indirect(T.LL[:, 128 * b + c0:128 * b + c1])
+        rd, wr = TAK + " " + keys("LL%d%d#" % (j, w), 2), "G%d%s" % (b, q)
+        if q == "v":
+            cp(out, win, rd, wr)
+        else:
+            act(out, win, F.Copy, rd, wr)
+        if last:
+            dma("y", T.NN[:, 128 * b:128 * b + 128], T.G[0::16, 2048 * b:2048 * b + 2048], "G%dv G%ds" % (b, b), "N%d" % b)
+
+    look("v", 0, 0, 0, 128, True)
+    look("s", 0, 1, 0, 128, True)
+    look("v", 1, 0, 0, 96, False)
+    look("s", 1, 1, 0, 128, True)
+    look("s", 1, 0, 96, 128, True)
+
+    def bank(j, k):
+        return "P%d" % (4 * j + k), T["P%d" % (4 * j + k)]
+
+    def ranks(j):
+        c0, h = 128 * j, halves[j]
         for u in range(4):
-            act(T[nm][:, u:256:4], T[src][:, 64 * u:64 * u + 64], F.Identity, src, "%s%d" % (nm, u), bias=-MID)
-    diag(T.P3[:, 0:16], "P3", T.BS, "BS", [(T.S2, 0, 256, "S2")])
-    mm(T.P4[:, 0:64], "P4", [(T.BLK[:], T.S2[:, 3::4], "BLK S2")])
-    mm(T.P5[:, 0:256], "P5", [(T.TRI[:], T.PR[:], "TRI PR"), (T.BLK[:], T.S2[:], "BLK S2")])
-    act(T.CS[:], T.P4[:, 0:64], F.Identity, "P4", "CS", bias=float(CO * r))
-    act(T.CW[:, 0:256], T.P5[:, 0:256], F.Copy, "P5", "CW")
-    exchange(lambda k: T.CS[:, 8 * k:8 * k + 8], T.CL[:, 16 * r + 8:16 * r + 16], "aC", "CS", "CL")
+            tt(T.MN[:, c0 + u:c0 + 128:4], T.NN[:, 2 * c0 + 32 * u:2 * c0 + 32 * u + 32], T.NN[:, 2 * c0 + 128 + 32 * u:2 * c0 + 160 + 32 * u], A.min,
+               "N%d N%d" % (2 * j, 2 * j + 1), "MN%d%d" % (j, u))
+        pr, s2 = T.PR[:, c0:c0 + 128], T.S2[:, c0:c0 + 128]
+        ts(pr, T.MN[:, c0:c0 + 128], 1.0, None, A.is_gt, None, keys("MN%d#" % j, 4), "PR%d" % j)
+        scan(s2, T.KC[:], pr, A.min, A.add, "KC PR%d" % j, "S2%d" % j)
+        (n0, b0), (n1, b1) = bank(j, 0), bank(j, 1)
+        mm(n0, [(b0[:, 0:8], s2, T.BLK[:, 0::16], "BLK S2%d" % j)])
+        mm(n1, [(b1[:, 0:128], T.GT[:], pr, "GT PR%d" % j), (b1[:, 0:128], T.BLK[:], s2, "BLK S2%d" % j)])
+        mm(n1, [(b1[:, 128:160], T.BLK[:], T.S2[:, c0 + 3:c0 + 128:4], "BLK S2%d" % j)])
+        act(T.CW[:, 136 * j:136 * j + 128], b1[:, 0:128], F.Copy, n1, "CW%d" % j)
+        lin(T.CS[:, 32 * h:32 * h + 32], b1[:, 128:160], 1.0, float(CO * r), n1, "CS%d" % j)
+        ds = [k for k in range(4 * h, 4 * h + 4) if k != r]
+        send(ds, [pairs[k] for k in ds], lambda k: T.CS[:, 8 * k:8 * k + 8], T.CL[:, 16 * r + 8:16 * r + 16], "aC", "CS%d" % j)
+        if j == 1:
+            act(T.CL[:, 16 * r + 8:16 * r + 16], T.CS[:, 8 * r:8 * r + 8], F.Copy, "CS1 CLi", "CLo")
+            lands("aC", 2, "CL")
+
+    def columns(j):
+        (n0, b0), (n2, b2) = bank(j, 0), bank(j, 2)
+        for gg in range(8):
+            c = L * j + CO * gg
+            ts(T.CM[:, c:c + CO], T.KP[:], b0[:, gg:gg + 1], None, A.is_ge, None, "KP " + n0, "CM%d%d" % (j, gg))
+        mm(n2, [(b2[:, 0:40], T.IDN[:], T.D32[:], "IDN D32")] +
+           [(b2[:, kh:40:10], T.CM[:, L * j + kh:L * j + L:10], T.D4[:, 0:4], "D4 " + keys("CM%d#" % j, 8)) for kh in range(10)])
+        c = slice(40 * j, 40 * j + 40)
+        cp(T.LB[:, c], b2[:, 0:40], n2, "LB%d" % j)
+        lin(T.C16[:, c], b2[:, 0:40], 16.0, 0.0, n2, "C16%d" % j)
+        lin(T.AH[:, c], b2[:, 0:40], 0.25, 1025.0 - 0.375, n2, "AH%d" % j)
+
+    def rows(j):
+        (n1, b1), (n3, b3), c = bank(j, 1), bank(j, 3), slice(40 * j, 40 * j + 40)
+        tt(T.C[:, 640 * j:640 * j + 640], T.CW[:, 136 * j:136 * j + 136].indirect(T.LB[:, c]), T.K1[:], A.is_le,
+           "CW%d CWs%d LB%d K1" % (j, j, j), "C%d" % (10 + j))
+        out = b3[:, 0:40]
+        mm(n3, [(out, im(2.0), T.C16[:, c], "I2 C16%d" % j), (out, im(-127.0), T.AH[:, c], "I-127 AH%d" % j)] +
+           diag(out, T.BP, "BP", T.C, 640 * j, 640, "C%d" % (10 + j)))
+
+    def places(j):
+        (n0, b0), (n1, b1), (n3, b3), c = bank(j, 0), bank(j, 1), bank(j, 3), slice(40 * j, 40 * j + 40)
+        ts(T.LP[:, c], b3[:, 0:40], 127.0 * 1025, 2047.0, A.add, A.min, n3, "LP%d" % j)
+        lin(T.PH[:, c], b3[:, 0:40], 1.0 / 128, 127.0 * 1025 / 128 + 1025.0 - 127.0 / 256, n3, "PH%d" % j)
+        out = b1[:, 0:40]
+        mm(n1, [(out, im(1.0), T.C16[:, c], "I1 C16%d" % j), (out, im(-64.0), T.AH[:, c], "I-64 AH%d" % j), (out, im(1.0), T.PH[:, c], "PH%d" % j)])
+        for w in range(2):
+            b = 2 * j + w
+            out, win = T.XN[:, 640 * b:640 * b + 640], T.G[:, 2048 * b:2048 * b + 2048].indirect(T.LP[:, c])
+            rd = "G%dv G%ds LP%d" % (b, b, j)
+            if w == 0:
+                ts(out, win, -MID, None, A.add, None, rd, "XN%d" % b)
+            else:
+                lin(out, win, 1.0, -MID, rd, "XN%d" % b)
+        h = halves[j]
+        lin(T.ES[:, 40 * h:40 * h + 40], b1[:, 0:40], 1.0, 63.0 * 1025 + 64.0 * r, n1, "ES%d" % j)
+
+    def slots(j):
+        n0, b0 = bank(j, 0)
+        mm(n0, diag(b0[:, 0:80], T.BH, "BH", T.XN, L * j, L, "XN%d XN%d" % (2 * j, 2 * j + 1)))
+
+    def values(j):
+        (n0, b0), (n1, b1), h = bank(j, 0), bank(j, 1), halves[j]
+        ts(T.LN[:, 80 * j:80 * j + 80], b0[:, 0:80], MID, None, A.add, None, n0, "LN%d" % j)
+        win, rd = T.R1[:, 0:32 + 2560], "R1 R1o R1s LN%d" % j
+        act(T.GV[:, 640 * h:640 * h + 640], win.indirect(T.LN[:, 80 * j + 40:80 * j + 80]), F.Copy, rd, "GV%d" % j)
+
+    def derived(j):
+        h = halves[j]
+        win, rd = T.R1[:, 0:32 + 2560], "R1 R1o R1s LN%d GV%d" % (j, j)
+        runs = sorted(pieces(4 * h, 4 * h + 4), key=lambda p: p[0] == r)
+        for c0, c1 in runs:
+            out = T.R2[:, CO * r:CO * r + CO] if c0 == r else T.SV[:, CO * c0:CO * c1]
+            if c0 == r:
+                flush(j)
+            o = 80 * j - 40 * h
+            tt(out, win.indirect(T.LN[:, o + 10 * c0:o + 10 * c1]), T.GV[:, CO * c0:CO * c1], A.subtract, rd, "R2o" if c0 == r else "SV%d" % c0)
+        if j == 0:
+            flush(j)
+
+    def flush(j):
+        ds = [k for k in range(4 * halves[j], 4 * halves[j] + 4) if k != r]
+        send(ds, [eng[4 * n:4 * n + 4] for n in range(len(ds))], lambda k: T.SV[:, CO * k:CO * k + CO], T.R2[:, CO * r:CO * r + CO], "aY",
+             keys("SV#", ds))
+
+    def entities():
+        send(far + near, [pairs[k] for k in far + near], lambda k: T.ES[:, 10 * k:10 * k + 10], T.EL[:, 10 * r:10 * r + 10], "aE", "ES0 ES1")
+        before("y", ["ES1"], [])
+        g.sync.dma_start(T.EL[:, 10 * r:10 * r + 10], T.ES[:, 10 * r:10 * r + 10]).then_inc(T.sem.aE, 16)
+        after(bump("aE", 2 * (N - 1) + 16), [], ["EL"])
+        dma("y", T.PC[0::16, 0:1536], T.EL[:], "EL ELs", "PCa PCb")
+
+    def runs_a():
+        cp(T.IS[:], T.CL[:, 0:128].indirect(T.PU[:, 0:4]), "CL CLo PU0", "IS")
+        cp(T.EX[:], T.CL[:, 0:128].indirect(T.PU[:, 4:8]), "CL CLo PU1", "EX")
+        tt(T.NS[:], T.IS[:], T.EX[:], A.subtract, "IS EX", "NS")
+        scan(T.INC[:, 1:65], T.NS[:], T.NS[:], A.add, A.max, "NS", "INC")
+        tt(T.DL[:, 1:65], T.IS[:], T.INC[:, 1:65], A.subtract, "IS INC", "DL")
+        act(T.SJ[:, 0:64], T.INC[:, 0:64], F.Copy, "INC INC0", "SJ0")
+        tt(T.SJ[:, 64:128], T.DL[:, 1:65], T.DL[:, 0:64], A.subtract, "DL DL0", "SJ1")
+        mm("P2", diag(T.P2[:, 0:8], T.BH, "BH", T.SJ, 0, 128, "SJ0 SJ1"))
+        ts(T.EO[:], T.JN[:], T.INC[:, 64:65], float(L), A.is_ge, A.mult, "JN INC", "EO")
+        tt(T.CN[:], T.INC[:, 8:65:8], T.INC[:, 0:57:8], A.subtract, "INC INC0", "CN")
+        dma("y", T.cnt[:], T.CN[0::16, :], "CN", "cnt")
+
+    def runs_b():
+        ts(T.SH[:, 0:4], T.P2[:, 0:4], -7.5, 0.0625, A.add, A.mult, "P2", "SH")
+        ts(T.SG[:, 0:4], T.SH[:, 0:4], 16.0, None, A.mult, None, "SH", "SG0")
+        ts(T.SG[:, 4:8], T.SH[:, 0:4], -16.0, 100.0, A.mult, A.add, "SH", "SG1")
+        for k in range(4):
+            ts(T.RA[:, 80 * k:80 * k + 80], T.CB[:], T.SG[:, k:k + 1], T.P2[:, 4 + k:5 + k], A.is_gt, A.mult, "CB SG0 P2", "RA%d" % k)
+        tt(T.SG[:, 8:12], T.P2[:, 0:4], T.SG[:, 4:8], A.add, "P2 SG1", "SG2")
+        for k in range(4):
+            ts(T.RB[:, 80 * k:80 * k + 80], T.CB[:], T.SG[:, k:k + 1], T.P2[:, 4 + k:5 + k], A.is_equal, A.mult, "CB SG0 P2", "RB%d" % k)
+        for k in range(4):
+            ts(T.LK[:, 128 * k:128 * k + 128], T.XP[:], T.SG[:, 8 + k:9 + k], None, A.is_ge, None, "XP SG2", "LK%d" % k)
+        out = T.P3[:, 0:80]
+        mm("P3", [(out, im(1.0), T.JN[:], "I1 JN"), (out, im(1.0), T.EO[:], "EO")] +
+           [(out, T.BLH[:], T.RA[:, 80 * k:80 * k + 80], "BLH RA%d" % k) for k in range(4)] +
+           [(out, T.LK[:, 128 * k:128 * k + 128], T.RB[:, 80 * k:80 * k + 80], "LK%d RB%d" % (k, k)) for k in range(4)])
+
+    def runs_c():
+        ts(T.LV[:], T.P3[:, 0:80], float(L), None, A.min, None, "P3", "LV")
+        act(T.SF[:], T.LV[:], F.Copy, "LV", "SF")
+        lin(T.HF[:], T.LV[:], 0.0625, 1025.0 - 15.0 / 32, "LV", "HF")
+        out = T.P2[:, 0:80]
+        mm("P2", [(out, im(96.0), T.SF[:], "I96 SF"), (out, im(-1535.0), T.HF[:], "I-1535 HF")])
+        lin(T.LW[:], T.P2[:, 0:80], 1.0, 1535.0 * 1025, "P2", "LW")
+
+    ranks(0)
+    columns(0)
+    rows(0)
+    ranks(1)
+    places(0)
+    columns(1)
+    slots(0)
+    rows(1)
+    values(0)
+    places(1)
+    slots(1)
+    entities()
+    derived(0)
+    values(1)
+    runs_a()
+    derived(1)
+    runs_b()
+    lands("aY", 4, "R2")
+    runs_c()
     for hf in range(2):
-        for d in range(N):
-            ts(T.CM[:, L * hf + CO * d:L * hf + CO * d + CO], T.K160[:], T.P3[:, 2 * d + hf:2 * d + hf + 1], None, A.is_ge, None,
-               "K160 P3", "CM%d%d" % (hf, d))
-    diag(T.P6[:, 0:80], "P6", T.BS, "BS", [(T.CM, L * hf, L, " ".join("CM%d%d" % (hf, d) for d in range(N))) for hf in range(2)],
-         [(T.IDN[:], T.D32[:], "IDN D32")])
-    cp(T.LB[:], T.P6[:, 0:80], "P6", "LB")
-    tt(T.M[:], T.CW[:, 0:264].indirect(T.LB[:]), T.K1[:], A.is_equal, "CW CWs LB K1", "M")
-    cp(T.BI[:], T.P6[:, 0:80], "P6", "BI")
-    tt(T.X2[:], T.H2[:, 0:264].indirect(T.LB[:]), T.M[:], A.mult, "H20 H21 H22 H23 H2s LB M", "X2")
-    ts(T.BU[:], T.BI[:], 3, None, A.bitwise_and, None, "BI", "BU")
-    diag(T.P7[:, 0:80], "P7", T.BW, "BW", [(T.M, 0, L, "M")])
-    diag(T.P0[:, 0:80], "P0", T.BH, "BH", [(T.X2, 0, L, "X2")])
-    cp(T.IS[:], T.CL[:, 0:128].indirect(T.PU[:, 0:4]), "CL PU0", "IS")
-    cp(T.EX[:], T.CL[:, 0:128].indirect(T.PU[:, 4:8]), "CL PU1", "EX")
-    ts(T.UE[:], T.BU[:], 16.0, 64.0 * r, A.mult, A.add, "BU", "UE")
-    tt(T.NS[:], T.IS[:], T.EX[:], A.subtract, "IS EX", "NS")
-    tt(T.ES[:], T.P7[:, 0:80], T.UE[:], A.add, "P7 UE", "ES")
-    exchange(lambda k: T.ES[:, 10 * k:10 * k + 10], T.EL[:, 10 * r:10 * r + 10], "aE", "ES", "EL")
-    dma("y", T.EW[0::16, :], T.EL[:], "EL ELs", "EW")
-    tt(T.X1[:], T.H1[:, 0:264].indirect(T.LB[:]), T.M[:], A.mult, "H10 H11 H12 H13 H1s LB M", "X1")
-    ts(T.L2[:], T.P0[:, 0:80], MID - 32.0, None, A.add, None, "P0", "L2")
-    diag(T.P1[:, 0:80], "P1", T.BH, "BH", [(T.X1, 0, L, "X1")])
-    halves = sorted([range(0, 4), range(4, 8)], key=lambda h: r in h)
-    for h in halves:
-        act(T.GV[:, CO * h[0]:CO * h[0] + 640], T.R1[:, 0:2560].indirect(T.L2[:, 10 * h[0]:10 * h[0] + 40]), F.Copy, "R1 L2", "GV%d" % h[0])
-    scan(T.INC[:, 1:65], T.NS[:], T.NS[:], A.add, A.max, "NS", "INC")
-    ts(T.EM[:, 0:64], T.NS[:], 0.0, None, A.is_equal, None, "NS", "EM")
-    ts(T.SG[:, 0:64], T.NS[:], 0.0, 0.0625, A.is_gt, A.mult, "NS", "NZ")
-    tt(T.DL[:], T.IS[:], T.INC[:, 1:65], A.subtract, "IS INC", "DL")
-    tt(T.SM[:, 0:64], T.EM[:, 1:65], T.U0[:], A.mult, "EM EMs U0", "O1")
-    tt(T.SG[:, 64:128], T.DL[:], T.SG[:, 0:64], A.mult, "DL NZ", "DN")
-    tt(T.SM[:, 64:128], T.SM[:, 0:64], T.INC[:, 1:65], A.max, "O1 INC", "OF")
-    scan(T.SG[:, 128:192], T.EM[:, 0:64], T.SG[:, 64:128], A.mult, A.add, "EM DN", "CA")
-    tt(T.SM[:, 0:64], T.SM[:, 64:128], T.MK[:], A.mult, "OF MK", "O1")
-    tt(T.DD[:, 0:63], T.SG[:, 129:192], T.SG[:, 128:191], A.subtract, "CA", "DD")
-    for k in range(4):
-        op("v", lambda k=k: V.tensor_reduce(T.SC[:, k:k + 1], T.SM[:, 16 * k:16 * k + 16], AxisListType.X, A.add), "O1", "SC%d" % k)
-    ts(T.L1[:], T.P1[:, 0:80], MID - 32.0, None, A.add, None, "P1", "L1")
-    cp(T.SO[:], T.SC[:, 0:4], "SC0 SC1 SC2 SC3", "SO")
-    for h in halves:
-        c0 = CO * h[0]
-        tt(T.S2V[:, c0:c0 + 640], T.R1[:, 0:2560].indirect(T.L1[:, 10 * h[0]:10 * h[0] + 40]), T.GV[:, c0:c0 + 640], A.subtract,
-           "R1 L1 GV%d" % h[0], "SV%d" % h[0])
-        ds = [k for k in h if k != r]
-        send(ds, [eng[4 * n:4 * n + 4] for n in range(len(ds))], lambda k: T.S2V[:, CO * k:CO * k + CO],
-             T.R2[:, CO * r:CO * r + CO], "aY", "SV%d" % h[0])
-    before("y", ["SV%d" % halves[1][0]], [])
-    g.sync.dma_start(T.R2[:, CO * r:CO * r + CO], T.S2V[:, CO * r:CO * r + CO]).then_inc(T.sem.aY, 16)
-    after(bump("aY", 4 * (N - 1) + 16), [], ["R2"])
-    cp(T.JW[:, 0:L + 72].indirect(T.SO[:]), T.DD[:], "SO DD DDs", "JW")
-    tt(T.CN[:], T.INC[:, 8:65:8], T.INC[:, 0:57:8], A.subtract, "INC INC0", "CN")
-    scan(T.JS[:], T.JW[:, 0:L], T.GV[:], A.add, A.min, "JW BIG", "JS") if False else None
-    op("v", lambda: V.tensor_tensor_scan(T.JS[:], T.JW[:, 0:L], T.K1[:], 0.0, A.add, A.min), "JW K1", "JS")
-    dma("s", T.cnt[:], T.CN[0::16, :], "CN", "cnt")
-    diag(T.P2[:, 0:80], "P2", T.BH, "BH", [(T.JS, 0, L, "JS")])
-    tt(T.SR[:], T.P2[:, 0:80], T.JN[:], A.add, "P2 JN", "SR")
-    ts(T.LV[:], T.SR[:], float(L), None, A.min, None, "SR", "LV")
-    ts(T.W1[:], T.SR[:], float(L), -7.5, A.min, A.add, "SR", "W1")
-    ts(T.SQ[:], T.SR[:], float(L), 96.0, A.min, A.mult, "SR", "SQ")
-    act(T.WA[:, 640:L], T.R2[:, 0:L + 8].indirect(T.LV[:, 40:80]), F.Copy, "R2 R2s LV NAk NAt", "YO1")
-    dma("s", T.y[:, 640:L], T.WA[:, 640:L], "YO1", "y1")
-    ts(T.WI[:], T.W1[:], 0.0625, None, A.mult, None, "W1", "WI")
-    ts(T.W2[:], T.WI[:], -1535.0, None, A.mult, None, "WI", "W2")
-    tt(T.W3[:], T.SQ[:], T.W2[:], A.add, "SQ W2", "W3")
-    cp(T.LW[:], T.W3[:], "W3", "LW")
-    cp(T.WA[:, 0:640], T.R2[:, 0:L + 8].indirect(T.LV[:, 0:40]), "R2 R2s LV NAk NAt", "YO0")
-    dma("y", T.y[:, 0:640], T.WA[:, 0:640], "YO0", "y0")
-    cp(T.WB[:, 0:640], T.EW[:, 0:1536].indirect(T.LW[:, 0:40]), "EW LW NBk NBt", "WH0")
-    act(T.WB[:, 640:L], T.EW[:, 0:1536].indirect(T.LW[:, 40:80]), F.Copy, "EW LW NBk NBt", "WH1")
+        out, win = T.WB[:, 640 * hf:640 * hf + 640], T.PC[:, 0:1536].indirect(T.LW[:, 40 * hf:40 * hf + 40])
+        if hf == 0:
+            cp(out, win, "PCa PCb LW NBk NBt", "WH0")
+        else:
+            act(out, win, F.Copy, "PCa PCb LW NBk NBt", "WH1")
     dma("y", T.who[:], T.WB[0::16, 0:L], "WH0 WH1", "who")
+    for k in range(4):
+        out, win = T.WA[:, CP * k:CP * k + CP], T.R2[:, 0:L + 8].indirect(T.LV[:, 20 * k:20 * k + 20])
+        if k % 2 == 0:
+            cp(out, win, "R2 R2o R2s LV NAk NAt", "YO%d" % k)
+        else:
+            act(out, win, F.Copy, "R2 R2o R2s LV NAk NAt", "YO%d" % k)
+        dma("ys"[k % 2], T.y[:, CP * k:CP * k + CP], out, "YO%d" % k, "y%d" % k)
     done = [s for (q, s), n in seen.items() if n == total[s]]
     for s in sorted(total):
         if s not in done:

@@ -10,25 +10,36 @@ SB = {
     "XD": (128, bf), "VB": (128, bf), "PC1": (8, i32), "XF": (144, f32), "COL": (8, f32), "CI": (8, i32),
     "BA": (128, bf), "BB": (128, bf), "BLK": (128, bf), "GT": (128, bf), "IK": (128, bf), "TRI": (128, bf), "IB": (128, bf),
     "IM": (7 * 128, f16), "BS": (144, bf), "BP": (144, bf), "BH": (144, f16), "BLH": (128, f16), "D4": (8, bf), "IDN": (128, bf),
-    "OWB": (128, bf), "K0": (128, f32), "KZ": (128, f32), "KT": (128, f32),
-    "O": (1024, bf), "S": (1024, bf), "X": (1024, f16), "HB": (128, f16), "D1": (128, u16),
-    "P": (TR, f32), "DI": (320, f32), "WA": (2560, f32), "WB": (2560, f32), "NA": (320, f32), "NB": (320, f32),
-    "KS": (160, f32), "KF": (160, f32), "TS": (160, u16), "KR": (160, u16), "S1": (2560, f32), "R1": (32 + 2560, f32), "PC": (2560, f32),
+    "OWB": (128, bf), "EL6": (128, i32), "K0": (128, f32), "KZ": (128, f32), "KT": (128, f32),
+    "O": (1024, bf), "S": (1024, bf), "X": (1024, f16), "HB": (128, f16), "Y2": (128, f32), "D1": (128, u16),
+    "P": (1024, f32), "DI": (320, f32), "WA": (2560, f32), "WB": (2560, f32), "NA": (320, f32), "NB": (320, f32),
+    "KS": (160, u16), "TS": (160, u16), "KR": (160, u16), "S1": (2560, f32), "R1": (32 + 2560, f32), "PC": (2560, f32),
     "TA": (TW, f32), "TB": (TW, f32), "FZ": (128, f32), "FW": (128, f32), "LC": (16, u16), "FE": (256, i32), "FF": (512, i32),
-    "E64": (256, i32), "FG": (512, i32), "LL": (512, u16), "G": (8192, f32), "NN": (512, f32),
+    "E64": (256, i32), "FG": (512, i32), "LL": (512, u16), "G": (8192, i32), "NN": (512, i32),
     "MN": (256, bf), "PR": (256, bf), "KC": (128, bf), "S2": (256, bf), "CW": (272, f32),
     "CS": (64, f32), "CL": (128, f32), "KP": (CO, bf), "CM": (2560, bf), "D32": (40, bf), "LB": (80, u16), "K1": (640, bf),
-    "C16": (80, f16), "AH": (80, f16), "PH": (80, f16), "C": (L, bf), "LP": (80, u16), "XN": (2560, f16), "LN": (160, u16),
+    "C16": (80, f16), "AH": (80, f16), "PH": (80, f16), "C": (L, bf), "LP": (80, u16), "XN": (L + 128, f16), "LO": (80, f32), "DD": (64, f32), "LN": (160, u16),
     "GV": (L, f32), "SV": (L, f32), "R2": (L + 8, f32), "ES": (80, f32), "EL": (96, f32),
     "PI": (8, f32), "PU": (8, u16), "IS": (64, f32), "EX": (64, f32), "NS": (64, f32), "INC": (72, f32), "DL": (72, f32),
-    "SJ": (128, f16), "SH": (8, i32), "SG": (16, f32), "XP": (128, f16), "LK": (512, f16), "RA": (320, f16), "RB": (320, f16),
+    "SH": (8, i32), "SG": (16, f32), "XP": (128, f16), "LK": (512, f16), "RA": (320, f16), "RB": (320, f16),
     "CB": (80, bf), "JN": (80, f16), "EO": (80, f16), "CN": (8, f32), "LV": (80, u16), "SF": (80, f16), "HF": (80, f16), "LW": (80, u16),
 }
 SCRATCH = {k: ("sbuf", [128, w], t) for k, (w, t) in SB.items()}
 SCRATCH.update({"P%d" % k: ("psum", [128, 512], f32) for k in range(8)})
 ND = 44
 SEMAPHORES = ["cv", "cs", "cp", "cg", "ls", "aK", "aV", "aC", "aE", "aY"] + ["d%d" % k for k in range(ND)]
-MULT = [1.0, 140.0, 2.0, -127.0, -64.0, 96.0, -1535.0]
+MULT = [160.0, 1.0, 2.0, -127.0, -64.0, 96.0, -1535.0]
+CUT = [64, 64, 64, 64]
+TURNS = 6
+HOP = 120
+LAG = 1800
+FLY = 2200
+MMN = 55
+GA = 1.1
+COST = {"WAk": 2600, "WBk": 2600, "TA": 480, "TB": 3200, "Z": 450, "X": 250, "HB": 120, "Y": 120, "D": 120, "KS": 300, "TS": 300, "NBt": 150,
+        "FE": 360, "FF": 240, "FG": 480, "XN": 420, "DD": 120, "CX": 820, "YO": 430, "WH": 820, "IS": 130, "EX": 130, "NS": 120, "DL": 120, "SJ": 120,
+        "CM": 80, "CW": 120, "BLK": 240, "GT": 240, "TRI": 240, "XP": 240, "KT": 120, "FW": 120, "EL": 120, "K": 120, "MN": 120, "DIt": 150}
+ORDER = "R0 C0 W0 R1 P0 C1 W1 S0 P1 A V0 S1 E D0 V1 D1 B"
 
 
 def rank_program(g, core, T, topo):
@@ -68,29 +79,82 @@ def rank_program(g, core, T, topo):
         total[s] = total.get(s, 0) + n
         return (s, total[s])
 
-    def op(q, fn, rd, wr):
-        rd, wr = rd.split(), wr.split()
-        before(q, rd, wr)
-        fn().then_inc(T.sem["c" + q], 1)
-        after(bump("c" + q, 1), rd, wr)
+    calls = []
 
-    def dma(q, out, in_, rd, wr, **kw):
-        rd, wr = rd.split(), wr.split()
-        before(q, rd, wr)
-        s = "d%d" % nd[0]
-        nd[0] += 1
-        Q[q].dma_start(out, in_, **kw).then_inc(T.sem[s], 16)
-        after(bump(s, 16), rd, wr)
+    def put(q, emit, rd, wr, busy, lag):
+        calls.append((q, emit, rd.split(), wr.split(), busy, lag))
 
-    def mm(bank, items, start=True):
-        before("p", [], [bank])
-        allr = []
-        for n, (out, lt, rh, rd) in enumerate(items):
-            before("p", rd.split(), [])
-            allr += rd.split()
-            ins = g.tensor.matmul(out, lt, rh, start and n == 0, n == len(items) - 1)
-        ins.then_inc(T.sem.cp, 1)
-        after(bump("cp", 1), allr, [bank])
+    def gap(rd, wr, lag):
+        put("", lambda rd, wr: None, rd, wr, 0, lag)
+
+    def op(q, fn, rd, wr, n=0):
+        def emit(rd, wr):
+            before(q, rd, wr)
+            fn().then_inc(T.sem["c" + q], 1)
+            after(bump("c" + q, 1), rd, wr)
+        put(q, emit, rd, wr, n or COST.get(wr.split()[0].rstrip("0123456789"), 70), 50)
+
+    def dma(q, out, in_, rd, wr, lag=LAG, **kw):
+        def emit(rd, wr):
+            before(q, rd, wr)
+            s = "d%d" % nd[0]
+            nd[0] += 1
+            Q[q].dma_start(out, in_, **kw).then_inc(T.sem[s], 16)
+            after(bump(s, 16), rd, wr)
+        put(q, emit, rd, wr, 300 if q == "g" else 60, lag)
+
+    def mm(bank, items, n=MMN):
+        def emit(rd, wr):
+            before("p", [], wr)
+            for k, (out, lt, rh, part) in enumerate(items):
+                before("p", part.split(), [])
+                ins = g.tensor.matmul(out, lt, rh, k == 0, k == len(items) - 1)
+            ins.then_inc(T.sem.cp, 1)
+            after(bump("cp", 1), rd, wr)
+        put("p", emit, " ".join(sorted(set(" ".join(it[3] for it in items).split()))), bank, n * len(items), 50)
+
+    def issue():
+        pre, post, wrote, read = [], [[] for c in calls], {}, {}
+        for n, (q, emit, rd, wr, busy, lag) in enumerate(calls):
+            d = set()
+            for k in rd:
+                d |= set(wrote.get(k, []))
+                if k[0] == "P" and k[1:].isdigit():
+                    d |= {m for m in read.get(k, []) if calls[m][0] != q}
+            for k in wr:
+                d |= set(wrote.get(k, []) + read.get(k, []))
+            pre.append(sorted(d - {n}))
+            for m in pre[n]:
+                post[m].append(n)
+            for k in rd:
+                read.setdefault(k, []).append(n)
+            for k in wr:
+                wrote[k], read[k] = [n], []
+
+        def place(order, back):
+            start, taken = {}, {}
+            for n in order:
+                q, busy, lag = calls[n][0], calls[n][4], calls[n][5]
+                if back:
+                    t = max([start[m] + calls[m][4] + HOP for m in post[n]] + [0]) + lag
+                else:
+                    t = max([start[m] + calls[m][4] + calls[m][5] + HOP for m in pre[n]] + [0])
+                for t0, t1 in sorted(taken.setdefault(q, [])):
+                    if t + busy > t0 and t < t1:
+                        t = t1
+                taken[q].append((t, t + busy))
+                start[n] = t
+            return start
+
+        start, best = place(range(len(calls)), False), None
+        for turn in range(TURNS):
+            late = place(sorted(start, key=lambda n: (-start[n] - calls[n][4] - calls[n][5], -n)), True)
+            start = place(sorted(late, key=lambda n: (-late[n] - calls[n][4], n)), False)
+            end = max(start[n] + calls[n][4] + calls[n][5] for n in start)
+            if best is None or end < best[0]:
+                best = (end, start)
+        for n in sorted(start, key=lambda n: (best[1][n], n)):
+            calls[n][1](calls[n][2], calls[n][3])
 
     V, S = g.vector, g.scalar
 
@@ -100,11 +164,11 @@ def rank_program(g, core, T, topo):
         else:
             op("v", lambda: V.tensor_scalar(out, in0, s1, s2, o0, o1), rd, wr)
 
-    def tt(out, a, b, o, rd, wr):
-        op("v", lambda: V.tensor_tensor(out, a, b, o), rd, wr)
+    def tt(out, a, b, o, rd, wr, n=0):
+        op("v", lambda: V.tensor_tensor(out, a, b, o), rd, wr, n)
 
-    def cp(out, a, rd, wr):
-        op("v", lambda: V.tensor_copy(out, a), rd, wr)
+    def cp(out, a, rd, wr, n=0):
+        op("v", lambda: V.tensor_copy(out, a), rd, wr, n)
 
     def ms(out, c, wr):
         op("v", lambda: V.memset(out, c), "", wr)
@@ -112,15 +176,24 @@ def rank_program(g, core, T, topo):
     def scan(out, d0, d1, o0, o1, rd, wr):
         op("v", lambda: V.tensor_tensor_scan(out, d0, d1, 0.0, o0, o1), rd, wr)
 
-    def act(out, a, fn, rd, wr, **kw):
-        op("s", lambda: S.activation(out, a, fn, **kw), rd, wr)
+    def act(out, a, fn, rd, wr, n=0, **kw):
+        op("s", lambda: S.activation(out, a, fn, **kw), rd, wr, n)
 
     def lin(out, a, scale, bias, rd, wr):
         act(out, a, F.Identity, rd, wr, scale=scale, bias=bias)
 
-    def iota(name, out, pat, base, cm, wr=None):
+    def move(q, out, a, rd, wr, n=0):
+        if q == "v":
+            cp(out, a, rd, wr, n)
+        else:
+            act(out, a, F.Copy, rd, wr, n)
+
+    def iota(name, out, pat, base, cm, wr=None, rd=""):
         kw = {} if SB[name][1] == i32 else {"allow_small_or_imprecise_dtypes": True}
-        op("g", lambda: g.iota(out, pat, base, cm, **kw), "", wr or name)
+        n = 1
+        for step, cnt in pat:
+            n *= cnt
+        op("g", lambda: g.iota(out, pat, base, cm, **kw), rd, wr or name, 130 + 2 * n)
 
     def im(c):
         k = MULT.index(c)
@@ -141,18 +214,31 @@ def rank_program(g, core, T, topo):
     pairs.update({k: od[2 * n:2 * n + 2] for n, k in enumerate(near)})
     halves = sorted([0, 1], key=lambda h: h == r // 4)
 
-    def send(dests, masks, src, dst, sem, rd):
-        before("g", rd.split(), [])
-        trs = []
-        for k, m in zip(dests, masks):
-            rid, pid = topo.addr(cores[k])[:2]
-            trs.append(RemoteDMATransfer(dst_ids=[DstId(rid=rid, pnc=pid)], dma_engine_mask=sum(1 << e for e in m),
-                                         remote_sem=T.sem[sem], src=src(k), dst=dst))
-        g.remote_dma_fused(trs, local_sem=T.sem.ls)
-        bump("ls", sum(len(m) for m in masks))
+    def send(dests, masks, src, dst, sem, rd, tag, busy=300):
+        def emit(rd, wr):
+            before("g", rd, [])
+            trs = []
+            for k, m in zip(dests, masks):
+                rid, pid = topo.addr(cores[k])[:2]
+                trs.append(RemoteDMATransfer(dst_ids=[DstId(rid=rid, pnc=pid)], dma_engine_mask=sum(1 << e for e in m),
+                                             remote_sem=T.sem[sem], src=src(k), dst=dst(k)))
+            g.remote_dma_fused(trs, local_sem=T.sem.ls)
+            bump("ls", sum(len(m) for m in masks))
+        put("g", emit, rd, tag, busy, 0)
 
-    def lands(sem, n, key):
-        after(bump(sem, n * (N - 1)), [], [key])
+    def lands(sem, n, tags, key, lag):
+        put("", lambda rd, wr: after(bump(sem, n), [], wr), tags, key, 0, lag)
+
+    def exchange(src, dst, sem, rd, key, busy=300):
+        def emit(rd, wr):
+            before("y", rd, [])
+            g.sync.dma_start(dst(r), src(r)).then_inc(T.sem[sem], 16)
+        send(far + near, [pairs[k] for k in far + near], src, dst, sem, rd, sem + "s", busy)
+        put("y", emit, rd, sem + "o", 60, 0)
+        lands(sem, 2 * (N - 1) + 16, sem + "s " + sem + "o", key, FLY)
+
+    def pos(k):
+        return (r - k - 1) % N
 
     def diag(out, lhs, lk, buf, c0, n, key):
         return [(out, lhs[:, 15 - i:143 - i], buf[:, c0 + i:c0 + n:16], lk + " " + key) for i in range(16)]
@@ -161,86 +247,89 @@ def rank_program(g, core, T, topo):
         cuts = sorted({c0, c1} | ({r, r + 1} if c0 <= r < c1 else set()))
         return list(zip(cuts[:-1], cuts[1:]))
 
+    def zero(ks):
+        for k in ks:
+            act(T.TA[:, 64 + 512 * k:576 + 512 * k], T.Z[:], F.Copy, "Z0 Z", "TA%d" % k)
+
     for h in range(2):
         dma("ys"[h], T.EA[:, 64 * h:64 * h + 64], T.ent[:, 1024 * h:1024 * h + 1024], "", "EA%d" % h)
     for h in range(2):
-        dma("y", T.EB[:, 64 * h:64 * h + 64], T.ent[h::2, :], "", "EB%d" % h)
-        dma("s", T.EB[:, 128 + 64 * h:192 + 64 * h], T.att[h::2, :], "", "AB%d" % h)
-    dma("y", T.VAL[:, 32:], T.val[:], "", "VAL")
+        dma("y", T.EB[:, 64 * h:64 * h + 64], T.ent[h::2, :], "", "EB%d" % h, lag=LAG + 500)
+        dma("s", T.EB[:, 128 + 64 * h:192 + 64 * h], T.att[h::2, :], "", "AB%d" % h, lag=LAG + 500)
     iota("VB", T.VB[:], [[16, 8], [0, 16]], 0, -1)
     iota("XD", T.XD[:], [[1, 128]], 0, -1)
-    iota("P", T.P[:, 0:1024], [[1, 32], [1024, 2], [64, 16]], 32, 0, "Pa")
-    iota("DI", T.DI[:, 160:320], [[4096, 8], [16, 20]], 4160 + CP * (r % 4), 1, "DIk")
+    iota("DI", T.DI[:, 160:320], [[0, 8], [16, 20]], 4160 + CP * (r % 4), 1, "DIk")
+    iota("P", T.P[:], [[1, 32], [1024, 2], [64, 16]], 32, 0, "Pa")
     ms(T.Z[:, 0:64], 0.0, "Z0")
-    act(T.TA[:, 64:128], T.Z[:, 0:64], F.Silu, "Z0", "TA8")
-    ms(T.Z[:, 64:512], 0.0, "Z")
+    act(T.TA[:, 64:128], T.Z[:, 0:64], F.Silu, "Z0", "TA8 SL", 1400)
     ms(T.DI[:, 0:160], float(TR + 31), "DIt")
     for nm in ("WA", "WB"):
         dma("y", T[nm][0::16, :], T.DI[:, 0:160], "DIt", nm + "t")
     ts(T.BA[:], T.VB[:], -16.0, None, A.is_gt, None, "VB", "BA")
     ts(T.BB[:], T.VB[:], 0.0, None, A.is_gt, None, "VB", "BB")
+    tt(T.BLK[:], T.BA[:], T.BB[:], A.subtract, "BA BB", "BLK")
     ts(T.GT[:], T.XD[:], 0.0, -1.0, A.is_lt, A.mult, "XD", "GT")
     ts(T.IK[:], T.XD[:], 0.0, 1024.0, A.is_equal, A.mult, "XD", "IK")
-    tt(T.BLK[:], T.BA[:], T.BB[:], A.subtract, "BA BB", "BLK")
     tt(T.GT[:], T.GT[:], T.BA[:], A.mult, "GT BA", "GT")
-    ts(im(1.0), T.XD[:], 0.0, None, A.is_equal, None, "XD", "I1")
+    ts(T.IB[:], T.XD[:], 0.0, 20.0, A.is_equal, A.mult, "XD", "IB")
     tt(T.TRI[:], T.GT[:], T.IK[:], A.add, "GT IK", "TRI")
-    for nm in ("WA", "WB"):
-        dma("y", T[nm][1::16, :], T.DI[:, 160:320], "DIk", nm + "k")
+    dma("y", T.WA[1::16, :], T.DI[:, 160:320], "DIk", "WAk")
+    dma("y", T.WB[9::16, :], T.DI[:, 160:320], "DIk", "WBk")
 
     for h in range(2):
-        ts(T.OWB[:, h::2], T.EA[:, 64 * h:64 * h + 64], 1.0 / 64, 129.0 - 63.0 / 128, A.mult, A.add, "EA%d" % h, "OW%d" % h)
-    lin(T.K0[:], T.EB[:, 0:128], 64.0, 64.0, "EB0 EB1", "K0")
-    for hf in range(2):
-        for q in range(4 * hf, 4 * hf + 4):
+        lin(T.OWB[:, h::2], T.EA[:, 64 * h:64 * h + 64], 1.0 / 64, 129.0 - 63.0 / 128, "EA%d" % h, "OW%d" % h)
+    place = T.P4[:, 0:128]
+
+    def count(n):
+        ks, c = range(2 * n, 2 * n + 2), slice(256 * n, 256 * n + 256)
+        for q in ks:
             ts(T.O[:, 128 * q:128 * q + 128], T.OWB[:], 129.0 + q, None, A.is_equal, None, "OW0 OW1", "O%d" % q)
-        for q in range(4 * hf, 4 * hf + 4):
+        for q in ks:
             o = T.O[:, 128 * q:128 * q + 128]
             scan(T.S[:, 128 * q:128 * q + 128], o, o, A.add, A.max, "O%d" % q, "S%d" % q)
-        ks, out = range(4 * hf, 4 * hf + 4), T["P%d" % hf][:]
-        mm("P%d" % hf, [(out, T.TRI[:], T.O[:, 512 * hf:512 * hf + 512], "TRI " + keys("O#", ks)),
-                        (out, T.BLK[:], T.S[:, 512 * hf:512 * hf + 512], "BLK " + keys("S#", ks))])
-    lin(T.P[:, 1024:2048], T.P[:, 0:1024], 1.0, 32.0, "Pa", "Pb")
+        out = T["P%d" % n][:, 0:256]
+        mm("P%d" % n, [(out, T.TRI[:], T.O[:, c], "TRI " + keys("O#", ks)), (out, T.BLK[:], T.S[:, c], "BLK " + keys("S#", ks))], 190)
+
+    count(0)
+    ts(T.EL6[:], T.EB[:, 0:128], 63, None, A.bitwise_and, None, "EB0 EB1", "EL6")
+    count(1)
+    lin(T.K0[:], T.EL6[:], 64.0, 64.0, "EL6", "K0")
+    for b in range(4):
+        tt(T.KZ[:, 32 * b:32 * b + 32], T.K0[:, b::4], T.EB[:, 128 + b::4], A.add, "K0 AB0 AB1", "KZ%d" % b)
+    count(2)
+    op("v", lambda: V.transpose(T.KT[:], T.KZ[:]), keys("KZ#", 4), "KT")
+    count(3)
+    ts(im(160.0), T.XD[:], 0.0, 160.0, A.is_equal, A.mult, "XD", "I160")
+    ms(T.Z[:, 64:512], 0.0, "Z")
+    dma("y", T.P[1::8, :], T.KT[:], "KT Pa", "Pk")
+    gap("KT Pa", "Pg", 100)
+    dma("y", T.VAL[:, 32:], T.val[:], "Pg", "VAL", lag=3000)
     for h in range(2):
-        for b in range(2):
-            c = 64 * h + b
-            tt(T.KZ[:, 64 * h + 32 * b:64 * h + 32 * b + 32], T.K0[:, c:64 * h + 64:2], T.EB[:, 128 + c:192 + 64 * h:2], A.add, "K0 AB%d" % h, "KZ%d%d" % (h, b))
-    op("v", lambda: V.transpose(T.KT[:], T.KZ[:]), keys("KZ##", 2, 2), "KT")
-    for h in range(2):
-        dma("ys"[h], T.P[16 * h + 1::32, :], T.KT[:, 64 * h:64 * h + 64], "KT Pa Pb", "Pk%d" % h)
-    for h in range(2):
-        dma("y", T.FX[:, 64 * h:64 * h + 64], T.form[h::2, :], "", "FX%d" % h)
+        dma("y", T.FX[:, 64 * h:64 * h + 64], T.form[h::2, :], "Pg", "FX%d" % h)
     for ah in range(4):
-        dma("y", T.CL4[ah::4, :], T.cls[:], "", "CL4%d" % ah)
-    act(T.X[:, 0:512], T.P0[:], F.Relu, "P0", "X0", bias=-1024.0)
-    ts(T.X[:, 512:1024], T.P1[:], -1024.0, 0.0, A.add, A.max, "P1", "X1")
-    ts(im(140.0), T.XD[:], 0.0, 140.0, A.is_equal, A.mult, "XD", "I140")
-    ts(T.IB[:], T.XD[:], 0.0, 20.0, A.is_equal, A.mult, "XD", "IB")
-    mm("P2", [(T.P2[:, 0:128], im(1.0), T.X[:, 128 * q:128 * q + 128], "I1 X%d" % (q // 4)) for q in range(8)])
+        dma("y", T.CL4[ah::4, :], T.cls[:], "Pg", "CL4%d" % ah)
+    for n in range(4):
+        act(T.X[:, 256 * n:256 * n + 256], T["P%d" % n][:, 0:256], F.Relu, "P%d" % n, "X%d" % n, bias=-1024.0)
+    mm("P4", [(place, T.IB[:], T.OWB[:], "IB OW0 OW1")] + [(place, im(160.0), T.X[:, 128 * q:128 * q + 128], "I160 X%d" % (q // 2)) for q in range(8)], 30)
     act(T.TA[:, 128:576], T.Z[:, 64:512], F.Copy, "Z", "TA0")
-    for k in range(1, 3):
-        act(T.TA[:, 64 + 512 * k:576 + 512 * k], T.Z[:], F.Copy, "Z0 Z", "TA%d" % k)
-    ts(T.HB[:], T.P2[:, 0:128], 20489.5, 0.05, A.add, A.mult, "P2", "HB")
-    out = T.P3[:, 0:128]
-    mm("P3", [(out, T.IB[:], T.OWB[:], "IB OW0 OW1")] + [(out, im(1.0), T.X[:, 128 * q:128 * q + 128], "X%d" % (q // 4)) for q in range(8)] +
-       [(out, im(140.0), T.HB[:], "I140 HB")])
-    ts(T.D1[:], out, -(1.0 + 140 * 1025 + 20 * 129), None, A.add, None, "P3", "D1")
-    cp(T.WA[:, 0:2560].indirect(T.D1[:, 0:64]), T.P[:, 0:1024], "D1 Pa Pk0 Pk1", "WAk WAt")
-    act(T.WB[:, 0:2560].indirect(T.D1[:, 64:128]), T.P[:, 1024:2048], F.Silu, "D1 Pb Pk0 Pk1", "WBk WBt")
+    ts(T.HB[:], place, 1025.0 * 2560 - 2740 - 1270, 1.0 / 2560, A.add, A.mult, "P4", "HB")
+    ts(T.Y2[:], T.HB[:], -2559.0, 2559.0 * 1025 - 2740, A.mult, A.add, "HB", "Y2")
+    tt(T.D1[:], place, T.Y2[:], A.add, "P4 Y2", "D1")
+    cp(T.WA[:, 0:2560].indirect(T.D1[:, 0:64]), T.P[:], "D1 Pa Pk", "WAk WAt")
+    act(T.WB[:, 0:2560].indirect(T.D1[:, 64:128]), T.P[:], F.Silu, "D1 Pa Pk SL", "WBk WBt")
     dma("y", T.NA[:, 160:320], T.WA[1::16, :], "WAk", "NAk")
-    dma("s", T.NB[:, 160:320], T.WB[1::16, :], "WBk", "NBk")
+    dma("s", T.NB[:, 160:320], T.WB[9::16, :], "WBk", "NBk")
     dma("y", T.NA[:, 0:160], T.WA[0::16, :], "WAt", "NAt")
     dma("s", T.NB[:, 0:160], T.WB[0::16, :], "WBt", "NBt")
-    for k in range(3, 7):
-        act(T.TA[:, 64 + 512 * k:576 + 512 * k], T.Z[:], F.Copy, "Z0 Z", "TA%d" % k)
+    zero(range(1, 5))
     iota("PC1", T.PC1[:, 0:1], [[1, 1]], 0, 1)
     iota("XF", T.XF[:], [[1, 144]], 0, 0)
-    dma("g", T.TB[0::16, 64:4160], T.Z[:, 64:320], "Z", "TB")
     iota("PC", T.PC[:, 0:L], [[1, L]], 32, 0, "PCa")
+    dma("g", T.TB[0::16, 64:4160], T.Z[:, 64:320], "Z Pg", "TB")
+    gap("TB", "PCb", 0)
     iota("CL", T.CL[:], [[CO, 8], [0, 16]], 0, 0, "CLi")
     iota("E64", T.E64[:], [[64, 16], [1024, 4], [0, 4]], 0, 0)
-    iota("KC", T.KC[:], [[0, 4], [1, 32]], 0, 0)
-    iota("KP", T.KP[:], [[1, 16], [16, 10]], 0, 0)
+    iota("PC", T.PC[:, L:2 * L], [[1, L]], 32 + L, 0, "PCb")
     for k, m in ((1, 112), (2, 15), (3, 3), (4, 7)):
         ts(T.CI[:, k:k + 1], T.PC1[:, 0:1], m, None, A.bitwise_and, None, "PC1", "CI%d" % k)
     for h in range(2):
@@ -255,56 +344,53 @@ def rank_program(g, core, T, topo):
     ms(T.EL[:, 80:96], -1.0, "ELs")
     ms(T.R2[:, L:L + 8], 0.0, "R2s")
     tt(T.KS[:], T.NA[:, 160:320], T.NB[:, 160:320], A.min, "NAk NBk", "KS")
-    send(far + near, [pairs[k] for k in far + near], lambda k: T.KS[:, 20 * k:20 * k + 20], T.KF[:, 20 * r:20 * r + 20], "aK", "KS CLi ELs R2s R1s")
-    lands("aK", 2, "KF")
+    send(far + near, [pairs[k] for k in far + near], lambda k: T.KS[:, 20 * k:20 * k + 20], lambda k: T.KR[:, 20 * pos(k):20 * pos(k) + 20], "aK",
+         "KS CLi ELs R2s R1s", "aKs", 2000)
+    lands("aK", 2 * (N - 1), "aKs", "KR", FLY)
+    lin(T.NB[:, 0:160], T.NB[:, 0:160], 1.0, 32.0, "NBt", "NBt")
     tt(T.TS[:], T.NA[:, 0:160], T.NB[:, 0:160], A.min, "NAt NBt", "TS")
-    act(T.KF[:, 20 * r:20 * r + 20], T.KS[:, 20 * r:20 * r + 20], F.Copy, "KS", "KFo")
     for hf in range(2):
         for c0, c1 in pieces(4 * hf, 4 * hf + 4):
-            out = T.R1[:, 32 + CP * r:32 + CP * r + CP] if c0 == r else T.S1[:, CP * c0:CP * c1]
-            win, key = T.VAL[:, 0:32 + TR].indirect(T.TS[:, 20 * c0:20 * c1]), "R1o" if c0 == r else "S1%d" % c0
-            if hf == 0:
-                cp(out, win, "VAL VALs TS", key)
-            else:
-                act(out, win, F.Copy, "VAL VALs TS", key)
-    send(far + near, [pairs[k] for k in far + near], lambda k: T.S1[:, CP * k:CP * k + CP], T.R1[:, 32 + CP * r:32 + CP * r + CP], "aV",
-         keys("S1#", 8))
-    lands("aV", 2, "R1")
-    lin(T.PC[:, L:2 * L], T.PC[:, 0:L], 1.0, float(L), "PCa", "PCb")
-    for k in range(7, 8):
-        act(T.TA[:, 64 + 512 * k:576 + 512 * k], T.Z[:], F.Copy, "Z0 Z", "TA%d" % k)
+            out = T.R1[:, 32 + CP * (N - 1):] if c0 == r else T.S1[:, CP * c0:CP * c1]
+            move("vs"[hf], out, T.VAL[:, 0:32 + TR].indirect(T.TS[:, 20 * c0:20 * c1]), "VAL VALs TS", "R1o" if c0 == r else "S1%d" % c0,
+                 GA * CP * (c1 - c0))
+    send(far + near, [pairs[k] for k in far + near], lambda k: T.S1[:, CP * k:CP * k + CP],
+         lambda k: T.R1[:, 32 + CP * pos(k):32 + CP * pos(k) + CP], "aV", keys("S1#", 8) + " aKs", "aVs")
+    lands("aV", 2 * (N - 1), "aVs", "R1", 6000)
+    gap("aVs", "aVg", 4500)
+    zero(range(5, 8))
     TAK = keys("TA#", 9)
     cp(T.FE[:], T.FW[:, 0:128].indirect(T.LC[:]), "FW LC", "FE")
     ts(T.FF[:, 0:256], T.FE[:], 63, None, A.bitwise_and, None, "FE", "FF0")
     ts(T.FF[:, 256:512], T.FE[:], 6, None, A.arith_shift_right, None, "FE", "FF1")
     for w in range(2):
         tt(T.FG[:, 256 * w:256 * w + 256], T.FF[:, 256 * w:256 * w + 256], T.E64[:], A.add, "FF%d E64" % w, "FG%d" % w)
-    iota("K1", T.K1[:], [[0, 4], [1, CO]], 0, 0)
-    iota("D32", T.D32[:], [[32, 4], [0, 10]], 0, 0)
-    iota("PI", T.PI[:, 0:4], [[2, 4]], 0, 0)
-    iota("CB", T.CB[:], [[16, 80]], 0, 0)
+    iota("KC", T.KC[:], [[0, 4], [1, 32]], 0, 0, rd="aVs")
+    iota("KP", T.KP[:], [[1, 16], [16, 10]], 0, 0, rd="aVs")
+    iota("K1", T.K1[:], [[0, 4], [1, CO]], 0, 0, rd="aVs")
+    iota("D32", T.D32[:], [[32, 4], [0, 10]], 0, 0, rd="aVs")
+    iota("PI", T.PI[:, 0:4], [[2, 4]], 0, 0, rd="aVs")
+    iota("CB", T.CB[:], [[16, 80]], 0, 0, rd="aVs")
 
-    ts(T.KR[:, 0:80], T.KF[:, 0:80], -4096.0 * r, None, A.add, None, "KF KFo", "KR0")
-    lin(T.KR[:, 80:160], T.KF[:, 80:160], 1.0, -4096.0 * r, "KF KFo", "KR1")
-    cp(T.TA[:, 0:TW].indirect(T.KR[:, 0:80]), T.PC[:, 0:L], "KR0 PCa", TAK)
-    act(T.TB[:, 0:TW].indirect(T.KR[:, 80:160]), T.PC[:, L:2 * L], F.Silu, "KR1 PCb", "TB")
-    dma("g", T.TA[0::16, 64:4160], T.TB[0::16, 64:4160], "TB " + TAK, TAK, accum_op=A.add, max_dma_last_dim=2048)
+    cp(T.TA[:, 0:TW].indirect(T.KS[:, 20 * r:20 * r + 20]), T.PC[:, 2240:2560], "KS PCb", TAK, 800)
+    cp(T.TA[:, 0:TW].indirect(T.KR[:, 0:70]), T.PC[:, 0:1120], "KR PCa", TAK, 2800)
+    act(T.TB[:, 0:TW].indirect(T.KR[:, 70:140]), T.PC[:, 1120:2240], F.Silu, "KR PCa PCb", "TB", 2800)
+    dma("g", T.TA[0::16, 64:4160], T.TB[0::16, 64:4160], "TB aVg " + TAK, TAK, lag=2000, accum_op=A.add, max_dma_last_dim=2048)
     for j, h in enumerate(halves):
         for w in range(2):
             for b in range(2):
                 c0 = 128 * (2 * j + w)
-                if w == 0:
-                    cp(T.LL[:, c0 + b:c0 + 128:2], T.FG[:, 2 * h + b:256:4], "FG0", "LL%d%d%d" % (j, w, b))
-                else:
-                    act(T.LL[:, c0 + b:c0 + 128:2], T.FG[:, 256 + 2 * h + b:512:4], F.Copy, "FG1", "LL%d%d%d" % (j, w, b))
+                move("vs"[w], T.LL[:, c0 + b:c0 + 128:2], T.FG[:, 256 * w + 2 * h + b:256 * w + 256:4], "FG%d" % w, "LL%d%d%d" % (j, w, b))
     ts(T.BS[:], T.XF[:], T.COL[:, 1:2], 15.0, A.subtract, A.is_equal, "XF C1", "BS")
     ts(T.COL[:, 6:7], T.COL[:, 2:3], 0.0, None, A.is_equal, None, "C1", "C6")
     ts(T.IDN[:], T.XD[:], 0.0, None, A.is_equal, None, "XD", "IDN")
     tt(T.D4[:, 0:4], T.BLK[:, 0::32], T.BLK[:, 16::32], A.add, "BLK", "D4")
-    for c in MULT[2:]:
+    for c in MULT[1:]:
         ts(im(c), T.XD[:], 0.0, c, A.is_equal, A.mult, "XD", "I%d" % c)
     ts(T.BP[:], T.BS[:], 128.0, None, A.mult, None, "BS", "BP")
-    ts(T.BH[:], T.BS[:], T.COL[:, 6:7], None, A.mult, None, "BS C6", "BH")
+    ts(T.COL[:, 7:8], T.COL[:, 2:3], 1.0, 4096.0, A.is_equal, A.mult, "C1", "C7")
+    tt(T.COL[:, 0:1], T.COL[:, 6:7], T.COL[:, 7:8], A.add, "C6 C7", "C0")
+    ts(T.BH[:], T.BS[:], T.COL[:, 0:1], None, A.mult, None, "BS C0", "BH")
     for j in range(2):
         ms(T.CW[:, 136 * j + 128:136 * j + 136], 0.0, "CWs%d" % j)
     ms(T.INC[:, 0:1], 0.0, "INC0")
@@ -318,46 +404,36 @@ def rank_program(g, core, T, topo):
     ts(T.JN[:], T.CB[:], T.COL[:, 2:3], None, A.add, None, "CB C1", "JN")
     ts(T.PU[:, 0:4], T.PI[:, 0:4], T.COL[:, 5:6], 8.0, A.add, A.add, "PI C5", "PU0")
     ts(T.PU[:, 4:8], T.PI[:, 0:4], T.COL[:, 5:6], 7.0, A.add, A.add, "PI C5", "PU1")
-
-    def look(q, j, w, c0, c1, last):
-        b = 2 * j + w
-        out, win = T.G[:, 2048 * b + 16 * c0:2048 * b + 16 * c1], T.TA[:, 64:4160].indirect(T.LL[:, 128 * b + c0:128 * b + c1])
-        rd, wr = TAK + " " + keys("LL%d%d#" % (j, w), 2), "G%d%s" % (b, q)
-        if q == "v":
-            cp(out, win, rd, wr)
-        else:
-            act(out, win, F.Copy, rd, wr)
-        if last:
-            dma("y", T.NN[:, 128 * b:128 * b + 128], T.G[0::16, 2048 * b:2048 * b + 2048], "G%dv G%ds" % (b, b), "N%d" % b)
-
-    look("v", 0, 0, 0, 128, True)
-    look("s", 0, 1, 0, 128, True)
-    look("v", 1, 0, 0, 96, False)
-    look("s", 1, 1, 0, 128, True)
-    look("s", 1, 0, 96, 128, True)
+    for b in range(4):
+        for q, c0, c1 in (("v", 0, CUT[b]), ("s", CUT[b], 128)):
+            move(q, T.G[:, 2048 * b + 16 * c0:2048 * b + 16 * c1], T.TA[:, 64:4160].indirect(T.LL[:, 128 * b + c0:128 * b + c1]),
+                 TAK + " " + keys("LL%d%d#" % (b // 2, b % 2), 2), "G%d%s" % (b, q), GA * 16 * (c1 - c0))
+        dma("y", T.NN[:, 128 * b:128 * b + 128], T.G[0::16, 2048 * b:2048 * b + 2048], "G%dv G%ds" % (b, b), "N%d" % b)
+        if b % 2:
+            dma("y", T.G[1::16, 2048 * (b - 1):2048 * b], T.G[0::16, 2048 * b:2048 * b + 2048], keys("G#v", [b - 1, b]) + " " + keys("G#s", [b - 1, b]), "GG%d" % b)
 
     def bank(j, k):
         return "P%d" % (4 * j + k), T["P%d" % (4 * j + k)]
 
     def ranks(j):
         c0, h = 128 * j, halves[j]
+        ts(T.MN[:, c0:c0 + 128], T.NN[:, 2 * c0:2 * c0 + 128], 1.0, None, A.is_gt, None, "N%d" % (2 * j), "MN%d" % j)
         for u in range(4):
-            tt(T.MN[:, c0 + u:c0 + 128:4], T.NN[:, 2 * c0 + 32 * u:2 * c0 + 32 * u + 32], T.NN[:, 2 * c0 + 128 + 32 * u:2 * c0 + 160 + 32 * u], A.min,
-               "N%d N%d" % (2 * j, 2 * j + 1), "MN%d%d" % (j, u))
-        pr, s2 = T.PR[:, c0:c0 + 128], T.S2[:, c0:c0 + 128]
-        ts(pr, T.MN[:, c0:c0 + 128], 1.0, None, A.is_gt, None, keys("MN%d#" % j, 4), "PR%d" % j)
-        scan(s2, T.KC[:], pr, A.min, A.add, "KC PR%d" % j, "S2%d" % j)
+            tt(T.PR[:, c0 + u:c0 + 128:4], T.MN[:, c0 + 32 * u:c0 + 32 * u + 32], T.NN[:, 2 * c0 + 128 + 32 * u:2 * c0 + 160 + 32 * u], A.min,
+               "MN%d N%d" % (j, 2 * j + 1), "PR%d%d" % (j, u))
+        pr, s2, prk = T.PR[:, c0:c0 + 128], T.S2[:, c0:c0 + 128], keys("PR%d#" % j, 4)
+        scan(s2, T.KC[:], pr, A.min, A.add, "KC " + prk, "S2%d" % j)
         (n0, b0), (n1, b1) = bank(j, 0), bank(j, 1)
         mm(n0, [(b0[:, 0:8], s2, T.BLK[:, 0::16], "BLK S2%d" % j)])
-        mm(n1, [(b1[:, 0:128], T.GT[:], pr, "GT PR%d" % j), (b1[:, 0:128], T.BLK[:], s2, "BLK S2%d" % j)])
+        mm(n1, [(b1[:, 0:128], T.GT[:], pr, "GT " + prk), (b1[:, 0:128], T.BLK[:], s2, "BLK S2%d" % j)], 95)
         mm(n1, [(b1[:, 128:160], T.BLK[:], T.S2[:, c0 + 3:c0 + 128:4], "BLK S2%d" % j)])
         act(T.CW[:, 136 * j:136 * j + 128], b1[:, 0:128], F.Copy, n1, "CW%d" % j)
         lin(T.CS[:, 32 * h:32 * h + 32], b1[:, 128:160], 1.0, float(CO * r), n1, "CS%d" % j)
         ds = [k for k in range(4 * h, 4 * h + 4) if k != r]
-        send(ds, [pairs[k] for k in ds], lambda k: T.CS[:, 8 * k:8 * k + 8], T.CL[:, 16 * r + 8:16 * r + 16], "aC", "CS%d" % j)
+        send(ds, [pairs[k] for k in ds], lambda k: T.CS[:, 8 * k:8 * k + 8], lambda k: T.CL[:, 16 * r + 8:16 * r + 16], "aC", "CS%d" % j, "aC%d" % j)
         if j == 1:
             act(T.CL[:, 16 * r + 8:16 * r + 16], T.CS[:, 8 * r:8 * r + 8], F.Copy, "CS1 CLi", "CLo")
-            lands("aC", 2, "CL")
+            lands("aC", 2 * (N - 1), "aC0 aC1", "CL", FLY)
 
     def columns(j):
         (n0, b0), (n2, b2) = bank(j, 0), bank(j, 2)
@@ -366,30 +442,29 @@ def rank_program(g, core, T, topo):
             ts(T.CM[:, c:c + CO], T.KP[:], b0[:, gg:gg + 1], None, A.is_ge, None, "KP " + n0, "CM%d%d" % (j, gg))
         mm(n2, [(b2[:, 0:40], T.IDN[:], T.D32[:], "IDN D32")] +
            [(b2[:, kh:40:10], T.CM[:, L * j + kh:L * j + L:10], T.D4[:, 0:4], "D4 " + keys("CM%d#" % j, 8)) for kh in range(10)])
-        c = slice(40 * j, 40 * j + 40)
+
+    def rows(j):
+        (n2, b2), (n3, b3), c = bank(j, 2), bank(j, 3), slice(40 * j, 40 * j + 40)
         cp(T.LB[:, c], b2[:, 0:40], n2, "LB%d" % j)
         lin(T.C16[:, c], b2[:, 0:40], 16.0, 0.0, n2, "C16%d" % j)
         lin(T.AH[:, c], b2[:, 0:40], 0.25, 1025.0 - 0.375, n2, "AH%d" % j)
-
-    def rows(j):
-        (n1, b1), (n3, b3), c = bank(j, 1), bank(j, 3), slice(40 * j, 40 * j + 40)
         tt(T.C[:, 640 * j:640 * j + 640], T.CW[:, 136 * j:136 * j + 136].indirect(T.LB[:, c]), T.K1[:], A.is_le,
-           "CW%d CWs%d LB%d K1" % (j, j, j), "C%d" % (10 + j))
+           "CW%d CWs%d LB%d K1" % (j, j, j), "CX%d" % j)
         out = b3[:, 0:40]
-        mm(n3, [(out, im(2.0), T.C16[:, c], "I2 C16%d" % j), (out, im(-127.0), T.AH[:, c], "I-127 AH%d" % j)] +
-           diag(out, T.BP, "BP", T.C, 640 * j, 640, "C%d" % (10 + j)))
+        mm(n3, diag(out, T.BP, "BP", T.C, 640 * j, 640, "CX%d" % j) +
+           [(out, im(2.0), T.C16[:, c], "I2 C16%d" % j), (out, im(-127.0), T.AH[:, c], "I-127 AH%d" % j)])
 
     def places(j):
-        (n0, b0), (n1, b1), (n3, b3), c = bank(j, 0), bank(j, 1), bank(j, 3), slice(40 * j, 40 * j + 40)
+        (n1, b1), (n3, b3), c = bank(j, 1), bank(j, 3), slice(40 * j, 40 * j + 40)
         ts(T.LP[:, c], b3[:, 0:40], 127.0 * 1025, 2047.0, A.add, A.min, n3, "LP%d" % j)
         lin(T.PH[:, c], b3[:, 0:40], 1.0 / 128, 127.0 * 1025 / 128 + 1025.0 - 127.0 / 256, n3, "PH%d" % j)
         out = b1[:, 0:40]
         mm(n1, [(out, im(1.0), T.C16[:, c], "I1 C16%d" % j), (out, im(-64.0), T.AH[:, c], "I-64 AH%d" % j), (out, im(1.0), T.PH[:, c], "PH%d" % j)])
         for w in range(2):
             b = 2 * j + w
-            out, win = T.XN[:, 640 * b:640 * b + 640], T.G[:, 2048 * b:2048 * b + 2048].indirect(T.LP[:, c])
-            rd = "G%dv G%ds LP%d" % (b, b, j)
-            if w == 0:
+            out, win = T.XN[:, 320 * b:320 * b + 320], T.G[:, 4096 * j:4096 * j + 2048].indirect(T.LP[:, 20 * b:20 * b + 20])
+            rd = "GG%d LP%d" % (2 * j + 1, j)
+            if b == 2:
                 ts(out, win, -MID, None, A.add, None, rd, "XN%d" % b)
             else:
                 lin(out, win, 1.0, -MID, rd, "XN%d" % b)
@@ -398,37 +473,41 @@ def rank_program(g, core, T, topo):
 
     def slots(j):
         n0, b0 = bank(j, 0)
-        mm(n0, diag(b0[:, 0:80], T.BH, "BH", T.XN, L * j, L, "XN%d XN%d" % (2 * j, 2 * j + 1)))
+        mm(n0, diag(b0[:, 0:40 + 8 * j], T.BH, "BH", T.XN, 640 * j, 640 + 128 * j, "XN%d XN%d" % (2 * j, 2 * j + 1) + " SJ0 SJ1" * j))
+
+    def steps(j):
+        ks = range(4 * halves[j], 4 * halves[j] + 4)
+        return [(k, k + 2) for k in ks[::2]] if j == 0 else [(k, k + 1) for k in sorted(ks, key=lambda k: k == r)]
 
     def values(j):
-        (n0, b0), (n1, b1), h = bank(j, 0), bank(j, 1), halves[j]
-        ts(T.LN[:, 80 * j:80 * j + 80], b0[:, 0:80], MID, None, A.add, None, n0, "LN%d" % j)
-        win, rd = T.R1[:, 0:32 + 2560], "R1 R1o R1s LN%d" % j
-        act(T.GV[:, 640 * h:640 * h + 640], win.indirect(T.LN[:, 80 * j + 40:80 * j + 80]), F.Copy, rd, "GV%d" % j)
+        (n0, b0), h = bank(j, 0), halves[j]
+        lin(T.LN[:, 80 * j + 40:80 * j + 80], b0[:, 0:40], 1.0 / 4096, MID, n0, "LM%d" % j)
+        win, rd, o = T.R1[:, 0:32 + 2560], "R1 R1o R1s LM%d" % j, 80 * j + 40 - 40 * h
+        for c0, c1 in steps(j):
+            act(T.GV[:, CO * c0:CO * c1], win.indirect(T.LN[:, o + 10 * c0:o + 10 * c1]), F.Copy, rd, "GV%d" % c0, 50 + GA * CO * (c1 - c0))
 
     def derived(j):
-        h = halves[j]
-        win, rd = T.R1[:, 0:32 + 2560], "R1 R1o R1s LN%d GV%d" % (j, j)
-        runs = sorted(pieces(4 * h, 4 * h + 4), key=lambda p: p[0] == r)
-        for c0, c1 in runs:
+        (n0, b0), h = bank(j, 0), halves[j]
+        ts(T.LO[:, 40 * j:40 * j + 40], T.LN[:, 80 * j + 40:80 * j + 80], -4096.0, 4097 * MID, A.mult, A.add, "LM%d" % j, "LO%d" % j)
+        tt(T.LN[:, 80 * j:80 * j + 40], b0[:, 0:40], T.LO[:, 40 * j:40 * j + 40], A.add, n0 + " LO%d" % j, "LN%d" % j)
+        win, o = T.R1[:, 0:32 + 2560], 80 * j - 40 * h
+        for c0, c1 in steps(j):
             out = T.R2[:, CO * r:CO * r + CO] if c0 == r else T.SV[:, CO * c0:CO * c1]
             if c0 == r:
                 flush(j)
-            o = 80 * j - 40 * h
-            tt(out, win.indirect(T.LN[:, o + 10 * c0:o + 10 * c1]), T.GV[:, CO * c0:CO * c1], A.subtract, rd, "R2o" if c0 == r else "SV%d" % c0)
+            tt(out, win.indirect(T.LN[:, o + 10 * c0:o + 10 * c1]), T.GV[:, CO * c0:CO * c1], A.subtract,
+               "R1 R1o R1s LN%d GV%d" % (j, c0), "R2o" if c0 == r else "SV%d" % c0, 50 + GA * CO * (c1 - c0))
         if j == 0:
             flush(j)
 
     def flush(j):
         ds = [k for k in range(4 * halves[j], 4 * halves[j] + 4) if k != r]
-        send(ds, [eng[4 * n:4 * n + 4] for n in range(len(ds))], lambda k: T.SV[:, CO * k:CO * k + CO], T.R2[:, CO * r:CO * r + CO], "aY",
-             keys("SV#", ds))
+        send(ds, [eng[4 * n:4 * n + 4] for n in range(len(ds))], lambda k: T.SV[:, CO * k:CO * k + CO], lambda k: T.R2[:, CO * r:CO * r + CO], "aY",
+             keys("SV#", ds), "aY%d" % j)
+        gap("aY%d" % j, "aZ%d" % j, 1200 - 1200 * j)
 
     def entities():
-        send(far + near, [pairs[k] for k in far + near], lambda k: T.ES[:, 10 * k:10 * k + 10], T.EL[:, 10 * r:10 * r + 10], "aE", "ES0 ES1")
-        before("y", ["ES1"], [])
-        g.sync.dma_start(T.EL[:, 10 * r:10 * r + 10], T.ES[:, 10 * r:10 * r + 10]).then_inc(T.sem.aE, 16)
-        after(bump("aE", 2 * (N - 1) + 16), [], ["EL"])
+        exchange(lambda k: T.ES[:, 10 * k:10 * k + 10], lambda k: T.EL[:, 10 * r:10 * r + 10], "aE", "ES0 ES1", "EL")
         dma("y", T.PC[0::16, 0:1536], T.EL[:], "EL ELs", "PCa PCb")
 
     def runs_a():
@@ -437,28 +516,28 @@ def rank_program(g, core, T, topo):
         tt(T.NS[:], T.IS[:], T.EX[:], A.subtract, "IS EX", "NS")
         scan(T.INC[:, 1:65], T.NS[:], T.NS[:], A.add, A.max, "NS", "INC")
         tt(T.DL[:, 1:65], T.IS[:], T.INC[:, 1:65], A.subtract, "IS INC", "DL")
-        act(T.SJ[:, 0:64], T.INC[:, 0:64], F.Copy, "INC INC0", "SJ0")
-        tt(T.SJ[:, 64:128], T.DL[:, 1:65], T.DL[:, 0:64], A.subtract, "DL DL0", "SJ1")
-        mm("P2", diag(T.P2[:, 0:8], T.BH, "BH", T.SJ, 0, 128, "SJ0 SJ1"))
+        lin(T.XN[:, L:L + 64], T.INC[:, 0:64], T.COL[:, 6:7], 0.0, "INC INC0 C6", "SJ0")
+        tt(T.DD[:], T.DL[:, 1:65], T.DL[:, 0:64], A.subtract, "DL DL0", "DD")
+        lin(T.XN[:, L + 64:L + 128], T.DD[:], T.COL[:, 6:7], 0.0, "DD C6", "SJ1")
         ts(T.EO[:], T.JN[:], T.INC[:, 64:65], float(L), A.is_ge, A.mult, "JN INC", "EO")
         tt(T.CN[:], T.INC[:, 8:65:8], T.INC[:, 0:57:8], A.subtract, "INC INC0", "CN")
         dma("y", T.cnt[:], T.CN[0::16, :], "CN", "cnt")
 
     def runs_b():
-        ts(T.SH[:, 0:4], T.P2[:, 0:4], -7.5, 0.0625, A.add, A.mult, "P2", "SH")
+        ts(T.SH[:, 0:4], T.P4[:, 40:44], -7.5, 0.0625, A.add, A.mult, "P4", "SH")
         ts(T.SG[:, 0:4], T.SH[:, 0:4], 16.0, None, A.mult, None, "SH", "SG0")
         ts(T.SG[:, 4:8], T.SH[:, 0:4], -16.0, 100.0, A.mult, A.add, "SH", "SG1")
         for k in range(4):
-            ts(T.RA[:, 80 * k:80 * k + 80], T.CB[:], T.SG[:, k:k + 1], T.P2[:, 4 + k:5 + k], A.is_gt, A.mult, "CB SG0 P2", "RA%d" % k)
-        tt(T.SG[:, 8:12], T.P2[:, 0:4], T.SG[:, 4:8], A.add, "P2 SG1", "SG2")
+            ts(T.RA[:, 80 * k:80 * k + 80], T.CB[:], T.SG[:, k:k + 1], T.P4[:, 44 + k:45 + k], A.is_gt, A.mult, "CB SG0 P4", "RA%d" % k)
+        tt(T.SG[:, 8:12], T.P4[:, 40:44], T.SG[:, 4:8], A.add, "P4 SG1", "SG2")
         for k in range(4):
-            ts(T.RB[:, 80 * k:80 * k + 80], T.CB[:], T.SG[:, k:k + 1], T.P2[:, 4 + k:5 + k], A.is_equal, A.mult, "CB SG0 P2", "RB%d" % k)
+            ts(T.RB[:, 80 * k:80 * k + 80], T.CB[:], T.SG[:, k:k + 1], T.P4[:, 44 + k:45 + k], A.is_equal, A.mult, "CB SG0 P4", "RB%d" % k)
         for k in range(4):
             ts(T.LK[:, 128 * k:128 * k + 128], T.XP[:], T.SG[:, 8 + k:9 + k], None, A.is_ge, None, "XP SG2", "LK%d" % k)
         out = T.P3[:, 0:80]
         mm("P3", [(out, im(1.0), T.JN[:], "I1 JN"), (out, im(1.0), T.EO[:], "EO")] +
            [(out, T.BLH[:], T.RA[:, 80 * k:80 * k + 80], "BLH RA%d" % k) for k in range(4)] +
-           [(out, T.LK[:, 128 * k:128 * k + 128], T.RB[:, 80 * k:80 * k + 80], "LK%d RB%d" % (k, k)) for k in range(4)])
+           [(out, T.LK[:, 128 * k:128 * k + 128], T.RB[:, 80 * k:80 * k + 80], "LK%d RB%d" % (k, k)) for k in range(4)], 30)
 
     def runs_c():
         ts(T.LV[:], T.P3[:, 0:80], float(L), None, A.min, None, "P3", "LV")
@@ -468,39 +547,23 @@ def rank_program(g, core, T, topo):
         mm("P2", [(out, im(96.0), T.SF[:], "I96 SF"), (out, im(-1535.0), T.HF[:], "I-1535 HF")])
         lin(T.LW[:], T.P2[:, 0:80], 1.0, 1535.0 * 1025, "P2", "LW")
 
-    ranks(0)
-    columns(0)
-    rows(0)
-    ranks(1)
-    places(0)
-    columns(1)
-    slots(0)
-    rows(1)
-    values(0)
-    places(1)
-    slots(1)
-    entities()
-    derived(0)
-    values(1)
-    runs_a()
-    derived(1)
-    runs_b()
-    lands("aY", 4, "R2")
+    stage = {"R": ranks, "C": columns, "W": rows, "P": places, "S": slots, "V": values, "D": derived}
+    single = {"E": entities, "A": runs_a, "B": runs_b}
+    for step in ORDER.split():
+        if step in single:
+            single[step]()
+        else:
+            stage[step[0]](int(step[1]))
+    lands("aY", 4 * (N - 1), "aZ0 aZ1", "R2", FLY)
     runs_c()
-    for hf in range(2):
-        out, win = T.WB[:, 640 * hf:640 * hf + 640], T.PC[:, 0:1536].indirect(T.LW[:, 40 * hf:40 * hf + 40])
-        if hf == 0:
-            cp(out, win, "PCa PCb LW NBk NBt", "WH0")
-        else:
-            act(out, win, F.Copy, "PCa PCb LW NBk NBt", "WH1")
-    dma("y", T.who[:], T.WB[0::16, 0:L], "WH0 WH1", "who")
     for k in range(4):
-        out, win = T.WA[:, CP * k:CP * k + CP], T.R2[:, 0:L + 8].indirect(T.LV[:, 20 * k:20 * k + 20])
-        if k % 2 == 0:
-            cp(out, win, "R2 R2o R2s LV NAk NAt", "YO%d" % k)
-        else:
-            act(out, win, F.Copy, "R2 R2o R2s LV NAk NAt", "YO%d" % k)
-        dma("ys"[k % 2], T.y[:, CP * k:CP * k + CP], out, "YO%d" % k, "y%d" % k)
+        out = T.WA[:, CP * k:CP * k + CP]
+        move("vs"[k % 2], out, T.R2[:, 0:L + 8].indirect(T.LV[:, 20 * k:20 * k + 20]), "R2 R2o R2s LV NAk NAt", "YO%d" % k)
+        dma("y", T.y[:, CP * k:CP * k + CP], out, "YO%d" % k, "y%d" % k, lag=LAG + 100 + 200 * k)
+    for hf in range(2):
+        move("vs"[hf], T.WB[:, 640 * hf:640 * hf + 640], T.PC[:, 0:1536].indirect(T.LW[:, 40 * hf:40 * hf + 40]), "PCa PCb LW NBk NBt", "WH%d" % hf)
+    dma("y", T.who[:], T.WB[0::16, 0:L], "WH0 WH1", "who")
+    issue()
     done = [s for (q, s), n in seen.items() if n == total[s]]
     for s in sorted(total):
         if s not in done:

@@ -14,11 +14,11 @@ SB = {
     "O": (1024, bf), "S": (1024, bf), "X": (1024, f16), "HB": (128, f16), "Y2": (128, f32), "D1": (128, u16),
     "P": (1024, f32), "DI": (320, f32), "WA": (2560, f32), "WB": (2560, f32), "NA": (320, f32), "NB": (320, f32),
     "KS": (160, u16), "TS": (160, u16), "KR": (160, u16), "S1": (2560, f32), "R1": (32 + 2560, f32), "PC": (2560, f32),
-    "TA": (TW, f32), "TB": (TW, f32), "FZ": (128, f32), "FW": (128, f32), "LC": (16, u16), "FE": (256, i32), "FF": (512, i32),
-    "E64": (256, i32), "FG": (512, i32), "LL": (512, u16), "G": (8192, i32), "NN": (512, i32),
-    "MN": (256, bf), "PR": (256, bf), "KC": (128, bf), "S2": (256, bf), "CW": (272, f32),
+    "TA": (TW, f32), "TB": (TW, f32), "FZ": (128, f32), "FW": (128, f32), "LC": (16, u16), "FE": (256, f16), "FF": (256, f16),
+    "E64": (256, bf), "LL": (512, u16), "G": (8192, i32), "NN": (1024, i32),
+    "MN": (256, f32), "PR": (256, bf), "KC": (128, bf), "S2": (256, bf), "CW": (272, f32),
     "CS": (64, f32), "CL": (128, f32), "KP": (CO, bf), "CM": (2560, bf), "D32": (40, bf), "LB": (80, u16), "K1": (640, bf),
-    "C16": (80, f16), "AH": (80, f16), "PH": (80, f16), "C": (L, bf), "LP": (80, u16), "XN": (L + 128, f16), "LO": (80, f32), "DD": (64, f32), "LN": (160, u16),
+    "C16": (80, f16), "AH": (80, f16), "PH": (80, f16), "C": (L, bf), "LP": (80, u16), "XN": (L + 128, f16), "LO": (80, f32), "SN": (512, bf), "IW": (128, bf), "BO": (144, f16), "EU": (80, f32), "LN": (160, u16),
     "GV": (L, f32), "SV": (L, f32), "R2": (L + 8, f32), "ES": (80, f32), "EL": (96, f32),
     "PI": (8, f32), "PU": (8, u16), "IS": (64, f32), "EX": (64, f32), "NS": (64, f32), "INC": (72, f32), "DL": (72, f32),
     "SH": (8, i32), "SG": (16, f32), "XP": (128, f16), "LK": (512, f16), "RA": (320, f16), "RB": (320, f16),
@@ -26,20 +26,24 @@ SB = {
 }
 SCRATCH = {k: ("sbuf", [128, w], t) for k, (w, t) in SB.items()}
 SCRATCH.update({"P%d" % k: ("psum", [128, 512], f32) for k in range(8)})
-ND = 44
+ND = 48
 SEMAPHORES = ["cv", "cs", "cp", "cg", "ls", "aK", "aV", "aC", "aE", "aY"] + ["d%d" % k for k in range(ND)]
 MULT = [160.0, 1.0, 2.0, -127.0, -64.0, 96.0, -1535.0]
-CUT = [64, 64, 64, 64]
+YC = [0, 28, 80]
+OWN = [0, 2, 4, 6, 7, 8]
+CUT = [64, 64, 72, 64]
 TURNS = 6
-HOP = 120
+HOP = 140
 LAG = 1800
 FLY = 2200
+ROWS = 1300
+MORE = 700
 MMN = 55
 GA = 1.1
 COST = {"WAk": 2600, "WBk": 2600, "TA": 480, "TB": 3200, "Z": 450, "X": 250, "HB": 120, "Y": 120, "D": 120, "KS": 300, "TS": 300, "NBt": 150,
         "FE": 360, "FF": 240, "FG": 480, "XN": 420, "DD": 120, "CX": 820, "YO": 430, "WH": 820, "IS": 130, "EX": 130, "NS": 120, "DL": 120, "SJ": 120,
-        "CM": 80, "CW": 120, "BLK": 240, "GT": 240, "TRI": 240, "XP": 240, "KT": 120, "FW": 120, "EL": 120, "K": 120, "MN": 120, "DIt": 150}
-ORDER = "R0 C0 W0 R1 P0 C1 W1 S0 P1 A V0 S1 E D0 V1 D1 B"
+        "CM": 80, "CW": 120, "BLK": 240, "GT": 240, "TRI": 240, "XP": 240, "KT": 120, "FW": 120, "EL": 120, "EB": 120, "K": 120, "MN": 120, "DIt": 150}
+ORDER = "R0 C0 R1 C1 W0 W1 P0 P1 E S0 S1 V0 V1 A D0 D1 B"
 
 
 def rank_program(g, core, T, topo):
@@ -170,8 +174,8 @@ def rank_program(g, core, T, topo):
     def cp(out, a, rd, wr, n=0):
         op("v", lambda: V.tensor_copy(out, a), rd, wr, n)
 
-    def ms(out, c, wr):
-        op("v", lambda: V.memset(out, c), "", wr)
+    def ms(out, c, wr, rd=""):
+        op("v", lambda: V.memset(out, c), rd, wr)
 
     def scan(out, d0, d1, o0, o1, rd, wr):
         op("v", lambda: V.tensor_tensor_scan(out, d0, d1, 0.0, o0, o1), rd, wr)
@@ -226,6 +230,10 @@ def rank_program(g, core, T, topo):
             bump("ls", sum(len(m) for m in masks))
         put("g", emit, rd, tag, busy, 0)
 
+    def flight(tag, done, busy):
+        gap(tag, tag + "f", 400)
+        put("e", lambda rd, wr: None, tag + "f", done, busy, 0)
+
     def lands(sem, n, tags, key, lag):
         put("", lambda rd, wr: after(bump(sem, n), [], wr), tags, key, 0, lag)
 
@@ -235,7 +243,8 @@ def rank_program(g, core, T, topo):
             g.sync.dma_start(dst(r), src(r)).then_inc(T.sem[sem], 16)
         send(far + near, [pairs[k] for k in far + near], src, dst, sem, rd, sem + "s", busy)
         put("y", emit, rd, sem + "o", 60, 0)
-        lands(sem, 2 * (N - 1) + 16, sem + "s " + sem + "o", key, FLY)
+        flight(sem + "s", sem + "e", ROWS)
+        lands(sem, 2 * (N - 1) + 16, sem + "e " + sem + "o", key, 700)
 
     def pos(k):
         return (r - k - 1) % N
@@ -251,11 +260,12 @@ def rank_program(g, core, T, topo):
         for k in ks:
             act(T.TA[:, 64 + 512 * k:576 + 512 * k], T.Z[:], F.Copy, "Z0 Z", "TA%d" % k)
 
+    gap("", "Lg", 0)
     for h in range(2):
         dma("ys"[h], T.EA[:, 64 * h:64 * h + 64], T.ent[:, 1024 * h:1024 * h + 1024], "", "EA%d" % h)
     for h in range(2):
-        dma("y", T.EB[:, 64 * h:64 * h + 64], T.ent[h::2, :], "", "EB%d" % h, lag=LAG + 500)
-        dma("s", T.EB[:, 128 + 64 * h:192 + 64 * h], T.att[h::2, :], "", "AB%d" % h, lag=LAG + 500)
+        dma("y", T.EB[:, 64 * h:64 * h + 64], T.ent[h::2, :], "Lg", "EB%d" % h, lag=LAG + MORE)
+        dma("s", T.EB[:, 128 + 64 * h:192 + 64 * h], T.att[h::2, :], "Lg", "AB%d" % h, lag=LAG + MORE)
     iota("VB", T.VB[:], [[16, 8], [0, 16]], 0, -1)
     iota("XD", T.XD[:], [[1, 128]], 0, -1)
     iota("DI", T.DI[:, 160:320], [[0, 8], [16, 20]], 4160 + CP * (r % 4), 1, "DIk")
@@ -277,61 +287,63 @@ def rank_program(g, core, T, topo):
     dma("y", T.WB[9::16, :], T.DI[:, 160:320], "DIk", "WBk")
 
     for h in range(2):
-        lin(T.OWB[:, h::2], T.EA[:, 64 * h:64 * h + 64], 1.0 / 64, 129.0 - 63.0 / 128, "EA%d" % h, "OW%d" % h)
-    place = T.P4[:, 0:128]
+        ts(T.OWB[:, h::2], T.EA[:, 64 * h:64 * h + 64], 1.0 / 64, 129.0 - 63.0 / 128, A.mult, A.add, "EA%d" % h, "OW%d" % h)
+    place = T.P7[:, 0:128]
 
     def count(n):
-        ks, c = range(2 * n, 2 * n + 2), slice(256 * n, 256 * n + 256)
+        ks, c = range(OWN[n], OWN[n + 1]), slice(128 * OWN[n], 128 * OWN[n + 1])
         for q in ks:
             ts(T.O[:, 128 * q:128 * q + 128], T.OWB[:], 129.0 + q, None, A.is_equal, None, "OW0 OW1", "O%d" % q)
         for q in ks:
             o = T.O[:, 128 * q:128 * q + 128]
             scan(T.S[:, 128 * q:128 * q + 128], o, o, A.add, A.max, "O%d" % q, "S%d" % q)
-        out = T["P%d" % n][:, 0:256]
-        mm("P%d" % n, [(out, T.TRI[:], T.O[:, c], "TRI " + keys("O#", ks)), (out, T.BLK[:], T.S[:, c], "BLK " + keys("S#", ks))], 190)
+        out = T["P%d" % n][:, 0:128 * len(ks)]
+        mm("P%d" % n, [(out, T.TRI[:], T.O[:, c], "TRI " + keys("O#", ks)), (out, T.BLK[:], T.S[:, c], "BLK " + keys("S#", ks))], 95 * len(ks))
+        act(T.X[:, c], out, F.Relu, "P%d" % n, keys("X#", ks), 120 * len(ks), bias=-1024.0)
 
     count(0)
-    ts(T.EL6[:], T.EB[:, 0:128], 63, None, A.bitwise_and, None, "EB0 EB1", "EL6")
-    count(1)
-    lin(T.K0[:], T.EL6[:], 64.0, 64.0, "EL6", "K0")
+    lin(T.EB[:, 0:128], T.EB[:, 0:128], 64.0, 0.0, "EB0 EB1", "EB0 EB1")
+    lin(T.K0[:], T.EB[:, 128:256], 1.0, 64.0, "AB0 AB1", "K0")
+    for n in range(1, 5):
+        count(n)
+    ts(T.EL6[:], T.EB[:, 0:128], 4095, None, A.bitwise_and, None, "EB0 EB1 O7", "EL6")
     for b in range(4):
-        tt(T.KZ[:, 32 * b:32 * b + 32], T.K0[:, b::4], T.EB[:, 128 + b::4], A.add, "K0 AB0 AB1", "KZ%d" % b)
-    count(2)
+        tt(T.KZ[:, 32 * b:32 * b + 32], T.K0[:, b::4], T.EL6[:, b::4], A.add, "K0 EL6", "KZ%d" % b)
     op("v", lambda: V.transpose(T.KT[:], T.KZ[:]), keys("KZ#", 4), "KT")
-    count(3)
     ts(im(160.0), T.XD[:], 0.0, 160.0, A.is_equal, A.mult, "XD", "I160")
     ms(T.Z[:, 64:512], 0.0, "Z")
     dma("y", T.P[1::8, :], T.KT[:], "KT Pa", "Pk")
     gap("KT Pa", "Pg", 100)
-    dma("y", T.VAL[:, 32:], T.val[:], "Pg", "VAL", lag=3000)
+    gap("Pg", "Vg", 300)
+    dma("y", T.VAL[:, 32:], T.val[:], "Vg", "VAL", lag=3000)
     for h in range(2):
         dma("y", T.FX[:, 64 * h:64 * h + 64], T.form[h::2, :], "Pg", "FX%d" % h)
     for ah in range(4):
         dma("y", T.CL4[ah::4, :], T.cls[:], "Pg", "CL4%d" % ah)
-    for n in range(4):
-        act(T.X[:, 256 * n:256 * n + 256], T["P%d" % n][:, 0:256], F.Relu, "P%d" % n, "X%d" % n, bias=-1024.0)
-    mm("P4", [(place, T.IB[:], T.OWB[:], "IB OW0 OW1")] + [(place, im(160.0), T.X[:, 128 * q:128 * q + 128], "I160 X%d" % (q // 2)) for q in range(8)], 30)
+    mm("P7", [(place, T.IB[:], T.OWB[:], "IB OW0 OW1")] + [(place, im(160.0), T.X[:, 128 * q:128 * q + 128], "I160 X%d" % q) for q in range(8)], 30)
     act(T.TA[:, 128:576], T.Z[:, 64:512], F.Copy, "Z", "TA0")
-    ts(T.HB[:], place, 1025.0 * 2560 - 2740 - 1270, 1.0 / 2560, A.add, A.mult, "P4", "HB")
-    ts(T.Y2[:], T.HB[:], -2559.0, 2559.0 * 1025 - 2740, A.mult, A.add, "HB", "Y2")
-    tt(T.D1[:], place, T.Y2[:], A.add, "P4 Y2", "D1")
-    cp(T.WA[:, 0:2560].indirect(T.D1[:, 0:64]), T.P[:], "D1 Pa Pk", "WAk WAt")
-    act(T.WB[:, 0:2560].indirect(T.D1[:, 64:128]), T.P[:], F.Silu, "D1 Pa Pk SL", "WBk WBt")
+    for c, h in ((slice(64, 128), 1), (slice(0, 64), 0)):
+        ts(T.HB[:, c], T.P7[:, c], 1025.0 * 2560 - 2740 - 1270, 1.0 / 2560, A.add, A.mult, "P7", "Hb%d" % h)
+        ts(T.Y2[:, c], T.HB[:, c], -2559.0, 2559.0 * 1025 - 2740, A.mult, A.add, "Hb%d" % h, "Yb%d" % h)
+        tt(T.D1[:, c], T.P7[:, c], T.Y2[:, c], A.add, "P7 Yb%d" % h, "Db%d" % h)
+    cp(T.WA[:, 0:2560].indirect(T.D1[:, 0:64]), T.P[:], "Db0 Pa Pk", "WAk WAt")
+    act(T.WB[:, 0:2560].indirect(T.D1[:, 64:128]), T.P[:], F.Silu, "Db1 Pa Pk SL", "WBk WBt")
     dma("y", T.NA[:, 160:320], T.WA[1::16, :], "WAk", "NAk")
     dma("s", T.NB[:, 160:320], T.WB[9::16, :], "WBk", "NBk")
     dma("y", T.NA[:, 0:160], T.WA[0::16, :], "WAt", "NAt")
     dma("s", T.NB[:, 0:160], T.WB[0::16, :], "WBt", "NBt")
+    gap("WAk WBk", "Tg", 400)
+    gap("WAk", "Wg", 0)
     zero(range(1, 5))
     iota("PC1", T.PC1[:, 0:1], [[1, 1]], 0, 1)
     iota("XF", T.XF[:], [[1, 144]], 0, 0)
     iota("PC", T.PC[:, 0:L], [[1, L]], 32, 0, "PCa")
-    dma("g", T.TB[0::16, 64:4160], T.Z[:, 64:320], "Z Pg", "TB")
-    gap("TB", "PCb", 0)
+    dma("y", T.TB[0::16, 64:4160], T.Z[:, 64:320], "Z Tg", "TB")
     iota("CL", T.CL[:], [[CO, 8], [0, 16]], 0, 0, "CLi")
     iota("E64", T.E64[:], [[64, 16], [1024, 4], [0, 4]], 0, 0)
     iota("PC", T.PC[:, L:2 * L], [[1, L]], 32 + L, 0, "PCb")
     for k, m in ((1, 112), (2, 15), (3, 3), (4, 7)):
-        ts(T.CI[:, k:k + 1], T.PC1[:, 0:1], m, None, A.bitwise_and, None, "PC1", "CI%d" % k)
+        ts(T.CI[:, k:k + 1], T.PC1[:, 0:1], m, None, A.bitwise_and, None, "PC1 Wg", "CI%d" % k)
     for h in range(2):
         for b in range(4):
             cp(T.FZ[:, 32 * b + 16 * h:32 * b + 16 * h + 16], T.FX[:, 64 * h + 16 * b:64 * h + 16 * b + 16], "FX%d" % h, "FZ%d%d" % (h, b))
@@ -343,6 +355,9 @@ def rank_program(g, core, T, topo):
     ms(T.R1[:, 0:32], 0.0, "R1s")
     ms(T.EL[:, 80:96], -1.0, "ELs")
     ms(T.R2[:, L:L + 8], 0.0, "R2s")
+    ts(T.IDN[:], T.XD[:], 0.0, None, A.is_equal, None, "XD Wg", "IDN")
+    for c in MULT[1:]:
+        ts(im(c), T.XD[:], 0.0, c, A.is_equal, A.mult, "XD Wg", "I%d" % c)
     tt(T.KS[:], T.NA[:, 160:320], T.NB[:, 160:320], A.min, "NAk NBk", "KS")
     send(far + near, [pairs[k] for k in far + near], lambda k: T.KS[:, 20 * k:20 * k + 20], lambda k: T.KR[:, 20 * pos(k):20 * pos(k) + 20], "aK",
          "KS CLi ELs R2s R1s", "aKs", 2000)
@@ -351,20 +366,22 @@ def rank_program(g, core, T, topo):
     tt(T.TS[:], T.NA[:, 0:160], T.NB[:, 0:160], A.min, "NAt NBt", "TS")
     for hf in range(2):
         for c0, c1 in pieces(4 * hf, 4 * hf + 4):
-            out = T.R1[:, 32 + CP * (N - 1):] if c0 == r else T.S1[:, CP * c0:CP * c1]
-            move("vs"[hf], out, T.VAL[:, 0:32 + TR].indirect(T.TS[:, 20 * c0:20 * c1]), "VAL VALs TS", "R1o" if c0 == r else "S1%d" % c0,
-                 GA * CP * (c1 - c0))
-    send(far + near, [pairs[k] for k in far + near], lambda k: T.S1[:, CP * k:CP * k + CP],
-         lambda k: T.R1[:, 32 + CP * pos(k):32 + CP * pos(k) + CP], "aV", keys("S1#", 8) + " aKs", "aVs")
-    lands("aV", 2 * (N - 1), "aVs", "R1", 6000)
-    gap("aVs", "aVg", 4500)
+            if c0 != r:
+                move("sv"[hf == halves[1]], T.S1[:, CP * c0:CP * c1], T.VAL[:, 0:32 + TR].indirect(T.TS[:, 20 * c0:20 * c1]), "VAL VALs TS", "S1%d" % c0,
+                     GA * CP * (c1 - c0))
+
+    def triples(ds, rd, tag):
+        send(ds, [eng[4 * n:4 * n + 4] for n in range(len(ds))], lambda k: T.S1[:, CP * k:CP * k + CP],
+             lambda k: T.R1[:, 32 + CP * pos(k):32 + CP * pos(k) + CP], "aV", keys("S1#", 8) + " " + rd, tag)
+
+    triples(far, "aKs", "aVs")
+    gap("aVs", "aVg", 4000)
     zero(range(5, 8))
     TAK = keys("TA#", 9)
-    cp(T.FE[:], T.FW[:, 0:128].indirect(T.LC[:]), "FW LC", "FE")
-    ts(T.FF[:, 0:256], T.FE[:], 63, None, A.bitwise_and, None, "FE", "FF0")
-    ts(T.FF[:, 256:512], T.FE[:], 6, None, A.arith_shift_right, None, "FE", "FF1")
-    for w in range(2):
-        tt(T.FG[:, 256 * w:256 * w + 256], T.FF[:, 256 * w:256 * w + 256], T.E64[:], A.add, "FF%d E64" % w, "FG%d" % w)
+    ts(T.FE[:], T.FW[:, 0:128].indirect(T.LC[:]), -2048.0, None, A.add, None, "FW LC", "FE")
+    lin(T.FF[:], T.FE[:], 1.0 / 64, 1025.0 + 32 - 63.0 / 128, "FE", "FF")
+    mm("P0", [(T.P0[:, 0:256], T.IDN[:], T.E64[:], "IDN E64"), (T.P0[:, 0:256], im(1.0), T.FE[:], "I1 FE"), (T.P0[:, 0:256], im(-64.0), T.FF[:], "I-64 FF")], 200)
+    mm("P0", [(T.P0[:, 256:512], T.IDN[:], T.E64[:], "IDN E64"), (T.P0[:, 256:512], im(1.0), T.FF[:], "I1 FF")], 200)
     iota("KC", T.KC[:], [[0, 4], [1, 32]], 0, 0, rd="aVs")
     iota("KP", T.KP[:], [[1, 16], [16, 10]], 0, 0, rd="aVs")
     iota("K1", T.K1[:], [[0, 4], [1, CO]], 0, 0, rd="aVs")
@@ -375,30 +392,31 @@ def rank_program(g, core, T, topo):
     cp(T.TA[:, 0:TW].indirect(T.KS[:, 20 * r:20 * r + 20]), T.PC[:, 2240:2560], "KS PCb", TAK, 800)
     cp(T.TA[:, 0:TW].indirect(T.KR[:, 0:70]), T.PC[:, 0:1120], "KR PCa", TAK, 2800)
     act(T.TB[:, 0:TW].indirect(T.KR[:, 70:140]), T.PC[:, 1120:2240], F.Silu, "KR PCa PCb", "TB", 2800)
-    dma("g", T.TA[0::16, 64:4160], T.TB[0::16, 64:4160], "TB aVg " + TAK, TAK, lag=2000, accum_op=A.add, max_dma_last_dim=2048)
+    gap("TA0", "Ag", 0)
+    cp(T.R1[:, 32 + CP * (N - 1):], T.VAL[:, 0:32 + TR].indirect(T.TS[:, 20 * r:20 * r + 20]), "VAL VALs TS Ag", "R1o", GA * CP)
+    dma("y", T.TA[8::16, 64:4160], T.TB[0::16, 64:4160], "TB aVg " + TAK, TAK)
     for j, h in enumerate(halves):
         for w in range(2):
             for b in range(2):
                 c0 = 128 * (2 * j + w)
-                move("vs"[w], T.LL[:, c0 + b:c0 + 128:2], T.FG[:, 256 * w + 2 * h + b:256 * w + 256:4], "FG%d" % w, "LL%d%d%d" % (j, w, b))
-    ts(T.BS[:], T.XF[:], T.COL[:, 1:2], 15.0, A.subtract, A.is_equal, "XF C1", "BS")
+                lin(T.LL[:, c0 + b:c0 + 128:2], T.P0[:, 256 * w + 2 * h + b:256 * w + 256:4], 1.0, [2048.0 + 64 * 1025, -1025.0][w], "P0 TB", "LL%d%d%d" % (j, w, b))
+    ts(T.BS[:], T.XF[:], T.COL[:, 1:2], 15.0, A.subtract, A.is_equal, "XF C1 Ag", "BS")
     ts(T.COL[:, 6:7], T.COL[:, 2:3], 0.0, None, A.is_equal, None, "C1", "C6")
-    ts(T.IDN[:], T.XD[:], 0.0, None, A.is_equal, None, "XD", "IDN")
-    tt(T.D4[:, 0:4], T.BLK[:, 0::32], T.BLK[:, 16::32], A.add, "BLK", "D4")
-    for c in MULT[1:]:
-        ts(im(c), T.XD[:], 0.0, c, A.is_equal, A.mult, "XD", "I%d" % c)
+    ts(T.IW[:], T.XD[:], 0.0, 2048.0, A.is_equal, A.mult, "XD Ag", "IW")
+    tt(T.D4[:, 0:4], T.BLK[:, 0::32], T.BLK[:, 16::32], A.add, "BLK Ag", "D4")
     ts(T.BP[:], T.BS[:], 128.0, None, A.mult, None, "BS", "BP")
-    ts(T.COL[:, 7:8], T.COL[:, 2:3], 1.0, 4096.0, A.is_equal, A.mult, "C1", "C7")
-    tt(T.COL[:, 0:1], T.COL[:, 6:7], T.COL[:, 7:8], A.add, "C6 C7", "C0")
+    ts(T.COL[:, 7:8], T.CI[:, 4:5], 1.0, 4096.0, A.is_equal, A.mult, "CI4", "C7")
+    ts(T.COL[:, 0:1], T.CI[:, 4:5], 0.0, T.COL[:, 7:8], A.is_equal, A.add, "CI4 C7", "C0")
+    ts(T.BO[:], T.BS[:], T.COL[:, 6:7], None, A.mult, None, "BS C6", "BO")
     ts(T.BH[:], T.BS[:], T.COL[:, 0:1], None, A.mult, None, "BS C0", "BH")
     for j in range(2):
-        ms(T.CW[:, 136 * j + 128:136 * j + 136], 0.0, "CWs%d" % j)
-    ms(T.INC[:, 0:1], 0.0, "INC0")
-    ms(T.DL[:, 0:1], 0.0, "DL0")
-    ts(T.CI[:, 5:6], T.PC1[:, 0:1], 3, 1, A.arith_shift_right, A.bitwise_and, "PC1", "CI5")
+        ms(T.CW[:, 136 * j + 128:136 * j + 136], 0.0, "CWs%d" % j, "Wg")
+    ms(T.INC[:, 0:1], 0.0, "INC0", "Wg")
+    ms(T.DL[:, 0:1], 0.0, "DL0", "Wg")
+    ts(T.CI[:, 5:6], T.PC1[:, 0:1], 3, 1, A.arith_shift_right, A.bitwise_and, "PC1 Wg", "CI5")
     ts(T.COL[:, 4:5], T.CI[:, 4:5], 16.0, None, A.mult, None, "CI4", "C4")
     act(T.BLH[:], T.BLK[:], F.Copy, "BLK", "BLH")
-    ts(T.XP[:], T.XF[:, 0:128], T.COL[:, 1:2], 100.0, A.subtract, A.add, "XF C1", "XP")
+    ts(T.XP[:], T.XF[:, 0:128], T.COL[:, 1:2], 100.0, A.subtract, A.add, "XF C1 Ag", "XP")
     tt(T.COL[:, 5:6], T.COL[:, 4:5], T.CI[:, 5:6], A.add, "C4 CI5", "C5")
     tt(T.XP[:], T.XP[:], T.BLK[:], A.mult, "XP BLK", "XP")
     ts(T.JN[:], T.CB[:], T.COL[:, 2:3], None, A.add, None, "CB C1", "JN")
@@ -408,19 +426,28 @@ def rank_program(g, core, T, topo):
         for q, c0, c1 in (("v", 0, CUT[b]), ("s", CUT[b], 128)):
             move(q, T.G[:, 2048 * b + 16 * c0:2048 * b + 16 * c1], T.TA[:, 64:4160].indirect(T.LL[:, 128 * b + c0:128 * b + c1]),
                  TAK + " " + keys("LL%d%d#" % (b // 2, b % 2), 2), "G%d%s" % (b, q), GA * 16 * (c1 - c0))
-        dma("y", T.NN[:, 128 * b:128 * b + 128], T.G[0::16, 2048 * b:2048 * b + 2048], "G%dv G%ds" % (b, b), "N%d" % b)
+        for t in range(2):
+            dma("y", T.NN[:, 256 * b + 128 * t:256 * b + 128 * t + 128], T.G[8 * t::16, 2048 * b:2048 * b + 2048], "G%dv G%ds" % (b, b), "N%d%d" % (b, t),
+                lag=LAG - 300 + 300 * t)
         if b % 2:
-            dma("y", T.G[1::16, 2048 * (b - 1):2048 * b], T.G[0::16, 2048 * b:2048 * b + 2048], keys("G#v", [b - 1, b]) + " " + keys("G#s", [b - 1, b]), "GG%d" % b)
+            dma("y", T.G[1::8, 2048 * (b - 1):2048 * b], T.G[0::8, 2048 * b:2048 * b + 2048], keys("G#v", [b - 1, b]) + " " + keys("G#s", [b - 1, b]), "GG%d" % b)
+
+    triples(near, TAK, "aVn")
+    lands("aV", 4 * (N - 1), "aVs aVn", "R1", 3500)
 
     def bank(j, k):
         return "P%d" % (4 * j + k), T["P%d" % (4 * j + k)]
 
     def ranks(j):
         c0, h = 128 * j, halves[j]
-        ts(T.MN[:, c0:c0 + 128], T.NN[:, 2 * c0:2 * c0 + 128], 1.0, None, A.is_gt, None, "N%d" % (2 * j), "MN%d" % j)
+        mn, n0 = T.MN[:, c0:c0 + 128], 4 * c0
+        (n2, b2), sg = bank(j, 2), T.SN[:, 2 * c0:2 * c0 + 256]
+        act(sg, T.NN[:, n0:n0 + 256], F.Sign, "N%d0 N%d1" % (2 * j, 2 * j), "SN%d" % j, 240, scale=-1.0, bias=0.5)
+        mm(n2, [(b2[:, 128:256], T.IW[:], T.SN[:, 2 * c0 + 128 * t:2 * c0 + 128 * t + 128], "IW SN%d" % j) for t in range(2)], 100)
+        tt(mn, b2[:, 128:256], T.NN[:, n0 + 256:n0 + 384], A.subtract, n2 + " N%d0" % (2 * j + 1), "MN%d" % j)
         for u in range(4):
-            tt(T.PR[:, c0 + u:c0 + 128:4], T.MN[:, c0 + 32 * u:c0 + 32 * u + 32], T.NN[:, 2 * c0 + 128 + 32 * u:2 * c0 + 160 + 32 * u], A.min,
-               "MN%d N%d" % (j, 2 * j + 1), "PR%d%d" % (j, u))
+            tt(T.PR[:, c0 + u:c0 + 128:4], T.NN[:, n0 + 384 + 32 * u:n0 + 416 + 32 * u], T.MN[:, c0 + 32 * u:c0 + 32 * u + 32], A.is_gt,
+               "MN%d N%d1" % (j, 2 * j + 1), "PR%d%d" % (j, u))
         pr, s2, prk = T.PR[:, c0:c0 + 128], T.S2[:, c0:c0 + 128], keys("PR%d#" % j, 4)
         scan(s2, T.KC[:], pr, A.min, A.add, "KC " + prk, "S2%d" % j)
         (n0, b0), (n1, b1) = bank(j, 0), bank(j, 1)
@@ -429,11 +456,10 @@ def rank_program(g, core, T, topo):
         mm(n1, [(b1[:, 128:160], T.BLK[:], T.S2[:, c0 + 3:c0 + 128:4], "BLK S2%d" % j)])
         act(T.CW[:, 136 * j:136 * j + 128], b1[:, 0:128], F.Copy, n1, "CW%d" % j)
         lin(T.CS[:, 32 * h:32 * h + 32], b1[:, 128:160], 1.0, float(CO * r), n1, "CS%d" % j)
-        ds = [k for k in range(4 * h, 4 * h + 4) if k != r]
-        send(ds, [pairs[k] for k in ds], lambda k: T.CS[:, 8 * k:8 * k + 8], lambda k: T.CL[:, 16 * r + 8:16 * r + 16], "aC", "CS%d" % j, "aC%d" % j)
         if j == 1:
+            send(far + near, [pairs[k] for k in far + near], lambda k: T.CS[:, 8 * k:8 * k + 8], lambda k: T.CL[:, 16 * r + 8:16 * r + 16], "aC", "CS0 CS1", "aC1")
             act(T.CL[:, 16 * r + 8:16 * r + 16], T.CS[:, 8 * r:8 * r + 8], F.Copy, "CS1 CLi", "CLo")
-            lands("aC", 2 * (N - 1), "aC0 aC1", "CL", FLY)
+            lands("aC", 2 * (N - 1), "aC1", "CL", FLY)
 
     def columns(j):
         (n0, b0), (n2, b2) = bank(j, 0), bank(j, 2)
@@ -451,29 +477,30 @@ def rank_program(g, core, T, topo):
         tt(T.C[:, 640 * j:640 * j + 640], T.CW[:, 136 * j:136 * j + 136].indirect(T.LB[:, c]), T.K1[:], A.is_le,
            "CW%d CWs%d LB%d K1" % (j, j, j), "CX%d" % j)
         out = b3[:, 0:40]
-        mm(n3, diag(out, T.BP, "BP", T.C, 640 * j, 640, "CX%d" % j) +
-           [(out, im(2.0), T.C16[:, c], "I2 C16%d" % j), (out, im(-127.0), T.AH[:, c], "I-127 AH%d" % j)])
+        mm(n3, [(out, im(2.0), T.C16[:, c], "I2 C16%d" % j), (out, im(-127.0), T.AH[:, c], "I-127 AH%d" % j)] +
+           diag(out, T.BP, "BP", T.C, 640 * j, 640, "CX%d" % j), 50)
 
     def places(j):
         (n1, b1), (n3, b3), c = bank(j, 1), bank(j, 3), slice(40 * j, 40 * j + 40)
         ts(T.LP[:, c], b3[:, 0:40], 127.0 * 1025, 2047.0, A.add, A.min, n3, "LP%d" % j)
         lin(T.PH[:, c], b3[:, 0:40], 1.0 / 128, 127.0 * 1025 / 128 + 1025.0 - 127.0 / 256, n3, "PH%d" % j)
         out = b1[:, 0:40]
-        mm(n1, [(out, im(1.0), T.C16[:, c], "I1 C16%d" % j), (out, im(-64.0), T.AH[:, c], "I-64 AH%d" % j), (out, im(1.0), T.PH[:, c], "PH%d" % j)])
+        mm(n1, [(out, im(1.0), T.C16[:, c], "I1 C16%d" % j), (out, im(-64.0), T.AH[:, c], "I-64 AH%d" % j)])
+        lin(T.EU[:, c], out, 1.0, 63.0 * 1025 + 64.0 * r, n1, "EU%d" % j)
         for w in range(2):
             b = 2 * j + w
             out, win = T.XN[:, 320 * b:320 * b + 320], T.G[:, 4096 * j:4096 * j + 2048].indirect(T.LP[:, 20 * b:20 * b + 20])
             rd = "GG%d LP%d" % (2 * j + 1, j)
-            if b == 2:
-                ts(out, win, -MID, None, A.add, None, rd, "XN%d" % b)
+            if w == 0:
+                ts(out, win, -MID / 2, None, A.add, None, rd, "XN%d" % b)
             else:
-                lin(out, win, 1.0, -MID, rd, "XN%d" % b)
+                lin(out, win, 1.0, -MID / 2, rd, "XN%d" % b)
         h = halves[j]
-        lin(T.ES[:, 40 * h:40 * h + 40], b1[:, 0:40], 1.0, 63.0 * 1025 + 64.0 * r, n1, "ES%d" % j)
+        tt(T.ES[:, 40 * h:40 * h + 40], T.EU[:, c], T.PH[:, c], A.add, "EU%d PH%d" % (j, j), "ES%d" % j)
 
     def slots(j):
         n0, b0 = bank(j, 0)
-        mm(n0, diag(b0[:, 0:40 + 8 * j], T.BH, "BH", T.XN, 640 * j, 640 + 128 * j, "XN%d XN%d" % (2 * j, 2 * j + 1) + " SJ0 SJ1" * j))
+        mm(n0, diag(b0[:, 0:40], T.BH, "BH", T.XN, 640 * j, 640, "XN%d XN%d" % (2 * j, 2 * j + 1)))
 
     def steps(j):
         ks = range(4 * halves[j], 4 * halves[j] + 4)
@@ -493,22 +520,31 @@ def rank_program(g, core, T, topo):
         win, o = T.R1[:, 0:32 + 2560], 80 * j - 40 * h
         for c0, c1 in steps(j):
             out = T.R2[:, CO * r:CO * r + CO] if c0 == r else T.SV[:, CO * c0:CO * c1]
-            if c0 == r:
-                flush(j)
             tt(out, win.indirect(T.LN[:, o + 10 * c0:o + 10 * c1]), T.GV[:, CO * c0:CO * c1], A.subtract,
                "R1 R1o R1s LN%d GV%d" % (j, c0), "R2o" if c0 == r else "SV%d" % c0, 50 + GA * CO * (c1 - c0))
-        if j == 0:
-            flush(j)
+            ds = [k for k in range(4 * h, 4 * h + 4) if k != r]
+            if c1 - 1 == ds[1]:
+                flush(ds[:2], 2 * j)
+            if c1 - 1 == ds[-1]:
+                flush(ds[2:], 2 * j + 1)
 
-    def flush(j):
-        ds = [k for k in range(4 * halves[j], 4 * halves[j] + 4) if k != r]
-        send(ds, [eng[4 * n:4 * n + 4] for n in range(len(ds))], lambda k: T.SV[:, CO * k:CO * k + CO], lambda k: T.R2[:, CO * r:CO * r + CO], "aY",
-             keys("SV#", ds), "aY%d" % j)
-        gap("aY%d" % j, "aZ%d" % j, 1200 - 1200 * j)
+    def flush(ds, n):
+        m = len(eng) // len(ds)
+        send(ds, [eng[m * k:m * k + m] for k in range(len(ds))], lambda k: T.SV[:, CO * k:CO * k + CO], lambda k: T.R2[:, CO * r:CO * r + CO], "aY",
+             keys("SV#", ds), "aY%d" % n)
+        flight("aY%d" % n, "aZ%d" % n, [900, 900, 700, 350][n])
 
     def entities():
-        exchange(lambda k: T.ES[:, 10 * k:10 * k + 10], lambda k: T.EL[:, 10 * r:10 * r + 10], "aE", "ES0 ES1", "EL")
-        dma("y", T.PC[0::16, 0:1536], T.EL[:], "EL ELs", "PCa PCb")
+        for j, ds in enumerate((far, near)):
+            send(ds, [eng[4 * n:4 * n + 4] for n in range(len(ds))], lambda k: T.ES[:, 10 * k:10 * k + 10], lambda k: T.EL[:, 10 * r:10 * r + 10], "aE",
+                 "ES%d" % j, "aE%d" % j)
+            flight("aE%d" % j, "aF%d" % j, ROWS // 2)
+
+        def emit(rd, wr):
+            before("y", rd, [])
+            g.sync.dma_start(T.EL[:, 10 * r:10 * r + 10], T.ES[:, 10 * r:10 * r + 10]).then_inc(T.sem.aE, 16)
+        put("y", emit, "ES1", "aEo", 60, 0)
+        lands("aE", 4 * (N - 1) + 16, "aF0 aF1 aEo", "EL", 700)
 
     def runs_a():
         cp(T.IS[:], T.CL[:, 0:128].indirect(T.PU[:, 0:4]), "CL CLo PU0", "IS")
@@ -516,22 +552,22 @@ def rank_program(g, core, T, topo):
         tt(T.NS[:], T.IS[:], T.EX[:], A.subtract, "IS EX", "NS")
         scan(T.INC[:, 1:65], T.NS[:], T.NS[:], A.add, A.max, "NS", "INC")
         tt(T.DL[:, 1:65], T.IS[:], T.INC[:, 1:65], A.subtract, "IS INC", "DL")
-        lin(T.XN[:, L:L + 64], T.INC[:, 0:64], T.COL[:, 6:7], 0.0, "INC INC0 C6", "SJ0")
-        tt(T.DD[:], T.DL[:, 1:65], T.DL[:, 0:64], A.subtract, "DL DL0", "DD")
-        lin(T.XN[:, L + 64:L + 128], T.DD[:], T.COL[:, 6:7], 0.0, "DD C6", "SJ1")
+        act(T.XN[:, L:L + 64], T.INC[:, 0:64], F.Copy, "INC INC0", "SJ0")
+        tt(T.XN[:, L + 64:L + 128], T.DL[:, 1:65], T.DL[:, 0:64], A.subtract, "DL DL0", "SJ1")
+        mm("P2", diag(T.P2[:, 0:8], T.BO, "BO", T.XN, L, 128, "SJ0 SJ1"))
         ts(T.EO[:], T.JN[:], T.INC[:, 64:65], float(L), A.is_ge, A.mult, "JN INC", "EO")
         tt(T.CN[:], T.INC[:, 8:65:8], T.INC[:, 0:57:8], A.subtract, "INC INC0", "CN")
         dma("y", T.cnt[:], T.CN[0::16, :], "CN", "cnt")
 
     def runs_b():
-        ts(T.SH[:, 0:4], T.P4[:, 40:44], -7.5, 0.0625, A.add, A.mult, "P4", "SH")
+        ts(T.SH[:, 0:4], T.P2[:, 0:4], -7.5, 0.0625, A.add, A.mult, "P2", "SH")
         ts(T.SG[:, 0:4], T.SH[:, 0:4], 16.0, None, A.mult, None, "SH", "SG0")
         ts(T.SG[:, 4:8], T.SH[:, 0:4], -16.0, 100.0, A.mult, A.add, "SH", "SG1")
         for k in range(4):
-            ts(T.RA[:, 80 * k:80 * k + 80], T.CB[:], T.SG[:, k:k + 1], T.P4[:, 44 + k:45 + k], A.is_gt, A.mult, "CB SG0 P4", "RA%d" % k)
-        tt(T.SG[:, 8:12], T.P4[:, 40:44], T.SG[:, 4:8], A.add, "P4 SG1", "SG2")
+            ts(T.RA[:, 80 * k:80 * k + 80], T.CB[:], T.SG[:, k:k + 1], T.P2[:, 4 + k:5 + k], A.is_gt, A.mult, "CB SG0 P2", "RA%d" % k)
+        tt(T.SG[:, 8:12], T.P2[:, 0:4], T.SG[:, 4:8], A.add, "P2 SG1", "SG2")
         for k in range(4):
-            ts(T.RB[:, 80 * k:80 * k + 80], T.CB[:], T.SG[:, k:k + 1], T.P4[:, 44 + k:45 + k], A.is_equal, A.mult, "CB SG0 P4", "RB%d" % k)
+            ts(T.RB[:, 80 * k:80 * k + 80], T.CB[:], T.SG[:, k:k + 1], T.P2[:, 4 + k:5 + k], A.is_equal, A.mult, "CB SG0 P2", "RB%d" % k)
         for k in range(4):
             ts(T.LK[:, 128 * k:128 * k + 128], T.XP[:], T.SG[:, 8 + k:9 + k], None, A.is_ge, None, "XP SG2", "LK%d" % k)
         out = T.P3[:, 0:80]
@@ -554,12 +590,16 @@ def rank_program(g, core, T, topo):
             single[step]()
         else:
             stage[step[0]](int(step[1]))
-    lands("aY", 4 * (N - 1), "aZ0 aZ1", "R2", FLY)
+    mine = range(4 * halves[1], 4 * halves[1] + 4)
+    alone = [s for s in mine if s != r and r == max(k for k in mine if k != s)]
+    lands("aY", len(eng) // 2 * (N - 1 + len(alone)), keys("aZ#", 4), "R2", 700)
+    dma("y", T.PC[0::16, 0:1536], T.EL[:], "EL ELs " + keys("SV#", near), "PCa PCb")
     runs_c()
-    for k in range(4):
-        out = T.WA[:, CP * k:CP * k + CP]
-        move("vs"[k % 2], out, T.R2[:, 0:L + 8].indirect(T.LV[:, 20 * k:20 * k + 20]), "R2 R2o R2s LV NAk NAt", "YO%d" % k)
-        dma("y", T.y[:, CP * k:CP * k + CP], out, "YO%d" % k, "y%d" % k, lag=LAG + 100 + 200 * k)
+    for k, (c0, c1) in enumerate(zip(YC[:-1], YC[1:])):
+        m = (c0 + c1) // 4 * 2
+        for q, a, b in (("v", c0, m), ("s", m, c1)):
+            move(q, T.WA[:, 16 * a:16 * b], T.R2[:, 0:L + 8].indirect(T.LV[:, a:b]), "R2 R2o R2s LV NAk NAt", "YO%d%s" % (k, q), 50 + GA * 16 * (b - a))
+        dma("y", T.y[:, 16 * c0:16 * c1], T.WA[:, 16 * c0:16 * c1], "YO%dv YO%ds" % (k, k), "y%d" % k, lag=LAG + 100 + 300 * k)
     for hf in range(2):
         move("vs"[hf], T.WB[:, 640 * hf:640 * hf + 640], T.PC[:, 0:1536].indirect(T.LW[:, 40 * hf:40 * hf + 40]), "PCa PCb LW NBk NBt", "WH%d" % hf)
     dma("y", T.who[:], T.WB[0::16, 0:L], "WH0 WH1", "who")

from concourse.bass import DstId, RemoteDMATransfer
from concourse.mybir import AluOpType as A, ActivationFunctionType as F

N, TR, CP, CO, L = 8, 2048, 320, 160, 1280
TW = 5568
MID = 1328.0
f32, bf, i32, u16, f16 = "float32", "bfloat16", "int32", "uint16", "float16"
SB = {
    "EA": (128, i32), "EB": (256, i32), "VAL": (32 + TR, f32), "FX": (128, i32), "CL4": (16, i32), "Z": (512, f32),
    "XD": (128, bf), "VB": (128, bf), "PC1": (8, i32), "XF": (144, f32), "COL": (8, f32), "CI": (8, i32),
    "BA": (128, bf), "BB": (128, bf), "BLK": (128, bf), "GT": (128, bf), "IK": (128, bf), "TRI": (128, bf), "IB": (128, bf),
    "IM": (7 * 128, f16), "BS": (144, bf), "BP": (144, bf), "BH": (144, f16), "BLH": (128, f16), "D4": (8, bf), "IDN": (128, bf),
    "OWB": (128, bf), "EL6": (128, i32), "K0": (128, f32), "KZ": (128, f32), "KT": (128, f32),
    "O": (1024, bf), "S": (1024, bf), "X": (1024, f16), "HB": (128, f16), "Y2": (128, f32), "D1": (128, u16),
    "P": (1024, f32), "DI": (320, f32), "WA": (2560, f32), "WB": (2560, f32), "NA": (320, f32), "NB": (320, f32),
    "KS": (160, u16), "TS": (160, u16), "KR": (160, u16), "S1": (2560, f32), "R1": (32 + 2560, f32), "PC": (2560, f32),
    "TA": (TW, f32), "TB": (TW, f32), "FZ": (128, f32), "FW": (128, f32), "LC": (16, u16), "FE": (256, f16), "FF": (256, f16),
    "E64": (256, bf), "LL": (512, u16), "G": (8192, i32), "NN": (1024, i32),
    "MN": (256, f32), "PR": (256, bf), "KC": (128, bf), "S2": (256, bf), "CW": (272, f32),
    "CS": (64, f32), "CL": (128, f32), "KP": (CO, bf), "CM": (2560, bf), "D32": (40, bf), "LB": (80, u16), "K1": (640, bf),
    "C16": (80, f16), "AH": (80, f16), "PH": (80, f16), "C": (L, bf), "LP": (80, u16), "XN": (L + 128, f16), "LO": (80, f32), "SN": (512, bf), "IW": (128, bf), "BO": (144, f16), "EU": (80, f32), "LN": (160, u16),
    "GV": (L, f32), "SV": (L, f32), "R2": (L + 8, f32), "ES": (80, f32), "EL": (96, f32),
    "PI": (8, f32), "PU": (8, u16), "IS": (64, f32), "EX": (64, f32), "NS": (64, f32), "INC": (72, f32), "DL": (72, f32),
    "SH": (8, i32), "SG": (16, f32), "XP": (128, f16), "LK": (512, f16), "RA": (320, f16), "RB": (320, f16),
    "CB": (80, bf), "JN": (80, f16), "EO": (80, f16), "CN": (8, f32), "LV": (80, u16), "SF": (80, f16), "HF": (80, f16), "LW": (80, u16),
}
SCRATCH = {k: ("sbuf", [128, w], t) for k, (w, t) in SB.items()}
SCRATCH.update({"P%d" % k: ("psum", [128, 512], f32) for k in range(8)})
ND = 48
SEMAPHORES = ["cv", "cs", "cp", "cg", "ls", "aK", "aV", "aC", "aE", "aY"] + ["d%d" % k for k in range(ND)]
MULT = [160.0, 1.0, 2.0, -127.0, -64.0, 96.0, -1535.0]
YC = [0, 28, 80]
OWN = [0, 2, 4, 6, 7, 8]
CUT = [64, 64, 72, 64]
TURNS = 6
HOP = 140
LAG = 1800
FLY = 2200
ROWS = 1300
MORE = 700
MMN = 55
GA = 1.1
COST = {"WAk": 2600, "WBk": 2600, "TA": 480, "TB": 3200, "Z": 450, "X": 250, "HB": 120, "Y": 120, "D": 120, "KS": 300, "TS": 300, "NBt": 150,
        "FE": 360, "FF": 240, "FG": 480, "XN": 420, "DD": 120, "CX": 820, "YO": 430, "WH": 820, "IS": 130, "EX": 130, "NS": 120, "DL": 120, "SJ": 120,
        "CM": 80, "CW": 120, "BLK": 240, "GT": 240, "TRI": 240, "XP": 240, "KT": 120, "FW": 120, "EL": 120, "EB": 120, "K": 120, "MN": 120, "DIt": 150}
ORDER = "R0 C0 R1 C1 W0 W1 P0 P1 E S0 S1 V0 V1 A D0 D1 B"


def rank_program(g, core, T, topo):
    r = T.rank_of(core)
    if r is None:
        return
    Q = {"v": g.vector, "s": g.scalar, "p": g.tensor, "y": g.sync, "g": g}
    total, seen, lastw, readers, nd = {}, {}, {}, {}, [0]

    def wait(q, tok):
        if seen.get((q, tok[0]), 0) < tok[1]:
            Q[q].wait_ge(T.sem[tok[0]], tok[1])
            seen[(q, tok[0])] = tok[1]

    def before(q, rd, wr):
        need = {}
        for k in rd:
            toks = list(lastw.get(k, []))
            if k[0] == "P" and k[1:].isdigit():
                toks += [t for t in readers.get(k, []) if t[0] != "c" + q]
            for s, n in toks:
                need[s] = max(need.get(s, 0), n)
        for k in wr:
            for s, n in lastw.get(k, []) + readers.get(k, []):
                need[s] = max(need.get(s, 0), n)
        for s in sorted(need):
            wait(q, (s, need[s]))

    def after(tok, rd, wr):
        for k in rd:
            readers.setdefault(k, []).append(tok)
        for k in wr:
            lastw[k] = [tok]
            readers[k] = []

    def bump(s, n):
        total[s] = total.get(s, 0) + n
        return (s, total[s])

    calls = []

    def put(q, emit, rd, wr, busy, lag):
        calls.append((q, emit, rd.split(), wr.split(), busy, lag))

    def gap(rd, wr, lag):
        put("", lambda rd, wr: None, rd, wr, 0, lag)

    def op(q, fn, rd, wr, n=0):
        def emit(rd, wr):
            before(q, rd, wr)
            fn().then_inc(T.sem["c" + q], 1)
            after(bump("c" + q, 1), rd, wr)
        put(q, emit, rd, wr, n or COST.get(wr.split()[0].rstrip("0123456789"), 70), 50)

    def dma(q, out, in_, rd, wr, lag=LAG, **kw):
        def emit(rd, wr):
            before(q, rd, wr)
            s = "d%d" % nd[0]
            nd[0] += 1
            Q[q].dma_start(out, in_, **kw).then_inc(T.sem[s], 16)
            after(bump(s, 16), rd, wr)
        put(q, emit, rd, wr, 300 if q == "g" else 60, lag)

    def mm(bank, items, n=MMN):
        def emit(rd, wr):
            before("p", [], wr)
            for k, (out, lt, rh, part) in enumerate(items):
                before("p", part.split(), [])
                ins = g.tensor.matmul(out, lt, rh, k == 0, k == len(items) - 1)
            ins.then_inc(T.sem.cp, 1)
            after(bump("cp", 1), rd, wr)
        put("p", emit, " ".join(sorted(set(" ".join(it[3] for it in items).split()))), bank, n * len(items), 50)

    def issue():
        pre, post, wrote, read = [], [[] for c in calls], {}, {}
        for n, (q, emit, rd, wr, busy, lag) in enumerate(calls):
            d = set()
            for k in rd:
                d |= set(wrote.get(k, []))
                if k[0] == "P" and k[1:].isdigit():
                    d |= {m for m in read.get(k, []) if calls[m][0] != q}
            for k in wr:
                d |= set(wrote.get(k, []) + read.get(k, []))
            pre.append(sorted(d - {n}))
            for m in pre[n]:
                post[m].append(n)
            for k in rd:
                read.setdefault(k, []).append(n)
            for k in wr:
                wrote[k], read[k] = [n], []

        def place(order, back):
            start, taken = {}, {}
            for n in order:
                q, busy, lag = calls[n][0], calls[n][4], calls[n][5]
                if back:
                    t = max([start[m] + calls[m][4] + HOP for m in post[n]] + [0]) + lag
                else:
                    t = max([start[m] + calls[m][4] + calls[m][5] + HOP for m in pre[n]] + [0])
                for t0, t1 in sorted(taken.setdefault(q, [])):
                    if t + busy > t0 and t < t1:
                        t = t1
                taken[q].append((t, t + busy))
                start[n] = t
            return start

        start, best = place(range(len(calls)), False), None
        for turn in range(TURNS):
            late = place(sorted(start, key=lambda n: (-start[n] - calls[n][4] - calls[n][5], -n)), True)
            start = place(sorted(late, key=lambda n: (-late[n] - calls[n][4], n)), False)
            end = max(start[n] + calls[n][4] + calls[n][5] for n in start)
            if best is None or end < best[0]:
                best = (end, start)
        for n in sorted(start, key=lambda n: (best[1][n], n)):
            calls[n][1](calls[n][2], calls[n][3])

    V, S = g.vector, g.scalar

    def ts(out, in0, s1, s2, o0, o1, rd, wr):
        if o1 is None:
            op("v", lambda: V.tensor_scalar(out, in0, s1, None, o0), rd, wr)
        else:
            op("v", lambda: V.tensor_scalar(out, in0, s1, s2, o0, o1), rd, wr)

    def tt(out, a, b, o, rd, wr, n=0):
        op("v", lambda: V.tensor_tensor(out, a, b, o), rd, wr, n)

    def cp(out, a, rd, wr, n=0):
        op("v", lambda: V.tensor_copy(out, a), rd, wr, n)

    def ms(out, c, wr, rd=""):
        op("v", lambda: V.memset(out, c), rd, wr)

    def scan(out, d0, d1, o0, o1, rd, wr):
        op("v", lambda: V.tensor_tensor_scan(out, d0, d1, 0.0, o0, o1), rd, wr)

    def act(out, a, fn, rd, wr, n=0, **kw):
        op("s", lambda: S.activation(out, a, fn, **kw), rd, wr, n)

    def lin(out, a, scale, bias, rd, wr):
        act(out, a, F.Identity, rd, wr, scale=scale, bias=bias)

    def move(q, out, a, rd, wr, n=0):
        if q == "v":
            cp(out, a, rd, wr, n)
        else:
            act(out, a, F.Copy, rd, wr, n)

    def iota(name, out, pat, base, cm, wr=None, rd=""):
        kw = {} if SB[name][1] == i32 else {"allow_small_or_imprecise_dtypes": True}
        n = 1
        for step, cnt in pat:
            n *= cnt
        op("g", lambda: g.iota(out, pat, base, cm, **kw), rd, wr or name, 130 + 2 * n)

    def im(c):
        k = MULT.index(c)
        return T.IM[:, 128 * k:128 * k + 128]

    def keys(fmt, *rng):
        out = [fmt]
        for n in rng:
            out = [s.replace("#", str(k), 1) for s in out for k in (range(n) if isinstance(n, int) else n)]
        return " ".join(out)

    cores = list(T.cores)
    far = [k for k in range(N) if topo.die(cores[k]) != topo.die(core)]
    near = [k for k in range(N) if k != r and k not in far]
    eng = topo.engines(core, cores[far[0]])
    ev, od = eng[0::2], eng[1::2]
    pairs = {k: ev[2 * n:2 * n + 2] for n, k in enumerate(far)}
    pairs.update({k: od[2 * n:2 * n + 2] for n, k in enumerate(near)})
    halves = sorted([0, 1], key=lambda h: h == r // 4)

    def send(dests, masks, src, dst, sem, rd, tag, busy=300):
        def emit(rd, wr):
            before("g", rd, [])
            trs = []
            for k, m in zip(dests, masks):
                rid, pid = topo.addr(cores[k])[:2]
                trs.append(RemoteDMATransfer(dst_ids=[DstId(rid=rid, pnc=pid)], dma_engine_mask=sum(1 << e for e in m),
                                             remote_sem=T.sem[sem], src=src(k), dst=dst(k)))
            g.remote_dma_fused(trs, local_sem=T.sem.ls)
            bump("ls", sum(len(m) for m in masks))
        put("g", emit, rd, tag, busy, 0)

    def flight(tag, done, busy):
        gap(tag, tag + "f", 400)
        put("e", lambda rd, wr: None, tag + "f", done, busy, 0)

    def lands(sem, n, tags, key, lag):
        put("", lambda rd, wr: after(bump(sem, n), [], wr), tags, key, 0, lag)

    def exchange(src, dst, sem, rd, key, busy=300):
        def emit(rd, wr):
            before("y", rd, [])
            g.sync.dma_start(dst(r), src(r)).then_inc(T.sem[sem], 16)
        send(far + near, [pairs[k] for k in far + near], src, dst, sem, rd, sem + "s", busy)
        put("y", emit, rd, sem + "o", 60, 0)
        flight(sem + "s", sem + "e", ROWS)
        lands(sem, 2 * (N - 1) + 16, sem + "e " + sem + "o", key, 700)

    def pos(k):
        return (r - k - 1) % N

    def diag(out, lhs, lk, buf, c0, n, key):
        return [(out, lhs[:, 15 - i:143 - i], buf[:, c0 + i:c0 + n:16], lk + " " + key) for i in range(16)]

    def pieces(c0, c1):
        cuts = sorted({c0, c1} | ({r, r + 1} if c0 <= r < c1 else set()))
        return list(zip(cuts[:-1], cuts[1:]))

    def zero(ks):
        for k in ks:
            act(T.TA[:, 64 + 512 * k:576 + 512 * k], T.Z[:], F.Copy, "Z0 Z", "TA%d" % k)

    gap("", "Lg", 0)
    for h in range(2):
        dma("ys"[h], T.EA[:, 64 * h:64 * h + 64], T.ent[:, 1024 * h:1024 * h + 1024], "", "EA%d" % h)
    for h in range(2):
        dma("y", T.EB[:, 64 * h:64 * h + 64], T.ent[h::2, :], "Lg", "EB%d" % h, lag=LAG + MORE)
        dma("s", T.EB[:, 128 + 64 * h:192 + 64 * h], T.att[h::2, :], "Lg", "AB%d" % h, lag=LAG + MORE)
    iota("VB", T.VB[:], [[16, 8], [0, 16]], 0, -1)
    iota("XD", T.XD[:], [[1, 128]], 0, -1)
    iota("DI", T.DI[:, 160:320], [[0, 8], [16, 20]], 4160 + CP * (r % 4), 1, "DIk")
    iota("P", T.P[:], [[1, 32], [1024, 2], [64, 16]], 32, 0, "Pa")
    ms(T.Z[:, 0:64], 0.0, "Z0")
    act(T.TA[:, 64:128], T.Z[:, 0:64], F.Silu, "Z0", "TA8 SL", 1400)
    ms(T.DI[:, 0:160], float(TR + 31), "DIt")
    for nm in ("WA", "WB"):
        dma("y", T[nm][0::16, :], T.DI[:, 0:160], "DIt", nm + "t")
    ts(T.BA[:], T.VB[:], -16.0, None, A.is_gt, None, "VB", "BA")
    ts(T.BB[:], T.VB[:], 0.0, None, A.is_gt, None, "VB", "BB")
    tt(T.BLK[:], T.BA[:], T.BB[:], A.subtract, "BA BB", "BLK")
    ts(T.GT[:], T.XD[:], 0.0, -1.0, A.is_lt, A.mult, "XD", "GT")
    ts(T.IK[:], T.XD[:], 0.0, 1024.0, A.is_equal, A.mult, "XD", "IK")
    tt(T.GT[:], T.GT[:], T.BA[:], A.mult, "GT BA", "GT")
    ts(T.IB[:], T.XD[:], 0.0, 20.0, A.is_equal, A.mult, "XD", "IB")
    tt(T.TRI[:], T.GT[:], T.IK[:], A.add, "GT IK", "TRI")
    dma("y", T.WA[1::16, :], T.DI[:, 160:320], "DIk", "WAk")
    dma("y", T.WB[9::16, :], T.DI[:, 160:320], "DIk", "WBk")

    for h in range(2):
        ts(T.OWB[:, h::2], T.EA[:, 64 * h:64 * h + 64], 1.0 / 64, 129.0 - 63.0 / 128, A.mult, A.add, "EA%d" % h, "OW%d" % h)
    place = T.P7[:, 0:128]

    def count(n):
        ks, c = range(OWN[n], OWN[n + 1]), slice(128 * OWN[n], 128 * OWN[n + 1])
        for q in ks:
            ts(T.O[:, 128 * q:128 * q + 128], T.OWB[:], 129.0 + q, None, A.is_equal, None, "OW0 OW1", "O%d" % q)
        for q in ks:
            o = T.O[:, 128 * q:128 * q + 128]
            scan(T.S[:, 128 * q:128 * q + 128], o, o, A.add, A.max, "O%d" % q, "S%d" % q)
        out = T["P%d" % n][:, 0:128 * len(ks)]
        mm("P%d" % n, [(out, T.TRI[:], T.O[:, c], "TRI " + keys("O#", ks)), (out, T.BLK[:], T.S[:, c], "BLK " + keys("S#", ks))], 95 * len(ks))
        act(T.X[:, c], out, F.Relu, "P%d" % n, keys("X#", ks), 120 * len(ks), bias=-1024.0)

    count(0)
    lin(T.EB[:, 0:128], T.EB[:, 0:128], 64.0, 0.0, "EB0 EB1", "EB0 EB1")
    lin(T.K0[:], T.EB[:, 128:256], 1.0, 64.0, "AB0 AB1", "K0")
    for n in range(1, 5):
        count(n)
    ts(T.EL6[:], T.EB[:, 0:128], 4095, None, A.bitwise_and, None, "EB0 EB1 O7", "EL6")
    for b in range(4):
        tt(T.KZ[:, 32 * b:32 * b + 32], T.K0[:, b::4], T.EL6[:, b::4], A.add, "K0 EL6", "KZ%d" % b)
    op("v", lambda: V.transpose(T.KT[:], T.KZ[:]), keys("KZ#", 4), "KT")
    ts(im(160.0), T.XD[:], 0.0, 160.0, A.is_equal, A.mult, "XD", "I160")
    ms(T.Z[:, 64:512], 0.0, "Z")
    dma("y", T.P[1::8, :], T.KT[:], "KT Pa", "Pk")
    gap("KT Pa", "Pg", 100)
    gap("Pg", "Vg", 300)
    dma("y", T.VAL[:, 32:], T.val[:], "Vg", "VAL", lag=3000)
    for h in range(2):
        dma("y", T.FX[:, 64 * h:64 * h + 64], T.form[h::2, :], "Pg", "FX%d" % h)
    for ah in range(4):
        dma("y", T.CL4[ah::4, :], T.cls[:], "Pg", "CL4%d" % ah)
    mm("P7", [(place, T.IB[:], T.OWB[:], "IB OW0 OW1")] + [(place, im(160.0), T.X[:, 128 * q:128 * q + 128], "I160 X%d" % q) for q in range(8)], 30)
    act(T.TA[:, 128:576], T.Z[:, 64:512], F.Copy, "Z", "TA0")
    for c, h in ((slice(64, 128), 1), (slice(0, 64), 0)):
        ts(T.HB[:, c], T.P7[:, c], 1025.0 * 2560 - 2740 - 1270, 1.0 / 2560, A.add, A.mult, "P7", "Hb%d" % h)
        ts(T.Y2[:, c], T.HB[:, c], -2559.0, 2559.0 * 1025 - 2740, A.mult, A.add, "Hb%d" % h, "Yb%d" % h)
        tt(T.D1[:, c], T.P7[:, c], T.Y2[:, c], A.add, "P7 Yb%d" % h, "Db%d" % h)
    cp(T.WA[:, 0:2560].indirect(T.D1[:, 0:64]), T.P[:], "Db0 Pa Pk", "WAk WAt")
    act(T.WB[:, 0:2560].indirect(T.D1[:, 64:128]), T.P[:], F.Silu, "Db1 Pa Pk SL", "WBk WBt")
    dma("y", T.NA[:, 160:320], T.WA[1::16, :], "WAk", "NAk")
    dma("s", T.NB[:, 160:320], T.WB[9::16, :], "WBk", "NBk")
    dma("y", T.NA[:, 0:160], T.WA[0::16, :], "WAt", "NAt")
    dma("s", T.NB[:, 0:160], T.WB[0::16, :], "WBt", "NBt")
    gap("WAk WBk", "Tg", 400)
    gap("WAk", "Wg", 0)
    zero(range(1, 5))
    iota("PC1", T.PC1[:, 0:1], [[1, 1]], 0, 1)
    iota("XF", T.XF[:], [[1, 144]], 0, 0)
    iota("PC", T.PC[:, 0:L], [[1, L]], 32, 0, "PCa")
    dma("y", T.TB[0::16, 64:4160], T.Z[:, 64:320], "Z Tg", "TB")
    iota("CL", T.CL[:], [[CO, 8], [0, 16]], 0, 0, "CLi")
    iota("E64", T.E64[:], [[64, 16], [1024, 4], [0, 4]], 0, 0)
    iota("PC", T.PC[:, L:2 * L], [[1, L]], 32 + L, 0, "PCb")
    for k, m in ((1, 112), (2, 15), (3, 3), (4, 7)):
        ts(T.CI[:, k:k + 1], T.PC1[:, 0:1], m, None, A.bitwise_and, None, "PC1 Wg", "CI%d" % k)
    for h in range(2):
        for b in range(4):
            cp(T.FZ[:, 32 * b + 16 * h:32 * b + 16 * h + 16], T.FX[:, 64 * h + 16 * b:64 * h + 16 * b + 16], "FX%d" % h, "FZ%d%d" % (h, b))
    ts(T.COL[:, 3:4], T.CI[:, 3:4], 32.0, None, A.mult, None, "CI3", "C3")
    op("v", lambda: V.transpose(T.FW[:], T.FZ[:]), keys("FZ##", 2, 4), "FW")
    ts(T.LC[:], T.CL4[:], T.COL[:, 3:4], None, A.add, None, "CL40 CL41 CL42 CL43 C3", "LC")
    cp(T.COL[:, 1:3], T.CI[:, 1:3], "CI1 CI2", "C1")
    ms(T.VAL[:, 0:32], 0.0, "VALs")
    ms(T.R1[:, 0:32], 0.0, "R1s")
    ms(T.EL[:, 80:96], -1.0, "ELs")
    ms(T.R2[:, L:L + 8], 0.0, "R2s")
    ts(T.IDN[:], T.XD[:], 0.0, None, A.is_equal, None, "XD Wg", "IDN")
    for c in MULT[1:]:
        ts(im(c), T.XD[:], 0.0, c, A.is_equal, A.mult, "XD Wg", "I%d" % c)
    tt(T.KS[:], T.NA[:, 160:320], T.NB[:, 160:320], A.min, "NAk NBk", "KS")
    send(far + near, [pairs[k] for k in far + near], lambda k: T.KS[:, 20 * k:20 * k + 20], lambda k: T.KR[:, 20 * pos(k):20 * pos(k) + 20], "aK",
         "KS CLi ELs R2s R1s", "aKs", 2000)
    lands("aK", 2 * (N - 1), "aKs", "KR", FLY)
    lin(T.NB[:, 0:160], T.NB[:, 0:160], 1.0, 32.0, "NBt", "NBt")
    tt(T.TS[:], T.NA[:, 0:160], T.NB[:, 0:160], A.min, "NAt NBt", "TS")
    for hf in range(2):
        for c0, c1 in pieces(4 * hf, 4 * hf + 4):
            if c0 != r:
                move("sv"[hf == halves[1]], T.S1[:, CP * c0:CP * c1], T.VAL[:, 0:32 + TR].indirect(T.TS[:, 20 * c0:20 * c1]), "VAL VALs TS", "S1%d" % c0,
                     GA * CP * (c1 - c0))

    def triples(ds, rd, tag):
        send(ds, [eng[4 * n:4 * n + 4] for n in range(len(ds))], lambda k: T.S1[:, CP * k:CP * k + CP],
             lambda k: T.R1[:, 32 + CP * pos(k):32 + CP * pos(k) + CP], "aV", keys("S1#", 8) + " " + rd, tag)

    triples(far, "aKs", "aVs")
    gap("aVs", "aVg", 4000)
    zero(range(5, 8))
    TAK = keys("TA#", 9)
    ts(T.FE[:], T.FW[:, 0:128].indirect(T.LC[:]), -2048.0, None, A.add, None, "FW LC", "FE")
    lin(T.FF[:], T.FE[:], 1.0 / 64, 1025.0 + 32 - 63.0 / 128, "FE", "FF")
    mm("P0", [(T.P0[:, 0:256], T.IDN[:], T.E64[:], "IDN E64"), (T.P0[:, 0:256], im(1.0), T.FE[:], "I1 FE"), (T.P0[:, 0:256], im(-64.0), T.FF[:], "I-64 FF")], 200)
    mm("P0", [(T.P0[:, 256:512], T.IDN[:], T.E64[:], "IDN E64"), (T.P0[:, 256:512], im(1.0), T.FF[:], "I1 FF")], 200)
    iota("KC", T.KC[:], [[0, 4], [1, 32]], 0, 0, rd="aVs")
    iota("KP", T.KP[:], [[1, 16], [16, 10]], 0, 0, rd="aVs")
    iota("K1", T.K1[:], [[0, 4], [1, CO]], 0, 0, rd="aVs")
    iota("D32", T.D32[:], [[32, 4], [0, 10]], 0, 0, rd="aVs")
    iota("PI", T.PI[:, 0:4], [[2, 4]], 0, 0, rd="aVs")
    iota("CB", T.CB[:], [[16, 80]], 0, 0, rd="aVs")

    cp(T.TA[:, 0:TW].indirect(T.KS[:, 20 * r:20 * r + 20]), T.PC[:, 2240:2560], "KS PCb", TAK, 800)
    cp(T.TA[:, 0:TW].indirect(T.KR[:, 0:70]), T.PC[:, 0:1120], "KR PCa", TAK, 2800)
    act(T.TB[:, 0:TW].indirect(T.KR[:, 70:140]), T.PC[:, 1120:2240], F.Silu, "KR PCa PCb", "TB", 2800)
    gap("TA0", "Ag", 0)
    cp(T.R1[:, 32 + CP * (N - 1):], T.VAL[:, 0:32 + TR].indirect(T.TS[:, 20 * r:20 * r + 20]), "VAL VALs TS Ag", "R1o", GA * CP)
    dma("y", T.TA[8::16, 64:4160], T.TB[0::16, 64:4160], "TB aVg " + TAK, TAK)
    for j, h in enumerate(halves):
        for w in range(2):
            for b in range(2):
                c0 = 128 * (2 * j + w)
                lin(T.LL[:, c0 + b:c0 + 128:2], T.P0[:, 256 * w + 2 * h + b:256 * w + 256:4], 1.0, [2048.0 + 64 * 1025, -1025.0][w], "P0 TB", "LL%d%d%d" % (j, w, b))
    ts(T.BS[:], T.XF[:], T.COL[:, 1:2], 15.0, A.subtract, A.is_equal, "XF C1 Ag", "BS")
    ts(T.COL[:, 6:7], T.COL[:, 2:3], 0.0, None, A.is_equal, None, "C1", "C6")
    ts(T.IW[:], T.XD[:], 0.0, 2048.0, A.is_equal, A.mult, "XD Ag", "IW")
    tt(T.D4[:, 0:4], T.BLK[:, 0::32], T.BLK[:, 16::32], A.add, "BLK Ag", "D4")
    ts(T.BP[:], T.BS[:], 128.0, None, A.mult, None, "BS", "BP")
    ts(T.COL[:, 7:8], T.CI[:, 4:5], 1.0, 4096.0, A.is_equal, A.mult, "CI4", "C7")
    ts(T.COL[:, 0:1], T.CI[:, 4:5], 0.0, T.COL[:, 7:8], A.is_equal, A.add, "CI4 C7", "C0")
    ts(T.BO[:], T.BS[:], T.COL[:, 6:7], None, A.mult, None, "BS C6", "BO")
    ts(T.BH[:], T.BS[:], T.COL[:, 0:1], None, A.mult, None, "BS C0", "BH")
    for j in range(2):
        ms(T.CW[:, 136 * j + 128:136 * j + 136], 0.0, "CWs%d" % j, "Wg")
    ms(T.INC[:, 0:1], 0.0, "INC0", "Wg")
    ms(T.DL[:, 0:1], 0.0, "DL0", "Wg")
    ts(T.CI[:, 5:6], T.PC1[:, 0:1], 3, 1, A.arith_shift_right, A.bitwise_and, "PC1 Wg", "CI5")
    ts(T.COL[:, 4:5], T.CI[:, 4:5], 16.0, None, A.mult, None, "CI4", "C4")
    act(T.BLH[:], T.BLK[:], F.Copy, "BLK", "BLH")
    ts(T.XP[:], T.XF[:, 0:128], T.COL[:, 1:2], 100.0, A.subtract, A.add, "XF C1 Ag", "XP")
    tt(T.COL[:, 5:6], T.COL[:, 4:5], T.CI[:, 5:6], A.add, "C4 CI5", "C5")
    tt(T.XP[:], T.XP[:], T.BLK[:], A.mult, "XP BLK", "XP")
    ts(T.JN[:], T.CB[:], T.COL[:, 2:3], None, A.add, None, "CB C1", "JN")
    ts(T.PU[:, 0:4], T.PI[:, 0:4], T.COL[:, 5:6], 8.0, A.add, A.add, "PI C5", "PU0")
    ts(T.PU[:, 4:8], T.PI[:, 0:4], T.COL[:, 5:6], 7.0, A.add, A.add, "PI C5", "PU1")
    for b in range(4):
        for q, c0, c1 in (("v", 0, CUT[b]), ("s", CUT[b], 128)):
            move(q, T.G[:, 2048 * b + 16 * c0:2048 * b + 16 * c1], T.TA[:, 64:4160].indirect(T.LL[:, 128 * b + c0:128 * b + c1]),
                 TAK + " " + keys("LL%d%d#" % (b // 2, b % 2), 2), "G%d%s" % (b, q), GA * 16 * (c1 - c0))
        for t in range(2):
            dma("y", T.NN[:, 256 * b + 128 * t:256 * b + 128 * t + 128], T.G[8 * t::16, 2048 * b:2048 * b + 2048], "G%dv G%ds" % (b, b), "N%d%d" % (b, t),
                lag=LAG - 300 + 300 * t)
        if b % 2:
            dma("y", T.G[1::8, 2048 * (b - 1):2048 * b], T.G[0::8, 2048 * b:2048 * b + 2048], keys("G#v", [b - 1, b]) + " " + keys("G#s", [b - 1, b]), "GG%d" % b)

    triples(near, TAK, "aVn")
    lands("aV", 4 * (N - 1), "aVs aVn", "R1", 3500)

    def bank(j, k):
        return "P%d" % (4 * j + k), T["P%d" % (4 * j + k)]

    def ranks(j):
        c0, h = 128 * j, halves[j]
        mn, n0 = T.MN[:, c0:c0 + 128], 4 * c0
        (n2, b2), sg = bank(j, 2), T.SN[:, 2 * c0:2 * c0 + 256]
        act(sg, T.NN[:, n0:n0 + 256], F.Sign, "N%d0 N%d1" % (2 * j, 2 * j), "SN%d" % j, 240, scale=-1.0, bias=0.5)
        mm(n2, [(b2[:, 128:256], T.IW[:], T.SN[:, 2 * c0 + 128 * t:2 * c0 + 128 * t + 128], "IW SN%d" % j) for t in range(2)], 100)
        tt(mn, b2[:, 128:256], T.NN[:, n0 + 256:n0 + 384], A.subtract, n2 + " N%d0" % (2 * j + 1), "MN%d" % j)
        for u in range(4):
            tt(T.PR[:, c0 + u:c0 + 128:4], T.NN[:, n0 + 384 + 32 * u:n0 + 416 + 32 * u], T.MN[:, c0 + 32 * u:c0 + 32 * u + 32], A.is_gt,
               "MN%d N%d1" % (j, 2 * j + 1), "PR%d%d" % (j, u))
        pr, s2, prk = T.PR[:, c0:c0 + 128], T.S2[:, c0:c0 + 128], keys("PR%d#" % j, 4)
        scan(s2, T.KC[:], pr, A.min, A.add, "KC " + prk, "S2%d" % j)
        (n0, b0), (n1, b1) = bank(j, 0), bank(j, 1)
        mm(n0, [(b0[:, 0:8], s2, T.BLK[:, 0::16], "BLK S2%d" % j)])
        mm(n1, [(b1[:, 0:128], T.GT[:], pr, "GT " + prk), (b1[:, 0:128], T.BLK[:], s2, "BLK S2%d" % j)], 95)
        mm(n1, [(b1[:, 128:160], T.BLK[:], T.S2[:, c0 + 3:c0 + 128:4], "BLK S2%d" % j)])
        act(T.CW[:, 136 * j:136 * j + 128], b1[:, 0:128], F.Copy, n1, "CW%d" % j)
        lin(T.CS[:, 32 * h:32 * h + 32], b1[:, 128:160], 1.0, float(CO * r), n1, "CS%d" % j)
        if j == 1:
            send(far + near, [pairs[k] for k in far + near], lambda k: T.CS[:, 8 * k:8 * k + 8], lambda k: T.CL[:, 16 * r + 8:16 * r + 16], "aC", "CS0 CS1", "aC1")
            act(T.CL[:, 16 * r + 8:16 * r + 16], T.CS[:, 8 * r:8 * r + 8], F.Copy, "CS1 CLi", "CLo")
            lands("aC", 2 * (N - 1), "aC1", "CL", FLY)

    def columns(j):
        (n0, b0), (n2, b2) = bank(j, 0), bank(j, 2)
        for gg in range(8):
            c = L * j + CO * gg
            ts(T.CM[:, c:c + CO], T.KP[:], b0[:, gg:gg + 1], None, A.is_ge, None, "KP " + n0, "CM%d%d" % (j, gg))
        mm(n2, [(b2[:, 0:40], T.IDN[:], T.D32[:], "IDN D32")] +
           [(b2[:, kh:40:10], T.CM[:, L * j + kh:L * j + L:10], T.D4[:, 0:4], "D4 " + keys("CM%d#" % j, 8)) for kh in range(10)])

    def rows(j):
        (n2, b2), (n3, b3), c = bank(j, 2), bank(j, 3), slice(40 * j, 40 * j + 40)
        cp(T.LB[:, c], b2[:, 0:40], n2, "LB%d" % j)
        lin(T.C16[:, c], b2[:, 0:40], 16.0, 0.0, n2, "C16%d" % j)
        lin(T.AH[:, c], b2[:, 0:40], 0.25, 1025.0 - 0.375, n2, "AH%d" % j)
        tt(T.C[:, 640 * j:640 * j + 640], T.CW[:, 136 * j:136 * j + 136].indirect(T.LB[:, c]), T.K1[:], A.is_le,
           "CW%d CWs%d LB%d K1" % (j, j, j), "CX%d" % j)
        out = b3[:, 0:40]
        mm(n3, [(out, im(2.0), T.C16[:, c], "I2 C16%d" % j), (out, im(-127.0), T.AH[:, c], "I-127 AH%d" % j)] +
           diag(out, T.BP, "BP", T.C, 640 * j, 640, "CX%d" % j), 50)

    def places(j):
        (n1, b1), (n3, b3), c = bank(j, 1), bank(j, 3), slice(40 * j, 40 * j + 40)
        ts(T.LP[:, c], b3[:, 0:40], 127.0 * 1025, 2047.0, A.add, A.min, n3, "LP%d" % j)
        lin(T.PH[:, c], b3[:, 0:40], 1.0 / 128, 127.0 * 1025 / 128 + 1025.0 - 127.0 / 256, n3, "PH%d" % j)
        out = b1[:, 0:40]
        mm(n1, [(out, im(1.0), T.C16[:, c], "I1 C16%d" % j), (out, im(-64.0), T.AH[:, c], "I-64 AH%d" % j)])
        lin(T.EU[:, c], out, 1.0, 63.0 * 1025 + 64.0 * r, n1, "EU%d" % j)
        for w in range(2):
            b = 2 * j + w
            out, win = T.XN[:, 320 * b:320 * b + 320], T.G[:, 4096 * j:4096 * j + 2048].indirect(T.LP[:, 20 * b:20 * b + 20])
            rd = "GG%d LP%d" % (2 * j + 1, j)
            if w == 0:
                ts(out, win, -MID / 2, None, A.add, None, rd, "XN%d" % b)
            else:
                lin(out, win, 1.0, -MID / 2, rd, "XN%d" % b)
        h = halves[j]
        tt(T.ES[:, 40 * h:40 * h + 40], T.EU[:, c], T.PH[:, c], A.add, "EU%d PH%d" % (j, j), "ES%d" % j)

    def slots(j):
        n0, b0 = bank(j, 0)
        mm(n0, diag(b0[:, 0:40], T.BH, "BH", T.XN, 640 * j, 640, "XN%d XN%d" % (2 * j, 2 * j + 1)))

    def steps(j):
        ks = range(4 * halves[j], 4 * halves[j] + 4)
        return [(k, k + 2) for k in ks[::2]] if j == 0 else [(k, k + 1) for k in sorted(ks, key=lambda k: k == r)]

    def values(j):
        (n0, b0), h = bank(j, 0), halves[j]
        lin(T.LN[:, 80 * j + 40:80 * j + 80], b0[:, 0:40], 1.0 / 4096, MID, n0, "LM%d" % j)
        win, rd, o = T.R1[:, 0:32 + 2560], "R1 R1o R1s LM%d" % j, 80 * j + 40 - 40 * h
        for c0, c1 in steps(j):
            act(T.GV[:, CO * c0:CO * c1], win.indirect(T.LN[:, o + 10 * c0:o + 10 * c1]), F.Copy, rd, "GV%d" % c0, 50 + GA * CO * (c1 - c0))

    def derived(j):
        (n0, b0), h = bank(j, 0), halves[j]
        ts(T.LO[:, 40 * j:40 * j + 40], T.LN[:, 80 * j + 40:80 * j + 80], -4096.0, 4097 * MID, A.mult, A.add, "LM%d" % j, "LO%d" % j)
        tt(T.LN[:, 80 * j:80 * j + 40], b0[:, 0:40], T.LO[:, 40 * j:40 * j + 40], A.add, n0 + " LO%d" % j, "LN%d" % j)
        win, o = T.R1[:, 0:32 + 2560], 80 * j - 40 * h
        for c0, c1 in steps(j):
            out = T.R2[:, CO * r:CO * r + CO] if c0 == r else T.SV[:, CO * c0:CO * c1]
            tt(out, win.indirect(T.LN[:, o + 10 * c0:o + 10 * c1]), T.GV[:, CO * c0:CO * c1], A.subtract,
               "R1 R1o R1s LN%d GV%d" % (j, c0), "R2o" if c0 == r else "SV%d" % c0, 50 + GA * CO * (c1 - c0))
            ds = [k for k in range(4 * h, 4 * h + 4) if k != r]
            if c1 - 1 == ds[1]:
                flush(ds[:2], 2 * j)
            if c1 - 1 == ds[-1]:
                flush(ds[2:], 2 * j + 1)

    def flush(ds, n):
        m = len(eng) // len(ds)
        send(ds, [eng[m * k:m * k + m] for k in range(len(ds))], lambda k: T.SV[:, CO * k:CO * k + CO], lambda k: T.R2[:, CO * r:CO * r + CO], "aY",
             keys("SV#", ds), "aY%d" % n)
        flight("aY%d" % n, "aZ%d" % n, [900, 900, 700, 350][n])

    def entities():
        for j, ds in enumerate((far, near)):
            send(ds, [eng[4 * n:4 * n + 4] for n in range(len(ds))], lambda k: T.ES[:, 10 * k:10 * k + 10], lambda k: T.EL[:, 10 * r:10 * r + 10], "aE",
                 "ES%d" % j, "aE%d" % j)
            flight("aE%d" % j, "aF%d" % j, ROWS // 2)

        def emit(rd, wr):
            before("y", rd, [])
            g.sync.dma_start(T.EL[:, 10 * r:10 * r + 10], T.ES[:, 10 * r:10 * r + 10]).then_inc(T.sem.aE, 16)
        put("y", emit, "ES1", "aEo", 60, 0)
        lands("aE", 4 * (N - 1) + 16, "aF0 aF1 aEo", "EL", 700)

    def runs_a():
        cp(T.IS[:], T.CL[:, 0:128].indirect(T.PU[:, 0:4]), "CL CLo PU0", "IS")
        cp(T.EX[:], T.CL[:, 0:128].indirect(T.PU[:, 4:8]), "CL CLo PU1", "EX")
        tt(T.NS[:], T.IS[:], T.EX[:], A.subtract, "IS EX", "NS")
        scan(T.INC[:, 1:65], T.NS[:], T.NS[:], A.add, A.max, "NS", "INC")
        tt(T.DL[:, 1:65], T.IS[:], T.INC[:, 1:65], A.subtract, "IS INC", "DL")
        act(T.XN[:, L:L + 64], T.INC[:, 0:64], F.Copy, "INC INC0", "SJ0")
        tt(T.XN[:, L + 64:L + 128], T.DL[:, 1:65], T.DL[:, 0:64], A.subtract, "DL DL0", "SJ1")
        mm("P2", diag(T.P2[:, 0:8], T.BO, "BO", T.XN, L, 128, "SJ0 SJ1"))
        ts(T.EO[:], T.JN[:], T.INC[:, 64:65], float(L), A.is_ge, A.mult, "JN INC", "EO")
        tt(T.CN[:], T.INC[:, 8:65:8], T.INC[:, 0:57:8], A.subtract, "INC INC0", "CN")
        dma("y", T.cnt[:], T.CN[0::16, :], "CN", "cnt")

    def runs_b():
        ts(T.SH[:, 0:4], T.P2[:, 0:4], -7.5, 0.0625, A.add, A.mult, "P2", "SH")
        ts(T.SG[:, 0:4], T.SH[:, 0:4], 16.0, None, A.mult, None, "SH", "SG0")
        ts(T.SG[:, 4:8], T.SH[:, 0:4], -16.0, 100.0, A.mult, A.add, "SH", "SG1")
        for k in range(4):
            ts(T.RA[:, 80 * k:80 * k + 80], T.CB[:], T.SG[:, k:k + 1], T.P2[:, 4 + k:5 + k], A.is_gt, A.mult, "CB SG0 P2", "RA%d" % k)
        tt(T.SG[:, 8:12], T.P2[:, 0:4], T.SG[:, 4:8], A.add, "P2 SG1", "SG2")
        for k in range(4):
            ts(T.RB[:, 80 * k:80 * k + 80], T.CB[:], T.SG[:, k:k + 1], T.P2[:, 4 + k:5 + k], A.is_equal, A.mult, "CB SG0 P2", "RB%d" % k)
        for k in range(4):
            ts(T.LK[:, 128 * k:128 * k + 128], T.XP[:], T.SG[:, 8 + k:9 + k], None, A.is_ge, None, "XP SG2", "LK%d" % k)
        out = T.P3[:, 0:80]
        mm("P3", [(out, im(1.0), T.JN[:], "I1 JN"), (out, im(1.0), T.EO[:], "EO")] +
           [(out, T.BLH[:], T.RA[:, 80 * k:80 * k + 80], "BLH RA%d" % k) for k in range(4)] +
           [(out, T.LK[:, 128 * k:128 * k + 128], T.RB[:, 80 * k:80 * k + 80], "LK%d RB%d" % (k, k)) for k in range(4)], 30)

    def runs_c():
        ts(T.LV[:], T.P3[:, 0:80], float(L), None, A.min, None, "P3", "LV")
        act(T.SF[:], T.LV[:], F.Copy, "LV", "SF")
        lin(T.HF[:], T.LV[:], 0.0625, 1025.0 - 15.0 / 32, "LV", "HF")
        out = T.P2[:, 0:80]
        mm("P2", [(out, im(96.0), T.SF[:], "I96 SF"), (out, im(-1535.0), T.HF[:], "I-1535 HF")])
        lin(T.LW[:], T.P2[:, 0:80], 1.0, 1535.0 * 1025, "P2", "LW")

    stage = {"R": ranks, "C": columns, "W": rows, "P": places, "S": slots, "V": values, "D": derived}
    single = {"E": entities, "A": runs_a, "B": runs_b}
    for step in ORDER.split():
        if step in single:
            single[step]()
        else:
            stage[step[0]](int(step[1]))
    mine = range(4 * halves[1], 4 * halves[1] + 4)
    alone = [s for s in mine if s != r and r == max(k for k in mine if k != s)]
    lands("aY", len(eng) // 2 * (N - 1 + len(alone)), keys("aZ#", 4), "R2", 700)
    dma("y", T.PC[0::16, 0:1536], T.EL[:], "EL ELs " + keys("SV#", near), "PCa PCb")
    runs_c()
    for k, (c0, c1) in enumerate(zip(YC[:-1], YC[1:])):
        m = (c0 + c1) // 4 * 2
        for q, a, b in (("v", c0, m), ("s", m, c1)):
            move(q, T.WA[:, 16 * a:16 * b], T.R2[:, 0:L + 8].indirect(T.LV[:, a:b]), "R2 R2o R2s LV NAk NAt", "YO%d%s" % (k, q), 50 + GA * 16 * (b - a))
        dma("y", T.y[:, 16 * c0:16 * c1], T.WA[:, 16 * c0:16 * c1], "YO%dv YO%ds" % (k, k), "y%d" % k, lag=LAG + 100 + 300 * k)
    for hf in range(2):
        move("vs"[hf], T.WB[:, 640 * hf:640 * hf + 640], T.PC[:, 0:1536].indirect(T.LW[:, 40 * hf:40 * hf + 40]), "PCa PCb LW NBk NBt", "WH%d" % hf)
    dma("y", T.who[:], T.WB[0::16, 0:L], "WH0 WH1", "who")
    issue()
    done = [s for (q, s), n in seen.items() if n == total[s]]
    for s in sorted(total):
        if s not in done:
            wait("g", (s, total[s]))
